import numpy as np
import ml_dtypes


def mxq(x, axis, fmt="e4m3"):
    dtype, down = {"e4m3": (ml_dtypes.float8_e4m3fn, 7), "e5m2": (ml_dtypes.float8_e5m2, 14)}[fmt]
    v = np.moveaxis(np.asarray(x, np.float32).astype(ml_dtypes.bfloat16).astype(np.float64), axis, -1)
    blocks = v.reshape(v.shape[:-1] + (-1, 32))
    amax = np.abs(blocks).max(-1, keepdims=True)
    byte = np.maximum(np.where(amax > 0, np.frexp(amax)[1] - 1 + 127, 0) - down, 1)
    scale = np.exp2(byte - 127.0)
    codes = (blocks / scale).astype(np.float32).astype(dtype).astype(np.float64)
    return np.moveaxis((codes * scale).reshape(v.shape), -1, axis)


WIDE = False


def mx_kscale(k):
    if not WIDE:
        return np.ones(k)
    levels = np.array([30, -30])
    if k % 512:
        return np.exp2(np.random.permutation(np.resize(levels, k // 32))).repeat(32)
    a = np.empty((k // 512, 16))
    for p in range(k // 512):
        a[p, :8] = np.random.permutation(np.resize(levels, 8))
        for g in range(8):
            far = levels[np.abs(levels - a[p, g]) >= 10]
            a[p, g + 8] = far[np.random.randint(len(far))]
    return np.exp2(a.ravel()).repeat(32)


def f64(x):
    return np.asarray(x).astype(np.float64)


def striped(idx):
    return np.tile(idx.reshape(-1, 16).T, (8, 1)).astype(np.uint16)


def unstriped(offs):
    return offs[:16].T.reshape(-1).astype(np.int64)


def silu(v):
    return v / (1.0 + np.exp(-np.maximum(v, -700.0)))


def d_silu(v):
    s = 1.0 / (1.0 + np.exp(-np.maximum(v, -700.0)))
    return s * (1.0 + v * (1.0 - s))


K, T, E, C, H, N = 128, 1024, 4, 512, 512, 512


def by_expert(wq, xq):
    return np.concatenate([wq[e].T @ xq[:, e * C:(e + 1) * C] for e in range(E)], axis=1)


def setup_inputs():
    n = np.random.standard_normal
    s = mx_kscale(N)[:, None]
    u = mx_kscale(H)
    first = np.random.permutation(np.repeat(np.arange(E), T // E))
    second = (first + 1 + np.random.permutation(np.repeat(np.arange(E - 1), -(-T // (E - 1)))[:T])) % E
    while np.bincount(second, minlength=E).max() != T // E:
        load = np.bincount(second, minlength=E); hi, lo = int(load.argmax()), int(load.argmin())
        t = np.flatnonzero((second == hi) & (first != lo))[0]; second[t] = lo
    slot_token = np.empty(E * C, np.int64); pos = np.empty((2, T), np.int64); fill = np.zeros(E, np.int64)
    place = np.stack([np.random.permutation(C) for _ in range(E)])
    for r, deal in enumerate((first, second)):
        for t in np.random.permutation(T):
            e = deal[t]; j = e * C + place[e, fill[e]]; fill[e] += 1; slot_token[j] = t; pos[r, t] = j
    g = np.random.uniform(0.2, 0.8, T)
    w_slot = np.empty(E * C); w_slot[pos[0]] = g; w_slot[pos[1]] = 1.0 - g
    return {
        "dyT": (n((N, T)) * s).astype(np.float32),
        "a1": n((H, E * C)).astype(np.float32),
        "a3": n((H, E * C)).astype(np.float32),
        "w2": (n((E, N, H)) / np.sqrt(N) / s[None] * u[None, None, :]).astype(np.float32),
        "w1": (n((E, H, K)) / np.sqrt(H) / u[None, :, None]).astype(np.float32),
        "w3": (n((E, H, K)) / np.sqrt(H) / u[None, :, None]).astype(np.float32),
        "gate": np.tile(w_slot, (N, 1)).astype(np.float32),
        "offs": striped(slot_token),
        "pos1": striped(pos[0]),
        "pos2": striped(pos[1]),
    }


def reference(dyT, a1, a3, w2, w1, w3, gate, offs, pos1, pos2):
    idx = unstriped(offs)
    gq = mxq(f64(gate) * f64(dyT)[:, idx], 0, "e5m2")
    dh = by_expert(mxq(f64(w2), 1, "e4m3"), gq)
    da1 = dh * f64(a3) * d_silu(f64(a1))
    da3 = dh * silu(f64(a1))
    dx = by_expert(mxq(f64(w1), 1, "e4m3"), mxq(da1, 0, "e5m2")) + by_expert(mxq(f64(w3), 1, "e4m3"), mxq(da3, 0, "e5m2"))
    return dx[:, unstriped(pos1)] + dx[:, unstriped(pos2)]

@@ -1,0 +1,283 @@
+from contextlib import ExitStack
+
+import concourse.mybir as mybir
+
+K, T, E, C, H, N = 128, 1024, 4, 512, 512, 512
+S = E * C
+P = 128
+PACK = 4
+
+FLOPS = 2 * S * H * N + 2 * 2 * S * H * K
+BYTES = 4 * (N * T + 2 * H * S + S + E * N * H + 2 * E * H * K + K * T) + 2 * P * (S + 2 * T) // 16
+
+F32 = mybir.dt.float32
+BF16 = mybir.dt.bfloat16
+U32 = mybir.dt.uint32
+U16 = mybir.dt.uint16
+U8 = mybir.dt.uint8
+E4M3X4 = mybir.dt.float8_e4m3fn_x4
+E5M2X4 = mybir.dt.float8_e5m2_x4
+
+ADD = mybir.AluOpType.add
+SUB = mybir.AluOpType.subtract
+MULT = mybir.AluOpType.mult
+SIGMOID = mybir.ActivationFunctionType.Sigmoid
+COPY = mybir.ActivationFunctionType.Copy
+SILU = mybir.ActivationFunctionType.Silu
+
+
+def tile_moe_bdx_glu_silu_kernel(tc, dyT, a1, a3, w2, w1, w3, gate, offs, pos1, pos2, out):
+    nc = tc.nc
+    with ExitStack() as ctx:
+        held = ctx.enter_context(tc.tile_pool(name="held", bufs=1))
+        work = ctx.enter_context(tc.tile_pool(name="work", bufs=2))
+        psum = ctx.enter_context(tc.psum_pool(name="psum", bufs=2))
+
+        offs_sb = held.tile([P, S // 16], U16, name="offs_sb")
+        pos1_sb = held.tile([P, T // 16], U16, name="pos1_sb")
+        pos2_sb = held.tile([P, T // 16], U16, name="pos2_sb")
+        dy_sb = [held.tile([P, T], F32, name="dy%d" % t) for t in range(PACK)]
+        gate_sb = [held.tile([P, C], F32, name="gate%d" % e) for e in range(E)]
+        a1_sb = [held.tile([P, PACK, C], F32, name="a1_%d" % e) for e in range(E)]
+        f_sb = [held.tile([P, PACK, C], F32, name="f_%d" % e) for e in range(E)]
+        dx_sb = held.tile([P, S], F32, name="dx_sb")
+        fin = held.tile([P, 2, T], F32, name="fin")
+        pin = held.tile([P, 4], F32, name="pin")
+        warm = held.tile([P, 1], F32, name="warm")
+        warm_out = held.tile([P, 1], F32, name="warm_out")
+
+        nc.vector.memset(warm[:], 0.0)
+        nc.scalar.activation(warm_out[:], warm[:], SIGMOID)
+
+        def load_gate(e):
+            nc.sync.dma_start(out=gate_sb[e][:], in_=gate[0:P, e * C : (e + 1) * C])
+
+        def load_w2(e):
+            raw = work.tile([P, PACK, H], F32, name="w2_raw", tag="w2_raw", bufs=2)
+            nc.sync.dma_start(out=raw[:], in_=w2[e].rearrange("(p t) i -> p t i", t=PACK))
+            return raw
+
+        def load_w13(e):
+            raw = work.tile([P, 2, C], F32, name="w13_raw", tag="w13_raw", bufs=2)
+            nc.sync.dma_start(out=raw[:, 0, :], in_=w1[e].rearrange("(q r) k -> q (r k)", r=PACK))
+            nc.sync.dma_start(out=raw[:, 1, :], in_=w3[e].rearrange("(q r) k -> q (r k)", r=PACK))
+            return raw
+
+        def load_a1(e):
+            nc.sync.dma_start(out=a1_sb[e][:], in_=a1[:, e * C : (e + 1) * C].rearrange("(q r) s -> q r s", r=PACK))
+
+        def load_a3(e):
+            raw = work.tile([P, PACK, C], F32, name="a3_raw", tag="a3_raw", bufs=2)
+            nc.sync.dma_start(out=raw[:], in_=a3[:, e * C : (e + 1) * C].rearrange("(q r) s -> q r s", r=PACK))
+            return raw
+
+        nc.sync.dma_start(offs_sb[:], offs)
+        load_gate(0)
+        dy_rows = dyT.rearrange("(p t) c -> p t c", t=PACK)
+        for t in range(PACK):
+            nc.sync.dma_start(out=dy_sb[t][:], in_=dy_rows[:, t, :])
+        w2_raw, w13_raw, a3_raw = {}, {}, {}
+        load_gate(1)
+        w2_raw[0] = load_w2(0)
+        load_a1(0)
+        load_gate(2)
+        load_a1(1)
+        load_gate(3)
+        a3_raw[0] = load_a3(0)
+        w2_raw[1] = load_w2(1)
+        w13_raw[0] = load_w13(0)
+        load_a1(2)
+        load_a1(3)
+        a3_raw[1] = load_a3(1)
+        w13_raw[1] = load_w13(1)
+
+        g_raw, g_grp, g_mx, w2_grp, w2_mx, w13_mx, dh_sb, da_mx = {}, {}, {}, {}, {}, {}, {}, {}
+
+        def gather(e):
+            g = work.tile([P, PACK, C], F32, name="g_raw", tag="g_raw", bufs=3)
+            cols = offs_sb[:, e * C // 16 : (e + 1) * C // 16]
+            for t in range(PACK):
+                nc.vector.tensor_tensor(g[:, t, :], dy_sb[t][:].indirect(cols), gate_sb[e][:], MULT)
+            g_raw[e] = g
+
+        def group_g(e):
+            grp = work.tile([P, C * PACK], BF16, name="g_grp", tag="g_grp", bufs=2, align_bytes=64)
+            nc.scalar.copy(
+                out=grp[:].rearrange("p (c i t) -> p c t i", i=4, t=PACK),
+                in_=g_raw[e][:].rearrange("p t (c i) -> p c t i", i=4),
+            )
+            g_grp[e] = grp
+
+        def group_w2(e):
+            grp = work.tile([P, H * PACK], BF16, name="w2_grp", tag="w2_grp", bufs=2, align_bytes=64)
+            nc.scalar.copy(
+                out=grp[:].rearrange("p (r q t) -> p q t r", r=PACK, t=PACK),
+                in_=w2_raw[e][:].rearrange("p t (q r) -> p q t r", r=PACK),
+            )
+            w2_grp[e] = grp
+
+        def group_w13(e):
+            grp = work.tile([P, 2 * K * PACK], BF16, name="w13_grp", tag="w13_grp", bufs=2, align_bytes=64)
+            for m in range(2):
+                nc.scalar.copy(
+                    out=grp[:, m * K * PACK : (m + 1) * K * PACK].rearrange("p (c i r) -> p c r i", i=4, r=PACK),
+                    in_=w13_raw[e][:, m, :].rearrange("p (r c i) -> p c r i", i=4, r=PACK),
+                )
+            return grp
+
+        def quantise(grp, tag, bufs, fmt, width, parts=1):
+            codes = work.tile([P, width], U32, name=tag + "_codes", tag=tag + "_codes", bufs=bufs, align_bytes=64)
+            scales = work.tile([P, width], U8, name=tag + "_scales", tag=tag + "_scales", bufs=bufs, align_bytes=64)
+            step = width // parts
+            for a in range(0, width, step):
+                nc.vector.quantize_mx(
+                    out=codes[:, a : a + step].bitcast(fmt),
+                    scales=scales[:, a : a + step],
+                    in_=grp[:, a * PACK : (a + step) * PACK],
+                )
+            return codes, scales
+
+        def first_product(e):
+            gc, gs = g_mx[e]
+            wc, ws = w2_mx[e]
+            banks = []
+            for r in range(PACK):
+                bank = psum.tile([P, C], F32, name="dh", tag="dh", bufs=6)
+                cols = slice(r * P, (r + 1) * P)
+                nc.tensor.matmul_mx(
+                    out=bank[:],
+                    lhsT=wc[:, cols].bitcast(E4M3X4),
+                    lhsT_scale=ws[:, cols],
+                    rhs=gc[:].bitcast(E5M2X4),
+                    rhs_scale=gs[:],
+                    start=True,
+                    stop=True,
+                )
+                banks.append(bank)
+            return banks
+
+        def empty_dh(e, banks):
+            dh = work.tile([P, PACK, C], F32, name="dh_sb", tag="dh_sb", bufs=2)
+            for r in range(PACK):
+                nc.scalar.copy(out=dh[:, r, :], in_=banks[r][:])
+            dh_sb[e] = dh
+
+        def derivative(e, step):
+            f, h = f_sb[e], a1_sb[e]
+            for r in range(0, PACK, step):
+                rows = slice(r, r + step)
+                nc.vector.scalar_tensor_tensor(
+                    out=f[:, rows, :], in0=h[:, rows, :], scalar=1.0, in1=f[:, rows, :], op0=SUB, op1=MULT
+                )
+
+        def times_a3(e, step):
+            f = f_sb[e]
+            for r in range(0, PACK, step):
+                rows = slice(r, r + step)
+                nc.vector.scalar_tensor_tensor(
+                    out=f[:, rows, :], in0=f[:, rows, :], scalar=1.0, in1=a3_raw[e][:, rows, :], op0=ADD, op1=MULT
+                )
+
+        def sigmoids(e0, e1, bias):
+            for e in range(e0, e1):
+                nc.scalar.activation(f_sb[e][:], a1_sb[e][:], SIGMOID, scale=-1.0, bias=bias)
+
+        def silus(e, bias):
+            for r in (0, 2):
+                nc.scalar.activation(a1_sb[e][:, r : r + 2, :], a1_sb[e][:, r : r + 2, :], SILU, bias=bias)
+
+        def pin_order(j, src):
+            nc.scalar.activation(pin[:, j : j + 1], src, COPY, scale=0.0)
+            return pin[:, j : j + 1]
+
+        def make_da(e, factor, grp):
+            nc.vector.tensor_tensor(
+                grp.rearrange("p (c i r) -> p c r i", i=4, r=PACK),
+                dh_sb[e][:].rearrange("p r (c i) -> p c r i", i=4),
+                factor[:].rearrange("p r (c i) -> p c r i", i=4),
+                MULT,
+            )
+
+        def second_product(e, da):
+            wc, ws = w13_mx[e]
+            bank = psum.tile([P, C], F32, name="dx", tag="dx", bufs=2)
+            codes, scales = da
+            for m in range(2):
+                cols = slice(m * K, (m + 1) * K)
+                slots = slice(m * C, (m + 1) * C)
+                nc.tensor.matmul_mx(
+                    out=bank[:],
+                    lhsT=wc[:, cols].bitcast(E4M3X4),
+                    lhsT_scale=ws[:, cols],
+                    rhs=codes[:, slots].bitcast(E5M2X4),
+                    rhs_scale=scales[:, slots],
+                    start=m == 0,
+                    stop=m == 1,
+                )
+            nc.scalar.copy(out=dx_sb[:, e * C : (e + 1) * C], in_=bank[:])
+
+        gather(0)
+        group_g(0)
+        group_w2(0)
+        sigmoids(0, 2, 0.0)
+        after_n1 = pin_order(0, f_sb[1][:, 0, 0:1])
+        gather(1)
+        w2_mx[0] = quantise(w2_grp[0], "w2", 2, E4M3X4, H)
+        g_mx[0] = quantise(g_grp[0], "g", 2, E5M2X4, C)
+        banks = first_product(0)
+        silus(0, after_n1)
+        empty_dh(0, banks)
+        derivative(0, 2)
+        times_a3(0, 2)
+        silus(1, after_n1)
+        after_h1 = pin_order(1, a1_sb[1][:, 3, 0:1])
+        for e in range(E):
+            if e + 1 < E:
+                group_g(e + 1)
+                group_w2(e + 1)
+            w13_grp = group_w13(e)
+            if e + 2 < E:
+                gather(e + 2)
+                w2_raw[e + 2] = load_w2(e + 2)
+                a3_raw[e + 2] = load_a3(e + 2)
+            da_grp = work.tile([P, 2 * C * PACK], BF16, name="da_grp", tag="da_grp", bufs=1, align_bytes=64)
+            make_da(e, f_sb[e], da_grp[:, : C * PACK])
+            make_da(e, a1_sb[e], da_grp[:, C * PACK :])
+            if e + 1 < E:
+                w2_mx[e + 1] = quantise(w2_grp[e + 1], "w2", 2, E4M3X4, H)
+                g_mx[e + 1] = quantise(g_grp[e + 1], "g", 2, E5M2X4, C)
+                banks = first_product(e + 1)
+                empty_dh(e + 1, banks)
+            if e == 0:
+                sigmoids(2, 4, after_h1)
+                after_n3 = pin_order(2, f_sb[3][:, 0, 0:1])
+            w13_mx[e] = quantise(w13_grp, "w13", 2, E4M3X4, 2 * K)
+            if e + 2 < E:
+                w13_raw[e + 2] = load_w13(e + 2)
+            if e == 0:
+                nc.sync.dma_start(pos1_sb[:], pos1)
+                nc.sync.dma_start(pos2_sb[:], pos2)
+            if e + 1 < E:
+                derivative(e + 1, PACK)
+            second_product(e, quantise(da_grp, "da", 2, E5M2X4, 2 * C, parts=1 if e + 1 < E else 2))
+            if e + 2 < E:
+                silus(e + 2, after_n3)
+            if e + 1 < E:
+                times_a3(e + 1, PACK)
+
+        ends = (0, 512, 768, 1024)
+        pieces = list(zip(ends, ends[1:]))
+
+        def fetch(j, slot_list, a, b):
+            nc.vector.tensor_copy(fin[:, j, a:b], dx_sb[:].indirect(slot_list[:, a // 16 : b // 16]))
+
+        def add_and_store(engine, a, b):
+            engine.tensor_tensor(fin[:, 0, a:b], fin[:, 0, a:b], fin[:, 1, a:b], ADD)
+            nc.sync.dma_start(out=out[:, a:b], in_=fin[:, 0, a:b])
+
+        for i, (a, b) in enumerate(pieces):
+            fetch(0, pos1_sb, a, b)
+            if i > 0:
+                add_and_store(nc.gpsimd, *pieces[i - 1])
+            fetch(1, pos2_sb, a, b)
+        add_and_store(nc.vector, *pieces[-1])

@@ -1,11 +1,13 @@
 from contextlib import ExitStack
 
 import concourse.mybir as mybir
+from concourse.masks import make_identity
 
 K, T, E, C, H, N = 128, 1024, 4, 512, 512, 512
 S = E * C
 P = 128
 PACK = 4
+UNITS = C // P
 
 FLOPS = 2 * S * H * N + 2 * 2 * S * H * K
 BYTES = 4 * (N * T + 2 * H * S + S + E * N * H + 2 * E * H * K + K * T) + 2 * P * (S + 2 * T) // 16
@@ -21,7 +23,7 @@ E5M2X4 = mybir.dt.float8_e5m2_x4
 ADD = mybir.AluOpType.add
 SUB = mybir.AluOpType.subtract
 MULT = mybir.AluOpType.mult
-SIGMOID = mybir.ActivationFunctionType.Sigmoid
+TANH = mybir.ActivationFunctionType.Tanh
 COPY = mybir.ActivationFunctionType.Copy
 SILU = mybir.ActivationFunctionType.Silu
 
@@ -38,16 +40,19 @@ def tile_moe_bdx_glu_silu_kernel(tc, dyT, a1, a3, w2, w1, w3, gate, offs, pos1, 
         pos2_sb = held.tile([P, T // 16], U16, name="pos2_sb")
         dy_sb = [held.tile([P, T], F32, name="dy%d" % t) for t in range(PACK)]
         gate_sb = [held.tile([P, C], F32, name="gate%d" % e) for e in range(E)]
-        a1_sb = [held.tile([P, PACK, C], F32, name="a1_%d" % e) for e in range(E)]
-        f_sb = [held.tile([P, PACK, C], F32, name="f_%d" % e) for e in range(E)]
+        turn = [[held.tile([P, C], F32, name="turn%d_%d" % (j, u)) for u in range(UNITS)] for j in range(2)]
         dx_sb = held.tile([P, S], F32, name="dx_sb")
-        fin = held.tile([P, 2, T], F32, name="fin")
-        pin = held.tile([P, 4], F32, name="pin")
+        first = held.tile([P, T], F32, name="first")
+        both = held.tile([P, T], F32, name="both")
+        ident = held.tile([P, P], F32, name="ident")
         warm = held.tile([P, 1], F32, name="warm")
         warm_out = held.tile([P, 1], F32, name="warm_out")
 
         nc.vector.memset(warm[:], 0.0)
-        nc.scalar.activation(warm_out[:], warm[:], SIGMOID)
+        nc.scalar.activation(warm_out[:], warm[:], SILU)
+        make_identity(nc, ident[:])
+
+        w2_raw, w13_raw, a1_sb, a3_sb = {}, {}, {}, {}
 
         def load_gate(e):
             nc.sync.dma_start(out=gate_sb[e][:], in_=gate[0:P, e * C : (e + 1) * C])
@@ -55,43 +60,26 @@ def tile_moe_bdx_glu_silu_kernel(tc, dyT, a1, a3, w2, w1, w3, gate, offs, pos1, 
         def load_w2(e):
             raw = work.tile([P, PACK, H], F32, name="w2_raw", tag="w2_raw", bufs=2)
             nc.sync.dma_start(out=raw[:], in_=w2[e].rearrange("(p t) i -> p t i", t=PACK))
-            return raw
+            w2_raw[e] = raw
 
         def load_w13(e):
             raw = work.tile([P, 2, C], F32, name="w13_raw", tag="w13_raw", bufs=2)
             nc.sync.dma_start(out=raw[:, 0, :], in_=w1[e].rearrange("(q r) k -> q (r k)", r=PACK))
             nc.sync.dma_start(out=raw[:, 1, :], in_=w3[e].rearrange("(q r) k -> q (r k)", r=PACK))
-            return raw
+            w13_raw[e] = raw
 
         def load_a1(e):
-            nc.sync.dma_start(out=a1_sb[e][:], in_=a1[:, e * C : (e + 1) * C].rearrange("(q r) s -> q r s", r=PACK))
+            raw = work.tile([P, PACK, C], F32, name="a1_sb", tag="a1_sb", bufs=3)
+            nc.sync.dma_start(out=raw[:], in_=a1[:, e * C : (e + 1) * C].rearrange("(q r) s -> q r s", r=PACK))
+            a1_sb[e] = raw
 
         def load_a3(e):
-            raw = work.tile([P, PACK, C], F32, name="a3_raw", tag="a3_raw", bufs=2)
+            raw = work.tile([P, PACK, C], F32, name="a3_sb", tag="a3_sb", bufs=2)
             nc.sync.dma_start(out=raw[:], in_=a3[:, e * C : (e + 1) * C].rearrange("(q r) s -> q r s", r=PACK))
-            return raw
+            a3_sb[e] = raw
 
-        nc.sync.dma_start(offs_sb[:], offs)
-        load_gate(0)
-        dy_rows = dyT.rearrange("(p t) c -> p t c", t=PACK)
-        for t in range(PACK):
-            nc.sync.dma_start(out=dy_sb[t][:], in_=dy_rows[:, t, :])
-        w2_raw, w13_raw, a3_raw = {}, {}, {}
-        load_gate(1)
-        w2_raw[0] = load_w2(0)
-        load_a1(0)
-        load_gate(2)
-        load_a1(1)
-        load_gate(3)
-        a3_raw[0] = load_a3(0)
-        w2_raw[1] = load_w2(1)
-        w13_raw[0] = load_w13(0)
-        load_a1(2)
-        load_a1(3)
-        a3_raw[1] = load_a3(1)
-        w13_raw[1] = load_w13(1)
-
-        g_raw, g_grp, g_mx, w2_grp, w2_mx, w13_mx, dh_sb, da_mx = {}, {}, {}, {}, {}, {}, {}, {}
+        g_raw, g_grp, g_mx, w2_grp, w2_mx, w13_grp, w13_mx, n_sb, da_grp = {}, {}, {}, {}, {}, {}, {}, {}, {}
+        dh_ps, m_sb, m_ps = {}, {}, {}
 
         def gather(e):
             g = work.tile([P, PACK, C], F32, name="g_raw", tag="g_raw", bufs=3)
@@ -110,24 +98,28 @@ def tile_moe_bdx_glu_silu_kernel(tc, dyT, a1, a3, w2, w1, w3, gate, offs, pos1, 
 
         def group_w2(e):
             grp = work.tile([P, H * PACK], BF16, name="w2_grp", tag="w2_grp", bufs=2, align_bytes=64)
-            nc.scalar.copy(
-                out=grp[:].rearrange("p (r q t) -> p q t r", r=PACK, t=PACK),
-                in_=w2_raw[e][:].rearrange("p t (q r) -> p q t r", r=PACK),
+            nc.scalar.activation(
+                grp[:].rearrange("p (r q t) -> p q t r", r=PACK, t=PACK),
+                w2_raw[e][:].rearrange("p t (q r) -> p q t r", r=PACK),
+                COPY,
+                scale=0.5,
             )
             w2_grp[e] = grp
 
         def group_w13(e):
             grp = work.tile([P, 2 * K * PACK], BF16, name="w13_grp", tag="w13_grp", bufs=2, align_bytes=64)
-            for m in range(2):
-                nc.scalar.copy(
-                    out=grp[:, m * K * PACK : (m + 1) * K * PACK].rearrange("p (c i r) -> p c r i", i=4, r=PACK),
-                    in_=w13_raw[e][:, m, :].rearrange("p (r c i) -> p c r i", i=4, r=PACK),
+            for j, sign in enumerate((-1.0, 1.0)):
+                nc.scalar.activation(
+                    grp[:, j * K * PACK : (j + 1) * K * PACK].rearrange("p (c i r) -> p c r i", i=4, r=PACK),
+                    w13_raw[e][:, j, :].rearrange("p (r c i) -> p c r i", i=4, r=PACK),
+                    COPY,
+                    scale=sign,
                 )
-            return grp
+            w13_grp[e] = grp
 
-        def quantise(grp, tag, bufs, fmt, width, parts=1):
-            codes = work.tile([P, width], U32, name=tag + "_codes", tag=tag + "_codes", bufs=bufs, align_bytes=64)
-            scales = work.tile([P, width], U8, name=tag + "_scales", tag=tag + "_scales", bufs=bufs, align_bytes=64)
+        def quantise(grp, tag, fmt, width, parts=1):
+            codes = work.tile([P, width], U32, name=tag + "_codes", tag=tag + "_codes", bufs=2, align_bytes=64)
+            scales = work.tile([P, width], U8, name=tag + "_scales", tag=tag + "_scales", bufs=2, align_bytes=64)
             step = width // parts
             for a in range(0, width, step):
                 nc.vector.quantize_mx(
@@ -137,147 +129,169 @@ def tile_moe_bdx_glu_silu_kernel(tc, dyT, a1, a3, w2, w1, w3, gate, offs, pos1, 
                 )
             return codes, scales
 
-        def first_product(e):
+        def slots(u):
+            return slice(u * P, (u + 1) * P)
+
+        def tanh_turned(e, u):
+            bank = psum.tile([P, PACK, P], F32, name="a1_turned", tag="a1_turned", bufs=2)
+            for r in range(PACK):
+                nc.tensor.transpose(bank[:, r, :], a1_sb[e][:, r, slots(u)], ident[:])
+            nc.scalar.activation(turn[e % 2][u][:], bank[:].rearrange("p r q -> p (r q)"), TANH, scale=0.5)
+
+        def silu_negated(e):
+            n = work.tile([P, PACK, C], F32, name="n_sb", tag="n_sb", bufs=2)
+            nc.scalar.activation(n[:], a1_sb[e][:], SILU, scale=-1.0)
+            n_sb[e] = n
+
+        def less_one(e):
+            nc.scalar.activation(n_sb[e][:], n_sb[e][:], COPY, bias=-1.0)
+
+        def w_tile(e, u):
+            return turn[(e + 1) % 2][u][:].rearrange("p (r s) -> p r s", r=PACK)
+
+        def w_on_vector(e, u):
+            nc.vector.scalar_tensor_tensor(
+                out=w_tile(e, u), in0=n_sb[e][:, :, slots(u)], scalar=1.0, in1=a3_sb[e][:, :, slots(u)], op0=SUB, op1=MULT
+            )
+
+        def w_on_gpsimd(e, u):
+            nc.gpsimd.tensor_tensor(w_tile(e, u), n_sb[e][:, :, slots(u)], a3_sb[e][:, :, slots(u)], MULT)
+
+        def first_product(e, u):
             gc, gs = g_mx[e]
             wc, ws = w2_mx[e]
-            banks = []
+            bank = psum.tile([P, H], F32, name="dh", tag="dh", bufs=3)
+            nc.tensor.matmul_mx(
+                out=bank[:],
+                lhsT=gc[:, slots(u)].bitcast(E5M2X4),
+                lhsT_scale=gs[:, slots(u)],
+                rhs=wc[:].bitcast(E4M3X4),
+                rhs_scale=ws[:],
+                start=True,
+                stop=True,
+            )
+            dh_ps[e, u] = bank
+
+        def make_m(e, u):
+            m = work.tile([P, H], F32, name="m_sb", tag="m_sb", bufs=3)
+            nc.vector.scalar_tensor_tensor(
+                out=m[:], in0=turn[e % 2][u][:], scalar=1.0, in1=dh_ps[e, u][:], op0=ADD, op1=MULT
+            )
+            bank = psum.tile([P, PACK, P], F32, name="m_turned", tag="m_turned", bufs=2)
             for r in range(PACK):
-                bank = psum.tile([P, C], F32, name="dh", tag="dh", bufs=6)
-                cols = slice(r * P, (r + 1) * P)
-                nc.tensor.matmul_mx(
-                    out=bank[:],
-                    lhsT=wc[:, cols].bitcast(E4M3X4),
-                    lhsT_scale=ws[:, cols],
-                    rhs=gc[:].bitcast(E5M2X4),
-                    rhs_scale=gs[:],
-                    start=True,
-                    stop=True,
-                )
-                banks.append(bank)
-            return banks
+                nc.tensor.transpose(bank[:, r, :], m[:, r * P : (r + 1) * P], ident[:])
+            m_ps[e, u] = bank
 
-        def empty_dh(e, banks):
-            dh = work.tile([P, PACK, C], F32, name="dh_sb", tag="dh_sb", bufs=2)
-            for r in range(PACK):
-                nc.scalar.copy(out=dh[:, r, :], in_=banks[r][:])
-            dh_sb[e] = dh
-
-        def derivative(e, step):
-            f, h = f_sb[e], a1_sb[e]
-            for r in range(0, PACK, step):
-                rows = slice(r, r + step)
-                nc.vector.scalar_tensor_tensor(
-                    out=f[:, rows, :], in0=h[:, rows, :], scalar=1.0, in1=f[:, rows, :], op0=SUB, op1=MULT
-                )
-
-        def times_a3(e, step):
-            f = f_sb[e]
-            for r in range(0, PACK, step):
-                rows = slice(r, r + step)
-                nc.vector.scalar_tensor_tensor(
-                    out=f[:, rows, :], in0=f[:, rows, :], scalar=1.0, in1=a3_raw[e][:, rows, :], op0=ADD, op1=MULT
-                )
-
-        def sigmoids(e0, e1, bias):
-            for e in range(e0, e1):
-                nc.scalar.activation(f_sb[e][:], a1_sb[e][:], SIGMOID, scale=-1.0, bias=bias)
-
-        def silus(e, bias):
-            for r in (0, 2):
-                nc.scalar.activation(a1_sb[e][:, r : r + 2, :], a1_sb[e][:, r : r + 2, :], SILU, bias=bias)
-
-        def pin_order(j, src):
-            nc.scalar.activation(pin[:, j : j + 1], src, COPY, scale=0.0)
-            return pin[:, j : j + 1]
-
-        def make_da(e, factor, grp):
+        def make_da(e, u, j, factor):
+            a = (j * C + u * P) * PACK
             nc.vector.tensor_tensor(
-                grp.rearrange("p (c i r) -> p c r i", i=4, r=PACK),
-                dh_sb[e][:].rearrange("p r (c i) -> p c r i", i=4),
-                factor[:].rearrange("p r (c i) -> p c r i", i=4),
+                da_grp[e][:, a : a + P * PACK].rearrange("p (c i r) -> p c r i", i=4, r=PACK),
+                m_ps[e, u][:].rearrange("p r (c i) -> p c r i", i=4),
+                factor.rearrange("p r (c i) -> p c r i", i=4),
                 MULT,
             )
 
         def second_product(e, da):
             wc, ws = w13_mx[e]
-            bank = psum.tile([P, C], F32, name="dx", tag="dx", bufs=2)
+            bank = psum.tile([P, C], F32, name="dx", tag="dx", bufs=1)
             codes, scales = da
-            for m in range(2):
-                cols = slice(m * K, (m + 1) * K)
-                slots = slice(m * C, (m + 1) * C)
+            for j in range(2):
+                cols = slice(j * K, (j + 1) * K)
+                half = slice(j * C, (j + 1) * C)
                 nc.tensor.matmul_mx(
                     out=bank[:],
                     lhsT=wc[:, cols].bitcast(E4M3X4),
                     lhsT_scale=ws[:, cols],
-                    rhs=codes[:, slots].bitcast(E5M2X4),
-                    rhs_scale=scales[:, slots],
-                    start=m == 0,
-                    stop=m == 1,
+                    rhs=codes[:, half].bitcast(E5M2X4),
+                    rhs_scale=scales[:, half],
+                    start=j == 0,
+                    stop=j == 1,
                 )
             nc.scalar.copy(out=dx_sb[:, e * C : (e + 1) * C], in_=bank[:])
 
+        nc.sync.dma_start(offs_sb[:], offs)
+        load_gate(0)
+        dy_rows = dyT.rearrange("(p t) c -> p t c", t=PACK)
+        for t in range(PACK):
+            nc.sync.dma_start(out=dy_sb[t][:], in_=dy_rows[:, t, :])
+        load_gate(1)
+        load_w2(0)
+        load_a1(0)
+        load_gate(2)
+        load_a3(0)
+        load_a1(1)
+        load_w2(1)
+        load_a3(1)
+        load_w13(0)
+        load_gate(3)
+        load_a1(2)
+        load_w13(1)
+
+        def prepare(e):
+            group_g(e)
+            group_w2(e)
+
+        def first_stage(e):
+            w2_mx[e] = quantise(w2_grp[e], "w2", E4M3X4, H)
+            g_mx[e] = quantise(g_grp[e], "g", E5M2X4, C)
+
         gather(0)
-        group_g(0)
-        group_w2(0)
-        sigmoids(0, 2, 0.0)
-        after_n1 = pin_order(0, f_sb[1][:, 0, 0:1])
+        prepare(0)
+        silu_negated(0)
+        for u in range(UNITS):
+            tanh_turned(0, u)
         gather(1)
-        w2_mx[0] = quantise(w2_grp[0], "w2", 2, E4M3X4, H)
-        g_mx[0] = quantise(g_grp[0], "g", 2, E5M2X4, C)
-        banks = first_product(0)
-        silus(0, after_n1)
-        empty_dh(0, banks)
-        derivative(0, 2)
-        times_a3(0, 2)
-        silus(1, after_n1)
-        after_h1 = pin_order(1, a1_sb[1][:, 3, 0:1])
+        first_stage(0)
+        for u in range(UNITS):
+            w_on_vector(0, u)
         for e in range(E):
             if e + 1 < E:
-                group_g(e + 1)
-                group_w2(e + 1)
-            w13_grp = group_w13(e)
-            if e + 2 < E:
-                gather(e + 2)
-                w2_raw[e + 2] = load_w2(e + 2)
-                a3_raw[e + 2] = load_a3(e + 2)
-            da_grp = work.tile([P, 2 * C * PACK], BF16, name="da_grp", tag="da_grp", bufs=1, align_bytes=64)
-            make_da(e, f_sb[e], da_grp[:, : C * PACK])
-            make_da(e, a1_sb[e], da_grp[:, C * PACK :])
+                silu_negated(e + 1)
+                less_one(e + 1)
+            da_grp[e] = work.tile([P, 2 * C * PACK], BF16, name="da_grp", tag="da_grp", bufs=1, align_bytes=64)
+            for u in range(UNITS + 1):
+                if u < UNITS:
+                    first_product(e, u)
+                    make_m(e, u)
+                    if e + 1 < E:
+                        w_on_gpsimd(e + 1, u)
+                if u > 0:
+                    make_da(e, u - 1, 1, a1_sb[e][:, :, slots(u - 1)])
+                    make_da(e, u - 1, 0, w_tile(e, u - 1))
             if e + 1 < E:
-                w2_mx[e + 1] = quantise(w2_grp[e + 1], "w2", 2, E4M3X4, H)
-                g_mx[e + 1] = quantise(g_grp[e + 1], "g", 2, E5M2X4, C)
-                banks = first_product(e + 1)
-                empty_dh(e + 1, banks)
-            if e == 0:
-                sigmoids(2, 4, after_h1)
-                after_n3 = pin_order(2, f_sb[3][:, 0, 0:1])
-            w13_mx[e] = quantise(w13_grp, "w13", 2, E4M3X4, 2 * K)
+                prepare(e + 1)
+            group_w13(e)
+            if e + 1 < E:
+                for u in range(UNITS):
+                    tanh_turned(e + 1, u)
+                first_stage(e + 1)
             if e + 2 < E:
-                w13_raw[e + 2] = load_w13(e + 2)
+                load_w2(e + 2)
+                load_a3(e + 2)
+            if e + 3 < E:
+                load_a1(e + 3)
+            w13_mx[e] = quantise(w13_grp[e], "w13", E4M3X4, 2 * K)
+            if e + 2 < E:
+                load_w13(e + 2)
             if e == 0:
                 nc.sync.dma_start(pos1_sb[:], pos1)
                 nc.sync.dma_start(pos2_sb[:], pos2)
-            if e + 1 < E:
-                derivative(e + 1, PACK)
-            second_product(e, quantise(da_grp, "da", 2, E5M2X4, 2 * C, parts=1 if e + 1 < E else 2))
+            second_product(e, quantise(da_grp[e], "da", E5M2X4, 2 * C, parts=1 if e + 1 < E else 2))
             if e + 2 < E:
-                silus(e + 2, after_n3)
-            if e + 1 < E:
-                times_a3(e + 1, PACK)
+                gather(e + 2)
 
         ends = (0, 512, 768, 1024)
         pieces = list(zip(ends, ends[1:]))
 
-        def fetch(j, slot_list, a, b):
-            nc.vector.tensor_copy(fin[:, j, a:b], dx_sb[:].indirect(slot_list[:, a // 16 : b // 16]))
+        def fetch_first(a, b):
+            nc.vector.tensor_copy(first[:, a:b], dx_sb[:].indirect(pos1_sb[:, a // 16 : b // 16]))
 
-        def add_and_store(engine, a, b):
-            engine.tensor_tensor(fin[:, 0, a:b], fin[:, 0, a:b], fin[:, 1, a:b], ADD)
-            nc.sync.dma_start(out=out[:, a:b], in_=fin[:, 0, a:b])
+        def add_second(a, b):
+            nc.vector.tensor_tensor(both[:, a:b], dx_sb[:].indirect(pos2_sb[:, a // 16 : b // 16]), first[:, a:b], ADD)
+            nc.sync.dma_start(out=out[:, a:b], in_=both[:, a:b])
 
-        for i, (a, b) in enumerate(pieces):
-            fetch(0, pos1_sb, a, b)
+        for i, piece in enumerate(pieces):
+            fetch_first(*piece)
             if i > 0:
-                add_and_store(nc.gpsimd, *pieces[i - 1])
-            fetch(1, pos2_sb, a, b)
-        add_and_store(nc.vector, *pieces[-1])
+                add_second(*pieces[i - 1])
+        add_second(*pieces[-1])

@@ -8,6 +8,7 @@ S = E * C
 P = 128
 PACK = 4
 UNITS = C // P
+HALF = C // 2
 
 FLOPS = 2 * S * H * N + 2 * 2 * S * H * K
 BYTES = 4 * (N * T + 2 * H * S + S + E * N * H + 2 * E * H * K + K * T) + 2 * P * (S + 2 * T) // 16
@@ -21,7 +22,6 @@ E4M3X4 = mybir.dt.float8_e4m3fn_x4
 E5M2X4 = mybir.dt.float8_e5m2_x4
 
 ADD = mybir.AluOpType.add
-SUB = mybir.AluOpType.subtract
 MULT = mybir.AluOpType.mult
 TANH = mybir.ActivationFunctionType.Tanh
 COPY = mybir.ActivationFunctionType.Copy
@@ -41,6 +41,8 @@ def tile_moe_bdx_glu_silu_kernel(tc, dyT, a1, a3, w2, w1, w3, gate, offs, pos1, 
         dy_sb = [held.tile([P, T], F32, name="dy%d" % t) for t in range(PACK)]
         gate_sb = [held.tile([P, C], F32, name="gate%d" % e) for e in range(E)]
         turn = [[held.tile([P, C], F32, name="turn%d_%d" % (j, u)) for u in range(UNITS)] for j in range(2)]
+        w13_grp = [held.tile([P, 2 * K * PACK], BF16, name="w13_grp%d" % j, align_bytes=64) for j in range(2)]
+        late_nm = [held.tile([P, C], F32, name="late_nm%d" % j) for j in range(2)]
         dx_sb = held.tile([P, S], F32, name="dx_sb")
         first = held.tile([P, T], F32, name="first")
         both = held.tile([P, T], F32, name="both")
@@ -57,10 +59,10 @@ def tile_moe_bdx_glu_silu_kernel(tc, dyT, a1, a3, w2, w1, w3, gate, offs, pos1, 
         def load_gate(e):
             nc.sync.dma_start(out=gate_sb[e][:], in_=gate[0:P, e * C : (e + 1) * C])
 
-        def load_w2(e):
-            raw = work.tile([P, PACK, H], F32, name="w2_raw", tag="w2_raw", bufs=2)
-            nc.sync.dma_start(out=raw[:], in_=w2[e].rearrange("(p t) i -> p t i", t=PACK))
-            w2_raw[e] = raw
+        def load_w2(e, j):
+            raw = work.tile([P, PACK, HALF], F32, name="w2_raw", tag="w2_raw", bufs=4)
+            nc.sync.dma_start(out=raw[:], in_=w2[e][:, j * HALF : (j + 1) * HALF].rearrange("(p t) i -> p t i", t=PACK))
+            w2_raw[e, j] = raw
 
         def load_w13(e):
             raw = work.tile([P, 2, C], F32, name="w13_raw", tag="w13_raw", bufs=2)
@@ -68,25 +70,30 @@ def tile_moe_bdx_glu_silu_kernel(tc, dyT, a1, a3, w2, w1, w3, gate, offs, pos1, 
             nc.sync.dma_start(out=raw[:, 1, :], in_=w3[e].rearrange("(q r) k -> q (r k)", r=PACK))
             w13_raw[e] = raw
 
-        def load_a1(e):
-            raw = work.tile([P, PACK, C], F32, name="a1_sb", tag="a1_sb", bufs=3)
-            nc.sync.dma_start(out=raw[:], in_=a1[:, e * C : (e + 1) * C].rearrange("(q r) s -> q r s", r=PACK))
-            a1_sb[e] = raw
+        def load_a1(e, j):
+            raw = work.tile([P, PACK, HALF], F32, name="a1_sb", tag="a1_sb", bufs=6)
+            a = e * C + j * HALF
+            nc.sync.dma_start(out=raw[:], in_=a1[:, a : a + HALF].rearrange("(q r) s -> q r s", r=PACK))
+            a1_sb[e, j] = raw
+
+        def a1_unit(e, u):
+            return a1_sb[e, u // 2][:, :, slots(u % 2)]
 
         def load_a3(e):
             raw = work.tile([P, PACK, C], F32, name="a3_sb", tag="a3_sb", bufs=2)
             nc.sync.dma_start(out=raw[:], in_=a3[:, e * C : (e + 1) * C].rearrange("(q r) s -> q r s", r=PACK))
             a3_sb[e] = raw
 
-        g_raw, g_grp, g_mx, w2_grp, w2_mx, w13_grp, w13_mx, n_sb, da_grp = {}, {}, {}, {}, {}, {}, {}, {}, {}
+        g_raw, g_grp, g_mx, w2_grp, w2_mx, w13_mx, n_sb, da_grp = {}, {}, {}, {}, {}, {}, {}, {}
         dh_ps, m_sb, m_ps = {}, {}, {}
 
-        def gather(e):
-            g = work.tile([P, PACK, C], F32, name="g_raw", tag="g_raw", bufs=3)
-            cols = offs_sb[:, e * C // 16 : (e + 1) * C // 16]
+        def gather(experts):
+            for e in experts:
+                g_raw[e] = work.tile([P, PACK, C], F32, name="g_raw", tag="g_raw", bufs=4)
             for t in range(PACK):
-                nc.vector.tensor_tensor(g[:, t, :], dy_sb[t][:].indirect(cols), gate_sb[e][:], MULT)
-            g_raw[e] = g
+                for e in experts:
+                    cols = offs_sb[:, e * C // 16 : (e + 1) * C // 16]
+                    nc.vector.tensor_tensor(g_raw[e][:, t, :], dy_sb[t][:].indirect(cols), gate_sb[e][:], MULT)
 
         def group_g(e):
             grp = work.tile([P, C * PACK], BF16, name="g_grp", tag="g_grp", bufs=2, align_bytes=64)
@@ -98,16 +105,17 @@ def tile_moe_bdx_glu_silu_kernel(tc, dyT, a1, a3, w2, w1, w3, gate, offs, pos1, 
 
         def group_w2(e):
             grp = work.tile([P, H * PACK], BF16, name="w2_grp", tag="w2_grp", bufs=2, align_bytes=64)
-            nc.scalar.activation(
-                grp[:].rearrange("p (r q t) -> p q t r", r=PACK, t=PACK),
-                w2_raw[e][:].rearrange("p t (q r) -> p q t r", r=PACK),
-                COPY,
-                scale=0.5,
-            )
+            for j in range(2):
+                nc.scalar.activation(
+                    grp[:].rearrange("p (r q t) -> p q t r", r=PACK, t=PACK)[:, j * P // 2 : (j + 1) * P // 2],
+                    w2_raw[e, j][:].rearrange("p t (q r) -> p q t r", r=PACK),
+                    COPY,
+                    scale=0.5,
+                )
             w2_grp[e] = grp
 
         def group_w13(e):
-            grp = work.tile([P, 2 * K * PACK], BF16, name="w13_grp", tag="w13_grp", bufs=2, align_bytes=64)
+            grp = w13_grp[e % 2]
             for j, sign in enumerate((-1.0, 1.0)):
                 nc.scalar.activation(
                     grp[:, j * K * PACK : (j + 1) * K * PACK].rearrange("p (c i r) -> p c r i", i=4, r=PACK),
@@ -115,13 +123,12 @@ def tile_moe_bdx_glu_silu_kernel(tc, dyT, a1, a3, w2, w1, w3, gate, offs, pos1, 
                     COPY,
                     scale=sign,
                 )
-            w13_grp[e] = grp
 
         def quantise(grp, tag, fmt, width, parts=1):
             codes = work.tile([P, width], U32, name=tag + "_codes", tag=tag + "_codes", bufs=2, align_bytes=64)
             scales = work.tile([P, width], U8, name=tag + "_scales", tag=tag + "_scales", bufs=2, align_bytes=64)
             step = width // parts
-            for a in range(0, width, step):
+            for a in reversed(range(0, width, step)):
                 nc.vector.quantize_mx(
                     out=codes[:, a : a + step].bitcast(fmt),
                     scales=scales[:, a : a + step],
@@ -133,29 +140,42 @@ def tile_moe_bdx_glu_silu_kernel(tc, dyT, a1, a3, w2, w1, w3, gate, offs, pos1, 
             return slice(u * P, (u + 1) * P)
 
         def tanh_turned(e, u):
-            bank = psum.tile([P, PACK, P], F32, name="a1_turned", tag="a1_turned", bufs=2)
+            bank = psum.tile([P, PACK, P], F32, name="a1_turned", tag="for_scalar", bufs=2)
             for r in range(PACK):
-                nc.tensor.transpose(bank[:, r, :], a1_sb[e][:, r, slots(u)], ident[:])
+                nc.tensor.transpose(bank[:, r, :], a1_unit(e, u)[:, r, :], ident[:])
             nc.scalar.activation(turn[e % 2][u][:], bank[:].rearrange("p r q -> p (r q)"), TANH, scale=0.5)
 
         def silu_negated(e):
             n = work.tile([P, PACK, C], F32, name="n_sb", tag="n_sb", bufs=2)
-            nc.scalar.activation(n[:], a1_sb[e][:], SILU, scale=-1.0)
+            for j in range(2):
+                part = n[:, :, j * HALF : (j + 1) * HALF]
+                nc.scalar.activation(part, a1_sb[e, j][:], SILU, scale=-1.0)
+                if j == 0:
+                    nc.scalar.activation(part, part, COPY, bias=-1.0)
             n_sb[e] = n
+            if e == 0:
+                for u in (2, 3):
+                    nc.scalar.activation(nm_unit(e, u), n[:, :, slots(u)], COPY, bias=-1.0)
 
-        def less_one(e):
-            nc.scalar.activation(n_sb[e][:], n_sb[e][:], COPY, bias=-1.0)
+        def nm_unit(e, u):
+            if u < 2:
+                return n_sb[e][:, :, slots(u)]
+            return late_nm[u - 2][:].rearrange("p (r s) -> p r s", r=PACK)
+
+        def less_one_on_gpsimd(e, u):
+            nc.gpsimd.tensor_scalar(nm_unit(e, u), n_sb[e][:, :, slots(u)], 1.0, -1.0, op0=MULT, op1=ADD)
 
         def w_tile(e, u):
-            return turn[(e + 1) % 2][u][:].rearrange("p (r s) -> p r s", r=PACK)
-
-        def w_on_vector(e, u):
-            nc.vector.scalar_tensor_tensor(
-                out=w_tile(e, u), in0=n_sb[e][:, :, slots(u)], scalar=1.0, in1=a3_sb[e][:, :, slots(u)], op0=SUB, op1=MULT
-            )
+            if u > 0:
+                flat = turn[e % 2][u][:]
+            elif e > 0:
+                flat = w13_grp[(e + 1) % 2][:].bitcast(F32)
+            else:
+                flat = gate_sb[E - 1][:]
+            return flat.rearrange("p (r s) -> p r s", r=PACK)
 
         def w_on_gpsimd(e, u):
-            nc.gpsimd.tensor_tensor(w_tile(e, u), n_sb[e][:, :, slots(u)], a3_sb[e][:, :, slots(u)], MULT)
+            nc.gpsimd.tensor_tensor(w_tile(e, u), nm_unit(e, u), a3_sb[e][:, :, slots(u)], MULT)
 
         def first_product(e, u):
             gc, gs = g_mx[e]
@@ -177,7 +197,7 @@ def tile_moe_bdx_glu_silu_kernel(tc, dyT, a1, a3, w2, w1, w3, gate, offs, pos1, 
             nc.vector.scalar_tensor_tensor(
                 out=m[:], in0=turn[e % 2][u][:], scalar=1.0, in1=dh_ps[e, u][:], op0=ADD, op1=MULT
             )
-            bank = psum.tile([P, PACK, P], F32, name="m_turned", tag="m_turned", bufs=2)
+            bank = psum.tile([P, PACK, P], F32, name="m_turned", tag="m_turned", bufs=3)
             for r in range(PACK):
                 nc.tensor.transpose(bank[:, r, :], m[:, r * P : (r + 1) * P], ident[:])
             m_ps[e, u] = bank
@@ -193,9 +213,9 @@ def tile_moe_bdx_glu_silu_kernel(tc, dyT, a1, a3, w2, w1, w3, gate, offs, pos1, 
 
         def second_product(e, da):
             wc, ws = w13_mx[e]
-            bank = psum.tile([P, C], F32, name="dx", tag="dx", bufs=1)
+            bank = psum.tile([P, C], F32, name="dx", tag="for_scalar", bufs=2)
             codes, scales = da
-            for j in range(2):
+            for j in (1, 0):
                 cols = slice(j * K, (j + 1) * K)
                 half = slice(j * C, (j + 1) * C)
                 nc.tensor.matmul_mx(
@@ -204,94 +224,106 @@ def tile_moe_bdx_glu_silu_kernel(tc, dyT, a1, a3, w2, w1, w3, gate, offs, pos1, 
                     lhsT_scale=ws[:, cols],
                     rhs=codes[:, half].bitcast(E5M2X4),
                     rhs_scale=scales[:, half],
-                    start=j == 0,
-                    stop=j == 1,
+                    start=j == 1,
+                    stop=j == 0,
                 )
             nc.scalar.copy(out=dx_sb[:, e * C : (e + 1) * C], in_=bank[:])
 
-        nc.sync.dma_start(offs_sb[:], offs)
-        load_gate(0)
         dy_rows = dyT.rearrange("(p t) c -> p t c", t=PACK)
-        for t in range(PACK):
+
+        def load_dy(t):
             nc.sync.dma_start(out=dy_sb[t][:], in_=dy_rows[:, t, :])
+
+        nc.sync.dma_start(offs_sb[:], offs)
+        load_dy(0)
+        load_gate(0)
         load_gate(1)
-        load_w2(0)
-        load_a1(0)
+        load_a1(0, 0)
+        load_dy(1)
+        load_a1(0, 1)
+        load_dy(2)
+        load_w2(0, 0)
+        load_dy(3)
+        load_w2(0, 1)
         load_gate(2)
-        load_a3(0)
-        load_a1(1)
-        load_w2(1)
-        load_a3(1)
-        load_w13(0)
         load_gate(3)
-        load_a1(2)
+        load_a3(0)
+        load_a1(1, 0)
+        load_a1(1, 1)
+        load_w2(1, 0)
+        load_w2(1, 1)
+        load_w13(0)
+        load_a3(1)
+        load_a1(2, 0)
+        load_a1(2, 1)
         load_w13(1)
 
         def prepare(e):
-            group_g(e)
             group_w2(e)
+            group_g(e)
+
+        def functions(e):
+            for u in range(UNITS):
+                tanh_turned(e, u)
+            silu_negated(e)
 
         def first_stage(e):
-            w2_mx[e] = quantise(w2_grp[e], "w2", E4M3X4, H)
             g_mx[e] = quantise(g_grp[e], "g", E5M2X4, C)
+            w2_mx[e] = quantise(w2_grp[e], "w2", E4M3X4, H)
 
-        gather(0)
-        prepare(0)
-        silu_negated(0)
-        for u in range(UNITS):
-            tanh_turned(0, u)
-        gather(1)
-        first_stage(0)
-        for u in range(UNITS):
-            w_on_vector(0, u)
-        for e in range(E):
-            if e + 1 < E:
-                silu_negated(e + 1)
-                less_one(e + 1)
+        def window(e):
             da_grp[e] = work.tile([P, 2 * C * PACK], BF16, name="da_grp", tag="da_grp", bufs=1, align_bytes=64)
-            for u in range(UNITS + 1):
-                if u < UNITS:
-                    first_product(e, u)
-                    make_m(e, u)
-                    if e + 1 < E:
-                        w_on_gpsimd(e + 1, u)
-                if u > 0:
-                    make_da(e, u - 1, 1, a1_sb[e][:, :, slots(u - 1)])
-                    make_da(e, u - 1, 0, w_tile(e, u - 1))
+            for step in range(UNITS + 3):
+                if step < UNITS:
+                    first_product(e, step)
+                    make_m(e, step)
+                    w_on_gpsimd(e, step)
+                if 2 <= step < UNITS + 2:
+                    make_da(e, step - 2, 1, a1_unit(e, step - 2))
+                if step >= 3:
+                    make_da(e, step - 3, 0, w_tile(e, step - 3))
+
+        gather((0, 1))
+        prepare(0)
+        functions(0)
+        first_stage(0)
+        gather((2,))
+        gather((3,))
+        da_mx = {}
+        for e in range(E):
+            window(e)
+            if e > 0:
+                second_product(e - 1, da_mx[e - 1])
             if e + 1 < E:
                 prepare(e + 1)
             group_w13(e)
             if e + 1 < E:
-                for u in range(UNITS):
-                    tanh_turned(e + 1, u)
+                functions(e + 1)
+                less_one_on_gpsimd(e + 1, 2)
+                less_one_on_gpsimd(e + 1, 3)
                 first_stage(e + 1)
+            for j in range(2):
+                if e + 2 < E:
+                    load_w2(e + 2, j)
             if e + 2 < E:
-                load_w2(e + 2)
                 load_a3(e + 2)
-            if e + 3 < E:
-                load_a1(e + 3)
-            w13_mx[e] = quantise(w13_grp[e], "w13", E4M3X4, 2 * K)
+            for j in range(2):
+                if e + 3 < E:
+                    load_a1(e + 3, j)
+            if e + 1 == E:
+                w13_mx[e] = quantise(w13_grp[e % 2], "w13", E4M3X4, 2 * K)
+            da_mx[e] = quantise(da_grp[e], "da", E5M2X4, 2 * C, parts=1 if e + 1 < E else 2)
+            if e + 1 < E:
+                w13_mx[e] = quantise(w13_grp[e % 2], "w13", E4M3X4, 2 * K)
             if e + 2 < E:
                 load_w13(e + 2)
             if e == 0:
                 nc.sync.dma_start(pos1_sb[:], pos1)
                 nc.sync.dma_start(pos2_sb[:], pos2)
-            second_product(e, quantise(da_grp[e], "da", E5M2X4, 2 * C, parts=1 if e + 1 < E else 2))
-            if e + 2 < E:
-                gather(e + 2)
+        second_product(E - 1, da_mx[E - 1])
 
-        ends = (0, 512, 768, 1024)
-        pieces = list(zip(ends, ends[1:]))
-
-        def fetch_first(a, b):
+        for a, b in ((0, 512), (512, 1024)):
             nc.vector.tensor_copy(first[:, a:b], dx_sb[:].indirect(pos1_sb[:, a // 16 : b // 16]))
-
-        def add_second(a, b):
+        for a, b in ((0, 512), (512, 896), (896, 1024)):
             nc.vector.tensor_tensor(both[:, a:b], dx_sb[:].indirect(pos2_sb[:, a // 16 : b // 16]), first[:, a:b], ADD)
             nc.sync.dma_start(out=out[:, a:b], in_=both[:, a:b])
-
-        for i, piece in enumerate(pieces):
-            fetch_first(*piece)
-            if i > 0:
-                add_second(*pieces[i - 1])
-        add_second(*pieces[-1])

@@ -98,8 +98,8 @@ def tile_moe_bdx_glu_silu_kernel(tc, dyT, a1, a3, w2, w1, w3, gate, offs, pos1, 
         def group_g(e):
             grp = work.tile([P, C * PACK], BF16, name="g_grp", tag="g_grp", bufs=2, align_bytes=64)
             nc.scalar.copy(
-                out=grp[:].rearrange("p (c i t) -> p c t i", i=4, t=PACK),
-                in_=g_raw[e][:].rearrange("p t (c i) -> p c t i", i=4),
+                out=grp[:].rearrange("p (c i t) -> p c t i", i=2, t=PACK),
+                in_=g_raw[e][:].rearrange("p t (c i) -> p c t i", i=2),
             )
             g_grp[e] = grp
 
@@ -118,8 +118,8 @@ def tile_moe_bdx_glu_silu_kernel(tc, dyT, a1, a3, w2, w1, w3, gate, offs, pos1, 
             grp = w13_grp[e % 2]
             for j, sign in enumerate((-1.0, 1.0)):
                 nc.scalar.activation(
-                    grp[:, j * K * PACK : (j + 1) * K * PACK].rearrange("p (c i r) -> p c r i", i=4, r=PACK),
-                    w13_raw[e][:, j, :].rearrange("p (r c i) -> p c r i", i=4, r=PACK),
+                    grp[:, j * K * PACK : (j + 1) * K * PACK].rearrange("p (c i r) -> p c r i", i=2, r=PACK),
+                    w13_raw[e][:, j, :].rearrange("p (r c i) -> p c r i", i=2, r=PACK),
                     COPY,
                     scale=sign,
                 )
@@ -205,15 +205,15 @@ def tile_moe_bdx_glu_silu_kernel(tc, dyT, a1, a3, w2, w1, w3, gate, offs, pos1, 
         def make_da(e, u, j, factor):
             a = (j * C + u * P) * PACK
             nc.vector.tensor_tensor(
-                da_grp[e][:, a : a + P * PACK].rearrange("p (c i r) -> p c r i", i=4, r=PACK),
-                m_ps[e, u][:].rearrange("p r (c i) -> p c r i", i=4),
-                factor.rearrange("p r (c i) -> p c r i", i=4),
+                da_grp[e][:, a : a + P * PACK].rearrange("p (c i r) -> p c r i", i=2, r=PACK),
+                m_ps[e, u][:].rearrange("p r (c i) -> p c r i", i=2),
+                factor.rearrange("p r (c i) -> p c r i", i=2),
                 MULT,
             )
 
         def second_product(e, da):
             wc, ws = w13_mx[e]
-            bank = psum.tile([P, C], F32, name="dx", tag="for_scalar", bufs=2)
+            bank = psum.tile([P, C], F32, name="dx", tag="dh", bufs=3)
             codes, scales = da
             for j in (1, 0):
                 cols = slice(j * K, (j + 1) * K)
@@ -292,8 +292,6 @@ def tile_moe_bdx_glu_silu_kernel(tc, dyT, a1, a3, w2, w1, w3, gate, offs, pos1, 
         da_mx = {}
         for e in range(E):
             window(e)
-            if e > 0:
-                second_product(e - 1, da_mx[e - 1])
             if e + 1 < E:
                 prepare(e + 1)
             group_w13(e)
@@ -301,6 +299,9 @@ def tile_moe_bdx_glu_silu_kernel(tc, dyT, a1, a3, w2, w1, w3, gate, offs, pos1, 
                 functions(e + 1)
                 less_one_on_gpsimd(e + 1, 2)
                 less_one_on_gpsimd(e + 1, 3)
+            if e > 0:
+                second_product(e - 1, da_mx[e - 1])
+            if e + 1 < E:
                 first_stage(e + 1)
             for j in range(2):
                 if e + 2 < E:

@@ -39,13 +39,12 @@ def tile_moe_bdx_glu_silu_kernel(tc, dyT, a1, a3, w2, w1, w3, gate, offs, pos1, 
         pos1_sb = held.tile([P, T // 16], U16, name="pos1_sb")
         pos2_sb = held.tile([P, T // 16], U16, name="pos2_sb")
         dy_sb = [held.tile([P, T], F32, name="dy%d" % t) for t in range(PACK)]
-        gate_sb = [held.tile([P, C], F32, name="gate%d" % e) for e in range(E)]
-        turn = [[held.tile([P, C], F32, name="turn%d_%d" % (j, u)) for u in range(UNITS)] for j in range(2)]
-        w13_grp = [held.tile([P, 2 * K * PACK], BF16, name="w13_grp%d" % j, align_bytes=64) for j in range(2)]
-        late_nm = [held.tile([P, C], F32, name="late_nm%d" % j) for j in range(2)]
+        gate_sb = held.tile([P, S], F32, name="gate_sb")
+        turn = [held.tile([P, UNITS * H], F32, name="turn%d" % j) for j in range(2)]
+        da_grp = [held.tile([P, 2 * C * PACK], BF16, name="da_grp%d" % j, align_bytes=64) for j in range(2)]
+        nm = held.tile([P, PACK, C], F32, name="nm")
+        early_grp = held.tile([P, 2 * C * PACK], BF16, name="early_grp", align_bytes=64)
         dx_sb = held.tile([P, S], F32, name="dx_sb")
-        first = held.tile([P, T], F32, name="first")
-        both = held.tile([P, T], F32, name="both")
         ident = held.tile([P, P], F32, name="ident")
         warm = held.tile([P, 1], F32, name="warm")
         warm_out = held.tile([P, 1], F32, name="warm_out")
@@ -57,7 +56,7 @@ def tile_moe_bdx_glu_silu_kernel(tc, dyT, a1, a3, w2, w1, w3, gate, offs, pos1, 
         w2_raw, w13_raw, a1_sb, a3_sb = {}, {}, {}, {}
 
         def load_gate(e):
-            nc.sync.dma_start(out=gate_sb[e][:], in_=gate[0:P, e * C : (e + 1) * C])
+            nc.sync.dma_start(out=gate_sb[:, e * C : (e + 1) * C], in_=gate[0:P, e * C : (e + 1) * C])
 
         def load_w2(e, j):
             raw = work.tile([P, PACK, HALF], F32, name="w2_raw", tag="w2_raw", bufs=4)
@@ -84,19 +83,25 @@ def tile_moe_bdx_glu_silu_kernel(tc, dyT, a1, a3, w2, w1, w3, gate, offs, pos1, 
             nc.sync.dma_start(out=raw[:], in_=a3[:, e * C : (e + 1) * C].rearrange("(q r) s -> q r s", r=PACK))
             a3_sb[e] = raw
 
-        g_raw, g_grp, g_mx, w2_grp, w2_mx, w13_mx, n_sb, da_grp = {}, {}, {}, {}, {}, {}, {}, {}
+        g_raw, g_grp, g_mx, w2_grp, w2_mx, w13_grp, w13_mx, n_sb = {}, {}, {}, {}, {}, {}, {}, {}
         dh_ps, m_sb, m_ps = {}, {}, {}
 
         def gather(experts):
             for e in experts:
-                g_raw[e] = work.tile([P, PACK, C], F32, name="g_raw", tag="g_raw", bufs=4)
+                if e + 1 < E:
+                    g_raw[e] = work.tile([P, PACK, C], F32, name="g_raw", tag="g_raw", bufs=3)
+                else:
+                    g_raw[e] = early_grp[:].bitcast(F32).rearrange("p (t c) -> p t c", t=PACK)
             for t in range(PACK):
                 for e in experts:
                     cols = offs_sb[:, e * C // 16 : (e + 1) * C // 16]
-                    nc.vector.tensor_tensor(g_raw[e][:, t, :], dy_sb[t][:].indirect(cols), gate_sb[e][:], MULT)
+                    nc.vector.tensor_tensor(g_raw[e][:, t, :], dy_sb[t][:].indirect(cols), gate_sb[:, e * C : (e + 1) * C], MULT)
 
         def group_g(e):
-            grp = work.tile([P, C * PACK], BF16, name="g_grp", tag="g_grp", bufs=2, align_bytes=64)
+            if e == 0:
+                grp = early_grp[:, H * PACK :]
+            else:
+                grp = work.tile([P, C * PACK], BF16, name="g_grp", tag="g_grp", bufs=2, align_bytes=64)
             nc.scalar.copy(
                 out=grp[:].rearrange("p (c i t) -> p c t i", i=2, t=PACK),
                 in_=g_raw[e][:].rearrange("p t (c i) -> p c t i", i=2),
@@ -104,7 +109,10 @@ def tile_moe_bdx_glu_silu_kernel(tc, dyT, a1, a3, w2, w1, w3, gate, offs, pos1, 
             g_grp[e] = grp
 
         def group_w2(e):
-            grp = work.tile([P, H * PACK], BF16, name="w2_grp", tag="w2_grp", bufs=2, align_bytes=64)
+            if e == 0:
+                grp = early_grp[:, : H * PACK]
+            else:
+                grp = work.tile([P, H * PACK], BF16, name="w2_grp", tag="w2_grp", bufs=2, align_bytes=64)
             for j in range(2):
                 nc.scalar.activation(
                     grp[:].rearrange("p (r q t) -> p q t r", r=PACK, t=PACK)[:, j * P // 2 : (j + 1) * P // 2],
@@ -115,7 +123,8 @@ def tile_moe_bdx_glu_silu_kernel(tc, dyT, a1, a3, w2, w1, w3, gate, offs, pos1, 
             w2_grp[e] = grp
 
         def group_w13(e):
-            grp = w13_grp[e % 2]
+            grp = work.tile([P, 2 * K * PACK], BF16, name="w13_grp", tag="w13_grp", bufs=2, align_bytes=64)
+            w13_grp[e] = grp
             for j, sign in enumerate((-1.0, 1.0)):
                 nc.scalar.activation(
                     grp[:, j * K * PACK : (j + 1) * K * PACK].rearrange("p (c i r) -> p c r i", i=2, r=PACK),
@@ -143,39 +152,35 @@ def tile_moe_bdx_glu_silu_kernel(tc, dyT, a1, a3, w2, w1, w3, gate, offs, pos1, 
             bank = psum.tile([P, PACK, P], F32, name="a1_turned", tag="for_scalar", bufs=2)
             for r in range(PACK):
                 nc.tensor.transpose(bank[:, r, :], a1_unit(e, u)[:, r, :], ident[:])
-            nc.scalar.activation(turn[e % 2][u][:], bank[:].rearrange("p r q -> p (r q)"), TANH, scale=0.5)
+            nc.scalar.activation(turn[e % 2][:, u * H : (u + 1) * H], bank[:].rearrange("p r q -> p (r q)"), TANH, scale=0.5)
 
         def silu_negated(e):
             n = work.tile([P, PACK, C], F32, name="n_sb", tag="n_sb", bufs=2)
             for j in range(2):
                 part = n[:, :, j * HALF : (j + 1) * HALF]
                 nc.scalar.activation(part, a1_sb[e, j][:], SILU, scale=-1.0)
-                if j == 0:
-                    nc.scalar.activation(part, part, COPY, bias=-1.0)
+                if e == 0:
+                    nc.scalar.activation(nm[:, :, j * HALF : (j + 1) * HALF], part, COPY, bias=-1.0)
             n_sb[e] = n
-            if e == 0:
-                for u in (2, 3):
-                    nc.scalar.activation(nm_unit(e, u), n[:, :, slots(u)], COPY, bias=-1.0)
 
-        def nm_unit(e, u):
-            if u < 2:
-                return n_sb[e][:, :, slots(u)]
-            return late_nm[u - 2][:].rearrange("p (r s) -> p r s", r=PACK)
+        def less_one(e):
+            nc.gpsimd.tensor_scalar(nm[:], n_sb[e][:], 1.0, -1.0, op0=MULT, op1=ADD)
 
-        def less_one_on_gpsimd(e, u):
-            nc.gpsimd.tensor_scalar(nm_unit(e, u), n_sb[e][:, :, slots(u)], 1.0, -1.0, op0=MULT, op1=ADD)
-
-        def w_tile(e, u):
-            if u > 0:
-                flat = turn[e % 2][u][:]
-            elif e > 0:
-                flat = w13_grp[(e + 1) % 2][:].bitcast(F32)
+        def w_half(e, j):
+            if e > 0:
+                flat = da_grp[(e + 1) % 2][:].bitcast(F32)[:, j * PACK * HALF : (j + 1) * PACK * HALF]
+            elif j == 0:
+                flat = gate_sb[:, S - PACK * HALF :]
             else:
-                flat = gate_sb[E - 1][:]
+                flat = turn[0][:, PACK * HALF :]
             return flat.rearrange("p (r s) -> p r s", r=PACK)
 
-        def w_on_gpsimd(e, u):
-            nc.gpsimd.tensor_tensor(w_tile(e, u), nm_unit(e, u), a3_sb[e][:, :, slots(u)], MULT)
+        def w_tile(e, u):
+            return w_half(e, u // 2)[:, :, slots(u % 2)]
+
+        def w_on_gpsimd(e, j):
+            half = slice(j * HALF, (j + 1) * HALF)
+            nc.gpsimd.tensor_tensor(w_half(e, j), nm[:, :, half], a3_sb[e][:, :, half], MULT)
 
         def first_product(e, u):
             gc, gs = g_mx[e]
@@ -195,7 +200,7 @@ def tile_moe_bdx_glu_silu_kernel(tc, dyT, a1, a3, w2, w1, w3, gate, offs, pos1, 
         def make_m(e, u):
             m = work.tile([P, H], F32, name="m_sb", tag="m_sb", bufs=3)
             nc.vector.scalar_tensor_tensor(
-                out=m[:], in0=turn[e % 2][u][:], scalar=1.0, in1=dh_ps[e, u][:], op0=ADD, op1=MULT
+                out=m[:], in0=turn[e % 2][:, u * H : (u + 1) * H], scalar=1.0, in1=dh_ps[e, u][:], op0=ADD, op1=MULT
             )
             bank = psum.tile([P, PACK, P], F32, name="m_turned", tag="m_turned", bufs=3)
             for r in range(PACK):
@@ -205,7 +210,7 @@ def tile_moe_bdx_glu_silu_kernel(tc, dyT, a1, a3, w2, w1, w3, gate, offs, pos1, 
         def make_da(e, u, j, factor):
             a = (j * C + u * P) * PACK
             nc.vector.tensor_tensor(
-                da_grp[e][:, a : a + P * PACK].rearrange("p (c i r) -> p c r i", i=2, r=PACK),
+                da_grp[e % 2][:, a : a + P * PACK].rearrange("p (c i r) -> p c r i", i=2, r=PACK),
                 m_ps[e, u][:].rearrange("p r (c i) -> p c r i", i=2),
                 factor.rearrange("p r (c i) -> p c r i", i=2),
                 MULT,
@@ -265,19 +270,21 @@ def tile_moe_bdx_glu_silu_kernel(tc, dyT, a1, a3, w2, w1, w3, gate, offs, pos1, 
         def functions(e):
             for u in range(UNITS):
                 tanh_turned(e, u)
-            silu_negated(e)
 
         def first_stage(e):
             g_mx[e] = quantise(g_grp[e], "g", E5M2X4, C)
             w2_mx[e] = quantise(w2_grp[e], "w2", E4M3X4, H)
 
         def window(e):
-            da_grp[e] = work.tile([P, 2 * C * PACK], BF16, name="da_grp", tag="da_grp", bufs=1, align_bytes=64)
+            for u in range(UNITS - 1):
+                first_product(e, u)
             for step in range(UNITS + 3):
                 if step < UNITS:
-                    first_product(e, step)
                     make_m(e, step)
-                    w_on_gpsimd(e, step)
+                    if step == 0:
+                        first_product(e, UNITS - 1)
+                    if step % 2 == 1:
+                        w_on_gpsimd(e, step // 2)
                 if 2 <= step < UNITS + 2:
                     make_da(e, step - 2, 1, a1_unit(e, step - 2))
                 if step >= 3:
@@ -286,19 +293,20 @@ def tile_moe_bdx_glu_silu_kernel(tc, dyT, a1, a3, w2, w1, w3, gate, offs, pos1, 
         gather((0, 1))
         prepare(0)
         functions(0)
-        first_stage(0)
+        silu_negated(0)
         gather((2,))
+        first_stage(0)
         gather((3,))
         da_mx = {}
         for e in range(E):
             window(e)
             if e + 1 < E:
+                silu_negated(e + 1)
                 prepare(e + 1)
             group_w13(e)
             if e + 1 < E:
                 functions(e + 1)
-                less_one_on_gpsimd(e + 1, 2)
-                less_one_on_gpsimd(e + 1, 3)
+                less_one(e + 1)
             if e > 0:
                 second_product(e - 1, da_mx[e - 1])
             if e + 1 < E:
@@ -311,11 +319,8 @@ def tile_moe_bdx_glu_silu_kernel(tc, dyT, a1, a3, w2, w1, w3, gate, offs, pos1, 
             for j in range(2):
                 if e + 3 < E:
                     load_a1(e + 3, j)
-            if e + 1 == E:
-                w13_mx[e] = quantise(w13_grp[e % 2], "w13", E4M3X4, 2 * K)
-            da_mx[e] = quantise(da_grp[e], "da", E5M2X4, 2 * C, parts=1 if e + 1 < E else 2)
-            if e + 1 < E:
-                w13_mx[e] = quantise(w13_grp[e % 2], "w13", E4M3X4, 2 * K)
+            w13_mx[e] = quantise(w13_grp[e], "w13", E4M3X4, 2 * K)
+            da_mx[e] = quantise(da_grp[e % 2], "da", E5M2X4, 2 * C, parts=1 if e + 1 < E else 2)
             if e + 2 < E:
                 load_w13(e + 2)
             if e == 0:
@@ -323,6 +328,8 @@ def tile_moe_bdx_glu_silu_kernel(tc, dyT, a1, a3, w2, w1, w3, gate, offs, pos1, 
                 nc.sync.dma_start(pos2_sb[:], pos2)
         second_product(E - 1, da_mx[E - 1])
 
+        tokens = work.tile([P, 2, T], F32, name="tokens", tag="g_raw", bufs=3)
+        first, both = tokens[:, 0, :], tokens[:, 1, :]
         for a, b in ((0, 512), (512, 1024)):
             nc.vector.tensor_copy(first[:, a:b], dx_sb[:].indirect(pos1_sb[:, a // 16 : b // 16]))
         for a, b in ((0, 512), (512, 896), (896, 1024)):

@@ -55,8 +55,8 @@ def tile_moe_bdx_glu_silu_kernel(tc, dyT, a1, a3, w2, w1, w3, gate, offs, pos1, 
 
         w2_raw, w13_raw, a1_sb, a3_sb = {}, {}, {}, {}
 
-        def load_gate(e):
-            nc.sync.dma_start(out=gate_sb[:, e * C : (e + 1) * C], in_=gate[0:P, e * C : (e + 1) * C])
+        def load_gate(a, b):
+            nc.sync.dma_start(out=gate_sb[:, a:b], in_=gate[0:P, a:b])
 
         def load_w2(e, j):
             raw = work.tile([P, PACK, HALF], F32, name="w2_raw", tag="w2_raw", bufs=4)
@@ -94,8 +94,12 @@ def tile_moe_bdx_glu_silu_kernel(tc, dyT, a1, a3, w2, w1, w3, gate, offs, pos1, 
                     g_raw[e] = early_grp[:].bitcast(F32).rearrange("p (t c) -> p t c", t=PACK)
             for t in range(PACK):
                 for e in experts:
-                    cols = offs_sb[:, e * C // 16 : (e + 1) * C // 16]
-                    nc.vector.tensor_tensor(g_raw[e][:, t, :], dy_sb[t][:].indirect(cols), gate_sb[:, e * C : (e + 1) * C], MULT)
+                    ends = (0, HALF, C) if (e, t) == (0, 0) else (0, C)
+                    for a, b in zip(ends, ends[1:]):
+                        cols = offs_sb[:, (e * C + a) // 16 : (e * C + b) // 16]
+                        nc.vector.tensor_tensor(
+                            g_raw[e][:, t, a:b], dy_sb[t][:].indirect(cols), gate_sb[:, e * C + a : e * C + b], MULT
+                        )
 
         def group_g(e):
             if e == 0:
@@ -164,7 +168,8 @@ def tile_moe_bdx_glu_silu_kernel(tc, dyT, a1, a3, w2, w1, w3, gate, offs, pos1, 
             n_sb[e] = n
 
         def less_one(e):
-            nc.gpsimd.tensor_scalar(nm[:], n_sb[e][:], 1.0, -1.0, op0=MULT, op1=ADD)
+            nc.gpsimd.tensor_scalar(nm[:, :, : C - P], n_sb[e][:, :, : C - P], 1.0, -1.0, op0=MULT, op1=ADD)
+            nc.scalar.activation(nm[:, :, C - P :], n_sb[e][:, :, C - P :], COPY, bias=-1.0)
 
         def w_half(e, j):
             if e > 0:
@@ -241,8 +246,8 @@ def tile_moe_bdx_glu_silu_kernel(tc, dyT, a1, a3, w2, w1, w3, gate, offs, pos1, 
 
         nc.sync.dma_start(offs_sb[:], offs)
         load_dy(0)
-        load_gate(0)
-        load_gate(1)
+        load_gate(0, HALF)
+        load_gate(HALF, 2 * C)
         load_a1(0, 0)
         load_dy(1)
         load_a1(0, 1)
@@ -250,8 +255,7 @@ def tile_moe_bdx_glu_silu_kernel(tc, dyT, a1, a3, w2, w1, w3, gate, offs, pos1, 
         load_w2(0, 0)
         load_dy(3)
         load_w2(0, 1)
-        load_gate(2)
-        load_gate(3)
+        load_gate(2 * C, S)
         load_a3(0)
         load_a1(1, 0)
         load_a1(1, 1)

@@ -9,6 +9,10 @@ P = 128
 PACK = 4
 UNITS = C // P
 HALF = C // 2
+PAIR = 2
+ON_GPSIMD = 320
+FIRST_PIECES = ((0, 512), (512, 1024))
+SECOND_PIECES = ((0, 512), (512, 896), (896, 1024))
 
 FLOPS = 2 * S * H * N + 2 * 2 * S * H * K
 BYTES = 4 * (N * T + 2 * H * S + S + E * N * H + 2 * E * H * K + K * T) + 2 * P * (S + 2 * T) // 16
@@ -38,107 +42,119 @@ def tile_moe_bdx_glu_silu_kernel(tc, dyT, a1, a3, w2, w1, w3, gate, offs, pos1, 
         offs_sb = held.tile([P, S // 16], U16, name="offs_sb")
         pos1_sb = held.tile([P, T // 16], U16, name="pos1_sb")
         pos2_sb = held.tile([P, T // 16], U16, name="pos2_sb")
-        dy_sb = [held.tile([P, T], F32, name="dy%d" % t) for t in range(PACK)]
+        dy_sb = [held.tile([P, T], F32, name="dy%d" % j) for j in range(PACK)]
         gate_sb = held.tile([P, S], F32, name="gate_sb")
-        turn = [held.tile([P, UNITS * H], F32, name="turn%d" % j) for j in range(2)]
+        tanh_sb = [held.tile([P, UNITS * H], F32, name="tanh%d" % j) for j in range(2)]
         da_grp = [held.tile([P, 2 * C * PACK], BF16, name="da_grp%d" % j, align_bytes=64) for j in range(2)]
-        nm = held.tile([P, PACK, C], F32, name="nm")
+        less_sb = held.tile([P, PACK, C], F32, name="less_sb")
         early_grp = held.tile([P, 2 * C * PACK], BF16, name="early_grp", align_bytes=64)
         dx_sb = held.tile([P, S], F32, name="dx_sb")
         ident = held.tile([P, P], F32, name="ident")
-        warm = held.tile([P, 1], F32, name="warm")
-        warm_out = held.tile([P, 1], F32, name="warm_out")
+        zero_in = held.tile([P, 1], F32, name="zero_in")
+        zero_bias = held.tile([P, 1], F32, name="zero_bias")
 
-        nc.vector.memset(warm[:], 0.0)
-        nc.scalar.activation(warm_out[:], warm[:], SILU)
+        nc.vector.memset(zero_in[:], 0.0)
+        nc.scalar.activation(zero_bias[:], zero_in[:], SILU)
         make_identity(nc, ident[:])
 
+        def unit_slots(u):
+            return slice(u * P, (u + 1) * P)
+
         w2_raw, w13_raw, a1_sb, a3_sb = {}, {}, {}, {}
+        dy_rows = dyT.rearrange("(p j) c -> p j c", j=PACK)
+
+        def load_dy(j):
+            nc.sync.dma_start(out=dy_sb[j][:], in_=dy_rows[:, j, :])
 
         def load_gate(a, b):
             nc.sync.dma_start(out=gate_sb[:, a:b], in_=gate[0:P, a:b])
 
-        def load_w2(e, j):
+        def load_w2(e, half):
             raw = work.tile([P, PACK, HALF], F32, name="w2_raw", tag="w2_raw", bufs=4)
-            nc.sync.dma_start(out=raw[:], in_=w2[e][:, j * HALF : (j + 1) * HALF].rearrange("(p t) i -> p t i", t=PACK))
-            w2_raw[e, j] = raw
+            cols = w2[e][:, half * HALF : (half + 1) * HALF]
+            nc.sync.dma_start(out=raw[:], in_=cols.rearrange("(p j) i -> p j i", j=PACK))
+            w2_raw[e, half] = raw
 
         def load_w13(e):
-            raw = work.tile([P, 2, C], F32, name="w13_raw", tag="w13_raw", bufs=2)
+            raw = work.tile([P, 2, PACK * K], F32, name="w13_raw", tag="w13_raw", bufs=2)
             nc.sync.dma_start(out=raw[:, 0, :], in_=w1[e].rearrange("(q r) k -> q (r k)", r=PACK))
             nc.sync.dma_start(out=raw[:, 1, :], in_=w3[e].rearrange("(q r) k -> q (r k)", r=PACK))
             w13_raw[e] = raw
 
-        def load_a1(e, j):
-            raw = work.tile([P, PACK, HALF], F32, name="a1_sb", tag="a1_sb", bufs=6)
-            a = e * C + j * HALF
+        def load_a1(e, half):
+            if (e, half) == (E - 1, 1):
+                raw = work.tile([P, PACK, HALF], F32, name="a1_last", tag="a1_last", bufs=1, align_bytes=64)
+            else:
+                raw = work.tile([P, PACK, HALF], F32, name="a1_sb", tag="a1_sb", bufs=6)
+            a = e * C + half * HALF
             nc.sync.dma_start(out=raw[:], in_=a1[:, a : a + HALF].rearrange("(q r) s -> q r s", r=PACK))
-            a1_sb[e, j] = raw
+            a1_sb[e, half] = raw
 
         def a1_unit(e, u):
-            return a1_sb[e, u // 2][:, :, slots(u % 2)]
+            return a1_sb[e, u // 2][:, :, unit_slots(u % 2)]
 
         def load_a3(e):
             raw = work.tile([P, PACK, C], F32, name="a3_sb", tag="a3_sb", bufs=2)
             nc.sync.dma_start(out=raw[:], in_=a3[:, e * C : (e + 1) * C].rearrange("(q r) s -> q r s", r=PACK))
             a3_sb[e] = raw
 
-        g_raw, g_grp, g_mx, w2_grp, w2_mx, w13_grp, w13_mx, n_sb = {}, {}, {}, {}, {}, {}, {}, {}
-        dh_ps, m_sb, m_ps = {}, {}, {}
+        g_raw, g_grp, w2_grp, w13_grp = {}, {}, {}, {}
+        g_mx, w2_mx, w13_mx, da_mx = {}, {}, {}, {}
 
         def gather(experts):
             for e in experts:
                 if e + 1 < E:
-                    g_raw[e] = work.tile([P, PACK, C], F32, name="g_raw", tag="g_raw", bufs=3)
+                    g_raw[e] = work.tile([P, PACK, C], F32, name="g_raw", tag="g_raw", bufs=E - 1)
                 else:
-                    g_raw[e] = early_grp[:].bitcast(F32).rearrange("p (t c) -> p t c", t=PACK)
-            for t in range(PACK):
+                    g_raw[e] = early_grp[:].bitcast(F32).rearrange("p (j c) -> p j c", j=PACK)
+            for j in range(PACK):
                 for e in experts:
-                    ends = (0, HALF, C) if (e, t) == (0, 0) else (0, C)
+                    ends = (0, HALF, C) if (e, j) == (0, 0) else (0, C)
                     for a, b in zip(ends, ends[1:]):
                         cols = offs_sb[:, (e * C + a) // 16 : (e * C + b) // 16]
                         nc.vector.tensor_tensor(
-                            g_raw[e][:, t, a:b], dy_sb[t][:].indirect(cols), gate_sb[:, e * C + a : e * C + b], MULT
+                            g_raw[e][:, j, a:b], dy_sb[j][:].indirect(cols), gate_sb[:, e * C + a : e * C + b], MULT
                         )
 
-        def group_g(e):
+        def round_g(e):
             if e == 0:
                 grp = early_grp[:, H * PACK :]
             else:
                 grp = work.tile([P, C * PACK], BF16, name="g_grp", tag="g_grp", bufs=2, align_bytes=64)
             nc.scalar.copy(
-                out=grp[:].rearrange("p (c i t) -> p c t i", i=2, t=PACK),
-                in_=g_raw[e][:].rearrange("p t (c i) -> p c t i", i=2),
+                out=grp[:].rearrange("p (c i j) -> p c j i", i=PAIR, j=PACK),
+                in_=g_raw[e][:].rearrange("p j (c i) -> p c j i", i=PAIR),
             )
             g_grp[e] = grp
 
-        def group_w2(e):
+        def round_w2(e):
             if e == 0:
                 grp = early_grp[:, : H * PACK]
             else:
                 grp = work.tile([P, H * PACK], BF16, name="w2_grp", tag="w2_grp", bufs=2, align_bytes=64)
-            for j in range(2):
+            for half in range(2):
                 nc.scalar.activation(
-                    grp[:].rearrange("p (r q t) -> p q t r", r=PACK, t=PACK)[:, j * P // 2 : (j + 1) * P // 2],
-                    w2_raw[e, j][:].rearrange("p t (q r) -> p q t r", r=PACK),
+                    grp[:].rearrange("p (r q j) -> p q j r", r=PACK, j=PACK)[:, half * P // 2 : (half + 1) * P // 2],
+                    w2_raw[e, half][:].rearrange("p j (q r) -> p q j r", r=PACK),
                     COPY,
                     scale=0.5,
                 )
             w2_grp[e] = grp
 
-        def group_w13(e):
+        def round_w13(e):
             grp = work.tile([P, 2 * K * PACK], BF16, name="w13_grp", tag="w13_grp", bufs=2, align_bytes=64)
             w13_grp[e] = grp
-            for j, sign in enumerate((-1.0, 1.0)):
+            for which, sign in enumerate((-1.0, 1.0)):
                 nc.scalar.activation(
-                    grp[:, j * K * PACK : (j + 1) * K * PACK].rearrange("p (c i r) -> p c r i", i=2, r=PACK),
-                    w13_raw[e][:, j, :].rearrange("p (r c i) -> p c r i", i=2, r=PACK),
+                    grp[:, which * K * PACK : (which + 1) * K * PACK].rearrange("p (c i r) -> p c r i", i=PAIR, r=PACK),
+                    w13_raw[e][:, which, :].rearrange("p (r c i) -> p c r i", i=PAIR, r=PACK),
                     COPY,
                     scale=sign,
                 )
 
-        def quantise(grp, tag, fmt, width, parts=1):
-            codes = work.tile([P, width], U32, name=tag + "_codes", tag=tag + "_codes", bufs=2, align_bytes=64)
+        def quantise(grp, tag, fmt, width, parts=1, codes=None):
+            if codes is None:
+                codes = work.tile([P, width], U32, name=tag + "_codes", tag=tag + "_codes", bufs=2, align_bytes=64)
             scales = work.tile([P, width], U8, name=tag + "_scales", tag=tag + "_scales", bufs=2, align_bytes=64)
             step = width // parts
             for a in reversed(range(0, width, step)):
@@ -149,100 +165,131 @@ def tile_moe_bdx_glu_silu_kernel(tc, dyT, a1, a3, w2, w1, w3, gate, offs, pos1, 
                 )
             return codes, scales
 
-        def slots(u):
-            return slice(u * P, (u + 1) * P)
+        def quantise_g_and_w2(e):
+            g_mx[e] = quantise(g_grp[e], "g", E5M2X4, C)
+            w2_mx[e] = quantise(w2_grp[e], "w2", E4M3X4, H)
 
-        def tanh_turned(e, u):
-            bank = psum.tile([P, PACK, P], F32, name="a1_turned", tag="for_scalar", bufs=2)
-            for r in range(PACK):
-                nc.tensor.transpose(bank[:, r, :], a1_unit(e, u)[:, r, :], ident[:])
-            nc.scalar.activation(turn[e % 2][:, u * H : (u + 1) * H], bank[:].rearrange("p r q -> p (r q)"), TANH, scale=0.5)
-
-        def silu_negated(e):
-            n = work.tile([P, PACK, C], F32, name="n_sb", tag="n_sb", bufs=2)
+        def quantise_late_w13():
+            late = work.tile([P, 4 * K], U32, name="late_codes", tag="a1_last", bufs=1, align_bytes=64)
             for j in range(2):
-                part = n[:, :, j * HALF : (j + 1) * HALF]
-                nc.scalar.activation(part, a1_sb[e, j][:], SILU, scale=-1.0)
+                part = late[:, j * 2 * K : (j + 1) * 2 * K]
+                w13_mx[E - 2 + j] = quantise(w13_grp[E - 2 + j], "w13", E4M3X4, 2 * K, codes=part)
+
+        silu_sb = {}
+
+        def tanh_unit(e, u):
+            return tanh_sb[e % 2][:, u * H : (u + 1) * H]
+
+        def make_tanh(e):
+            for u in range(UNITS):
+                bank = psum.tile([P, PACK, P], F32, name="a1_turned", tag="a1_turned", bufs=2)
+                for r in range(PACK):
+                    nc.tensor.transpose(bank[:, r, :], a1_unit(e, u)[:, r, :], ident[:])
+                nc.scalar.activation(tanh_unit(e, u), bank[:].rearrange("p r q -> p (r q)"), TANH, scale=0.5)
+
+        def make_silu(e):
+            silu = work.tile([P, PACK, C], F32, name="silu_sb", tag="silu_sb", bufs=2)
+            for half in range(2):
+                cols = slice(half * HALF, (half + 1) * HALF)
+                nc.scalar.activation(silu[:, :, cols], a1_sb[e, half][:], SILU, scale=-1.0, bias=zero_bias[:])
                 if e == 0:
-                    nc.scalar.activation(nm[:, :, j * HALF : (j + 1) * HALF], part, COPY, bias=-1.0)
-            n_sb[e] = n
+                    nc.scalar.activation(less_sb[:, :, cols], silu[:, :, cols], COPY, bias=-1.0)
+            silu_sb[e] = silu
 
-        def less_one(e):
-            nc.gpsimd.tensor_scalar(nm[:, :, : C - P], n_sb[e][:, :, : C - P], 1.0, -1.0, op0=MULT, op1=ADD)
-            nc.scalar.activation(nm[:, :, C - P :], n_sb[e][:, :, C - P :], COPY, bias=-1.0)
+        def subtract_one(e):
+            silu = silu_sb[e]
+            nc.gpsimd.tensor_scalar(less_sb[:, :, :ON_GPSIMD], silu[:, :, :ON_GPSIMD], 1.0, -1.0, op0=MULT, op1=ADD)
+            nc.scalar.activation(less_sb[:, :, ON_GPSIMD:], silu[:, :, ON_GPSIMD:], COPY, bias=-1.0)
 
-        def w_half(e, j):
+        def w_half(e, half):
+            words = PACK * HALF
             if e > 0:
-                flat = da_grp[(e + 1) % 2][:].bitcast(F32)[:, j * PACK * HALF : (j + 1) * PACK * HALF]
-            elif j == 0:
-                flat = gate_sb[:, S - PACK * HALF :]
+                flat = da_grp[(e + 1) % 2][:].bitcast(F32)[:, half * words : (half + 1) * words]
+            elif half == 0:
+                flat = gate_sb[:, S - words :]
             else:
-                flat = turn[0][:, PACK * HALF :]
+                flat = tanh_sb[0][:, words:]
             return flat.rearrange("p (r s) -> p r s", r=PACK)
 
-        def w_tile(e, u):
-            return w_half(e, u // 2)[:, :, slots(u % 2)]
+        def w_unit(e, u):
+            return w_half(e, u // 2)[:, :, unit_slots(u % 2)]
 
-        def w_on_gpsimd(e, j):
-            half = slice(j * HALF, (j + 1) * HALF)
-            nc.gpsimd.tensor_tensor(w_half(e, j), nm[:, :, half], a3_sb[e][:, :, half], MULT)
+        def make_w(e, half):
+            cols = slice(half * HALF, (half + 1) * HALF)
+            nc.gpsimd.tensor_tensor(w_half(e, half), less_sb[:, :, cols], a3_sb[e][:, :, cols], MULT)
+
+        dh_ps, m_ps = {}, {}
+        DH_BANKS = 3
+        M_BANKS = 3
 
         def first_product(e, u):
-            gc, gs = g_mx[e]
-            wc, ws = w2_mx[e]
-            bank = psum.tile([P, H], F32, name="dh", tag="dh", bufs=3)
+            g_codes, g_scales = g_mx[e]
+            w_codes, w_scales = w2_mx[e]
+            bank = psum.tile([P, H], F32, name="dh", tag="dh", bufs=DH_BANKS)
             nc.tensor.matmul_mx(
                 out=bank[:],
-                lhsT=gc[:, slots(u)].bitcast(E5M2X4),
-                lhsT_scale=gs[:, slots(u)],
-                rhs=wc[:].bitcast(E4M3X4),
-                rhs_scale=ws[:],
+                lhsT=g_codes[:, unit_slots(u)].bitcast(E5M2X4),
+                lhsT_scale=g_scales[:, unit_slots(u)],
+                rhs=w_codes[:].bitcast(E4M3X4),
+                rhs_scale=w_scales[:],
                 start=True,
                 stop=True,
             )
             dh_ps[e, u] = bank
 
         def make_m(e, u):
-            m = work.tile([P, H], F32, name="m_sb", tag="m_sb", bufs=3)
+            m = work.tile([P, H], F32, name="m_sb", tag="m_sb", bufs=M_BANKS)
             nc.vector.scalar_tensor_tensor(
-                out=m[:], in0=turn[e % 2][:, u * H : (u + 1) * H], scalar=1.0, in1=dh_ps[e, u][:], op0=ADD, op1=MULT
+                out=m[:], in0=tanh_unit(e, u), scalar=1.0, in1=dh_ps[e, u][:], op0=ADD, op1=MULT
             )
-            bank = psum.tile([P, PACK, P], F32, name="m_turned", tag="m_turned", bufs=3)
+            bank = psum.tile([P, PACK, P], F32, name="m_turned", tag="m_turned", bufs=M_BANKS)
             for r in range(PACK):
                 nc.tensor.transpose(bank[:, r, :], m[:, r * P : (r + 1) * P], ident[:])
             m_ps[e, u] = bank
 
-        def make_da(e, u, j, factor):
-            a = (j * C + u * P) * PACK
+        def make_da(e, u, which, factor):
+            a = (which * C + u * P) * PACK
             nc.vector.tensor_tensor(
-                da_grp[e % 2][:, a : a + P * PACK].rearrange("p (c i r) -> p c r i", i=2, r=PACK),
-                m_ps[e, u][:].rearrange("p r (c i) -> p c r i", i=2),
-                factor.rearrange("p r (c i) -> p c r i", i=2),
+                da_grp[e % 2][:, a : a + P * PACK].rearrange("p (c i r) -> p c r i", i=PAIR, r=PACK),
+                m_ps[e, u][:].rearrange("p r (c i) -> p c r i", i=PAIR),
+                factor.rearrange("p r (c i) -> p c r i", i=PAIR),
                 MULT,
             )
 
-        def second_product(e, da):
-            wc, ws = w13_mx[e]
-            bank = psum.tile([P, C], F32, name="dx", tag="dh", bufs=3)
-            codes, scales = da
-            for j in (1, 0):
-                cols = slice(j * K, (j + 1) * K)
-                half = slice(j * C, (j + 1) * C)
+        def run(e):
+            for u in range(DH_BANKS):
+                first_product(e, u)
+            for step in range(UNITS + 3):
+                if step < UNITS:
+                    make_m(e, step)
+                    if step + DH_BANKS < UNITS:
+                        first_product(e, step + DH_BANKS)
+                    if step % 2 == 1:
+                        make_w(e, step // 2)
+                if 2 <= step < UNITS + 2:
+                    make_da(e, step - 2, 1, a1_unit(e, step - 2))
+                if (e, step - 2) == (E - 1, UNITS - 1):
+                    quantise_late_w13()
+                if step >= 3:
+                    make_da(e, step - 3, 0, w_unit(e, step - 3))
+
+        def second_product(e):
+            w_codes, w_scales = w13_mx[e]
+            bank = psum.tile([P, C], F32, name="dx", tag="dh", bufs=DH_BANKS)
+            da_codes, da_scales = da_mx[e]
+            for which in (1, 0):
+                cols = slice(which * K, (which + 1) * K)
+                slots = slice(which * C, (which + 1) * C)
                 nc.tensor.matmul_mx(
                     out=bank[:],
-                    lhsT=wc[:, cols].bitcast(E4M3X4),
-                    lhsT_scale=ws[:, cols],
-                    rhs=codes[:, half].bitcast(E5M2X4),
-                    rhs_scale=scales[:, half],
-                    start=j == 1,
-                    stop=j == 0,
+                    lhsT=w_codes[:, cols].bitcast(E4M3X4),
+                    lhsT_scale=w_scales[:, cols],
+                    rhs=da_codes[:, slots].bitcast(E5M2X4),
+                    rhs_scale=da_scales[:, slots],
+                    start=which == 1,
+                    stop=which == 0,
                 )
             nc.scalar.copy(out=dx_sb[:, e * C : (e + 1) * C], in_=bank[:])
-
-        dy_rows = dyT.rearrange("(p t) c -> p t c", t=PACK)
-
-        def load_dy(t):
-            nc.sync.dma_start(out=dy_sb[t][:], in_=dy_rows[:, t, :])
 
         nc.sync.dma_start(offs_sb[:], offs)
         load_dy(0)
@@ -267,75 +314,56 @@ def tile_moe_bdx_glu_silu_kernel(tc, dyT, a1, a3, w2, w1, w3, gate, offs, pos1, 
         load_a1(2, 1)
         load_w13(1)
 
-        def prepare(e):
-            group_w2(e)
-            group_g(e)
-
-        def functions(e):
-            for u in range(UNITS):
-                tanh_turned(e, u)
-
-        def first_stage(e):
-            g_mx[e] = quantise(g_grp[e], "g", E5M2X4, C)
-            w2_mx[e] = quantise(w2_grp[e], "w2", E4M3X4, H)
-
-        def window(e):
-            for u in range(UNITS - 1):
-                first_product(e, u)
-            for step in range(UNITS + 3):
-                if step < UNITS:
-                    make_m(e, step)
-                    if step == 0:
-                        first_product(e, UNITS - 1)
-                    if step % 2 == 1:
-                        w_on_gpsimd(e, step // 2)
-                if 2 <= step < UNITS + 2:
-                    make_da(e, step - 2, 1, a1_unit(e, step - 2))
-                if step >= 3:
-                    make_da(e, step - 3, 0, w_tile(e, step - 3))
-
         gather((0, 1))
-        prepare(0)
-        functions(0)
-        silu_negated(0)
+        round_w2(0)
+        round_g(0)
+        make_tanh(0)
+        make_silu(0)
         gather((2,))
-        first_stage(0)
+        quantise_g_and_w2(0)
         gather((3,))
-        da_mx = {}
         for e in range(E):
-            window(e)
+            run(e)
             if e + 1 < E:
-                silu_negated(e + 1)
-                prepare(e + 1)
-            group_w13(e)
-            if e + 1 < E:
-                functions(e + 1)
-                less_one(e + 1)
-            if e > 0:
-                second_product(e - 1, da_mx[e - 1])
-            if e + 1 < E:
-                first_stage(e + 1)
-            for j in range(2):
-                if e + 2 < E:
-                    load_w2(e + 2, j)
+                make_silu(e + 1)
+                round_w2(e + 1)
+                round_g(e + 1)
             if e + 2 < E:
+                round_w13(e)
+            if e + 1 < E:
+                make_tanh(e + 1)
+                subtract_one(e + 1)
+            if e == 1:
+                second_product(0)
+            if e + 1 == E:
+                second_product(e - 2)
+                second_product(e - 1)
+            if e + 2 == E:
+                round_w13(e)
+                round_w13(e + 1)
+            if e + 1 < E:
+                quantise_g_and_w2(e + 1)
+            if e + 2 < E:
+                load_w2(e + 2, 0)
+                load_w2(e + 2, 1)
                 load_a3(e + 2)
-            for j in range(2):
-                if e + 3 < E:
-                    load_a1(e + 3, j)
-            w13_mx[e] = quantise(w13_grp[e], "w13", E4M3X4, 2 * K)
+            if e + 3 < E:
+                load_a1(e + 3, 0)
+                load_a1(e + 3, 1)
+            if e + 2 < E:
+                w13_mx[e] = quantise(w13_grp[e], "w13", E4M3X4, 2 * K)
             da_mx[e] = quantise(da_grp[e % 2], "da", E5M2X4, 2 * C, parts=1 if e + 1 < E else 2)
             if e + 2 < E:
                 load_w13(e + 2)
             if e == 0:
                 nc.sync.dma_start(pos1_sb[:], pos1)
                 nc.sync.dma_start(pos2_sb[:], pos2)
-        second_product(E - 1, da_mx[E - 1])
+        second_product(E - 1)
 
-        tokens = work.tile([P, 2, T], F32, name="tokens", tag="g_raw", bufs=3)
+        tokens = work.tile([P, 2, T], F32, name="tokens", tag="g_raw", bufs=E - 1)
         first, both = tokens[:, 0, :], tokens[:, 1, :]
-        for a, b in ((0, 512), (512, 1024)):
+        for a, b in FIRST_PIECES:
             nc.vector.tensor_copy(first[:, a:b], dx_sb[:].indirect(pos1_sb[:, a // 16 : b // 16]))
-        for a, b in ((0, 512), (512, 896), (896, 1024)):
+        for a, b in SECOND_PIECES:
             nc.vector.tensor_tensor(both[:, a:b], dx_sb[:].indirect(pos2_sb[:, a // 16 : b // 16]), first[:, a:b], ADD)
             nc.sync.dma_start(out=out[:, a:b], in_=both[:, a:b])

@@ -10,7 +10,6 @@ PACK = 4
 UNITS = C // P
 HALF = C // 2
 PAIR = 2
-ON_GPSIMD = 320
 FIRST_PIECES = ((0, 512), (512, 1024))
 SECOND_PIECES = ((0, 512), (512, 896), (896, 1024))
 
@@ -42,11 +41,11 @@ def tile_moe_bdx_glu_silu_kernel(tc, dyT, a1, a3, w2, w1, w3, gate, offs, pos1, 
         offs_sb = held.tile([P, S // 16], U16, name="offs_sb")
         pos1_sb = held.tile([P, T // 16], U16, name="pos1_sb")
         pos2_sb = held.tile([P, T // 16], U16, name="pos2_sb")
-        dy_sb = [held.tile([P, T], F32, name="dy%d" % j) for j in range(PACK)]
+        dy_sb = [held.tile([P, T], F32, name="dy%d" % j, tag="dy%d" % j) for j in range(PACK)]
         gate_sb = held.tile([P, S], F32, name="gate_sb")
-        tanh_sb = [held.tile([P, UNITS * H], F32, name="tanh%d" % j) for j in range(2)]
+        tanh_sb = held.tile([P, UNITS * H], F32, name="tanh_sb")
         da_grp = [held.tile([P, 2 * C * PACK], BF16, name="da_grp%d" % j, align_bytes=64) for j in range(2)]
-        less_sb = held.tile([P, PACK, C], F32, name="less_sb")
+        less_sb = held.tile([P, PACK, HALF], F32, name="less_sb")
         early_grp = held.tile([P, 2 * C * PACK], BF16, name="early_grp", align_bytes=64)
         dx_sb = held.tile([P, S], F32, name="dx_sb")
         ident = held.tile([P, P], F32, name="ident")
@@ -69,11 +68,10 @@ def tile_moe_bdx_glu_silu_kernel(tc, dyT, a1, a3, w2, w1, w3, gate, offs, pos1, 
         def load_gate(a, b):
             nc.sync.dma_start(out=gate_sb[:, a:b], in_=gate[0:P, a:b])
 
-        def load_w2(e, half):
-            raw = work.tile([P, PACK, HALF], F32, name="w2_raw", tag="w2_raw", bufs=4)
-            cols = w2[e][:, half * HALF : (half + 1) * HALF]
-            nc.sync.dma_start(out=raw[:], in_=cols.rearrange("(p j) i -> p j i", j=PACK))
-            w2_raw[e, half] = raw
+        def load_w2(e):
+            raw = work.tile([P, PACK, H], F32, name="w2_raw", tag="w2_raw", bufs=2)
+            nc.sync.dma_start(out=raw[:], in_=w2[e].rearrange("(p j) i -> p j i", j=PACK))
+            w2_raw[e] = raw
 
         def load_w13(e):
             raw = work.tile([P, 2, PACK * K], F32, name="w13_raw", tag="w13_raw", bufs=2)
@@ -81,33 +79,37 @@ def tile_moe_bdx_glu_silu_kernel(tc, dyT, a1, a3, w2, w1, w3, gate, offs, pos1, 
             nc.sync.dma_start(out=raw[:, 1, :], in_=w3[e].rearrange("(q r) k -> q (r k)", r=PACK))
             w13_raw[e] = raw
 
-        def load_a1(e, half):
-            if (e, half) == (E - 1, 1):
-                raw = work.tile([P, PACK, HALF], F32, name="a1_last", tag="a1_last", bufs=1, align_bytes=64)
-            else:
-                raw = work.tile([P, PACK, HALF], F32, name="a1_sb", tag="a1_sb", bufs=6)
+        def a1_rows(a, b):
+            return a1[:, a:b].rearrange("(q r) s -> q r s", r=PACK)
+
+        def load_a1_half(e, half):
+            raw = work.tile([P, PACK, HALF], F32, name="a1_half", tag="a1_half%d" % half, bufs=1, align_bytes=64)
             a = e * C + half * HALF
-            nc.sync.dma_start(out=raw[:], in_=a1[:, a : a + HALF].rearrange("(q r) s -> q r s", r=PACK))
-            a1_sb[e, half] = raw
+            nc.sync.dma_start(out=raw[:], in_=a1_rows(a, a + HALF))
+            a1_sb[e, half] = raw[:]
+
+        def load_a1(e):
+            raw = work.tile([P, PACK, C], F32, name="a1_sb", tag="a1_sb%d" % e, bufs=1, align_bytes=64)
+            nc.sync.dma_start(out=raw[:], in_=a1_rows(e * C, (e + 1) * C))
+            for half in range(2):
+                a1_sb[e, half] = raw[:, :, half * HALF : (half + 1) * HALF]
 
         def a1_unit(e, u):
             return a1_sb[e, u // 2][:, :, unit_slots(u % 2)]
 
         def load_a3(e):
-            raw = work.tile([P, PACK, C], F32, name="a3_sb", tag="a3_sb", bufs=2)
+            raw = work.tile([P, PACK, C], F32, name="a3_sb", tag="a3_sb%d" % (e % 2), bufs=1, align_bytes=64)
             nc.sync.dma_start(out=raw[:], in_=a3[:, e * C : (e + 1) * C].rearrange("(q r) s -> q r s", r=PACK))
             a3_sb[e] = raw
 
         g_raw, g_grp, w2_grp, w13_grp = {}, {}, {}, {}
         g_mx, w2_mx, w13_mx, da_mx = {}, {}, {}, {}
+        for e in range(E - 1):
+            g_raw[e] = work.tile([P, PACK, C], F32, name="g_raw", tag="g_raw", bufs=E - 1)
+        g_raw[E - 1] = early_grp[:].bitcast(F32).rearrange("p (j c) -> p j c", j=PACK)
 
-        def gather(experts):
-            for e in experts:
-                if e + 1 < E:
-                    g_raw[e] = work.tile([P, PACK, C], F32, name="g_raw", tag="g_raw", bufs=E - 1)
-                else:
-                    g_raw[e] = early_grp[:].bitcast(F32).rearrange("p (j c) -> p j c", j=PACK)
-            for j in range(PACK):
+        def gather(experts, planes):
+            for j in planes:
                 for e in experts:
                     ends = (0, HALF, C) if (e, j) == (0, 0) else (0, C)
                     for a, b in zip(ends, ends[1:]):
@@ -120,7 +122,7 @@ def tile_moe_bdx_glu_silu_kernel(tc, dyT, a1, a3, w2, w1, w3, gate, offs, pos1, 
             if e == 0:
                 grp = early_grp[:, H * PACK :]
             else:
-                grp = work.tile([P, C * PACK], BF16, name="g_grp", tag="g_grp", bufs=2, align_bytes=64)
+                grp = work.tile([P, C * PACK], BF16, name="g_grp", tag="g_grp%d" % e, bufs=1, align_bytes=64)
             nc.scalar.copy(
                 out=grp[:].rearrange("p (c i j) -> p c j i", i=PAIR, j=PACK),
                 in_=g_raw[e][:].rearrange("p j (c i) -> p c j i", i=PAIR),
@@ -128,34 +130,30 @@ def tile_moe_bdx_glu_silu_kernel(tc, dyT, a1, a3, w2, w1, w3, gate, offs, pos1, 
             g_grp[e] = grp
 
         def round_w2(e):
-            if e == 0:
-                grp = early_grp[:, : H * PACK]
-            else:
-                grp = work.tile([P, H * PACK], BF16, name="w2_grp", tag="w2_grp", bufs=2, align_bytes=64)
-            for half in range(2):
-                nc.scalar.activation(
-                    grp[:].rearrange("p (r q j) -> p q j r", r=PACK, j=PACK)[:, half * P // 2 : (half + 1) * P // 2],
-                    w2_raw[e, half][:].rearrange("p j (q r) -> p q j r", r=PACK),
-                    COPY,
-                    scale=0.5,
-                )
+            grp = work.tile([P, H * PACK], BF16, name="w2_grp", tag="w2_grp", bufs=2, align_bytes=64)
+            nc.scalar.activation(
+                grp[:].rearrange("p (r q j) -> p q j r", r=PACK, j=PACK),
+                w2_raw[e][:].rearrange("p j (q r) -> p q j r", r=PACK),
+                COPY,
+                scale=0.5,
+            )
             w2_grp[e] = grp
 
         def round_w13(e):
-            grp = work.tile([P, 2 * K * PACK], BF16, name="w13_grp", tag="w13_grp", bufs=2, align_bytes=64)
-            w13_grp[e] = grp
-            for which, sign in enumerate((-1.0, 1.0)):
-                nc.scalar.activation(
-                    grp[:, which * K * PACK : (which + 1) * K * PACK].rearrange("p (c i r) -> p c r i", i=PAIR, r=PACK),
-                    w13_raw[e][:, which, :].rearrange("p (r c i) -> p c r i", i=PAIR, r=PACK),
-                    COPY,
-                    scale=sign,
+            if e % 2 == 0:
+                w13_grp[e // 2] = work.tile(
+                    [P, 4 * K * PACK], BF16, name="w13_grp", tag="w13_grp", bufs=1, align_bytes=64
                 )
+            a = (e % 2) * 2 * K * PACK
+            nc.scalar.copy(
+                out=w13_grp[e // 2][:, a : a + 2 * K * PACK].rearrange("p (w c i r) -> p w c r i", w=2, i=PAIR, r=PACK),
+                in_=w13_raw[e][:].rearrange("p w (r c i) -> p w c r i", i=PAIR, r=PACK),
+            )
 
-        def quantise(grp, tag, fmt, width, parts=1, codes=None):
+        def quantise(grp, tag, fmt, width, parts=1, codes=None, bufs=2):
             if codes is None:
                 codes = work.tile([P, width], U32, name=tag + "_codes", tag=tag + "_codes", bufs=2, align_bytes=64)
-            scales = work.tile([P, width], U8, name=tag + "_scales", tag=tag + "_scales", bufs=2, align_bytes=64)
+            scales = work.tile([P, width], U8, name=tag + "_scales", tag=tag + "_scales", bufs=bufs, align_bytes=64)
             step = width // parts
             for a in reversed(range(0, width, step)):
                 nc.vector.quantize_mx(
@@ -165,67 +163,80 @@ def tile_moe_bdx_glu_silu_kernel(tc, dyT, a1, a3, w2, w1, w3, gate, offs, pos1, 
                 )
             return codes, scales
 
-        def quantise_g_and_w2(e):
-            g_mx[e] = quantise(g_grp[e], "g", E5M2X4, C)
-            w2_mx[e] = quantise(w2_grp[e], "w2", E4M3X4, H)
+        codes_sb = {}
 
-        def quantise_late_w13():
-            late = work.tile([P, 4 * K], U32, name="late_codes", tag="a1_last", bufs=1, align_bytes=64)
-            for j in range(2):
-                part = late[:, j * 2 * K : (j + 1) * 2 * K]
-                w13_mx[E - 2 + j] = quantise(w13_grp[E - 2 + j], "w13", E4M3X4, 2 * K, codes=part)
+        def operand_codes(e):
+            if e not in codes_sb:
+                tag = ("codes0", "a3_sb0", "a1_sb1", "a1_sb2")[e]
+                codes_sb[e] = work.tile([P, 3 * C], U32, name="codes", tag=tag, bufs=1, align_bytes=64)
+            return codes_sb[e]
+
+        def quantise_w2(e):
+            w2_mx[e] = quantise(w2_grp[e], "w2", E4M3X4, H, codes=operand_codes(e)[:, :H])
+
+        def quantise_g(e):
+            g_mx[e] = quantise(g_grp[e], "g", E5M2X4, C, codes=operand_codes(e)[:, H : H + C])
+
+        def quantise_da(e):
+            codes = work.tile([P, 2 * C], U32, name="da_codes", tag="g_grp%d" % (e + 1), bufs=1, align_bytes=64)
+            da_mx[e] = quantise(da_grp[e % 2], "da", E5M2X4, 2 * C, parts=1 if e + 1 < E else 2, codes=codes, bufs=E)
+
+        def quantise_w13(pair):
+            if pair == 0:
+                codes = operand_codes(2)[:, H + C :]
+            else:
+                codes = work.tile([P, 4 * K], U32, name="w13_codes", tag="a1_half1", bufs=1, align_bytes=64)
+            w13_mx[pair] = quantise(w13_grp[pair], "w13", E4M3X4, 4 * K, codes=codes)
 
         silu_sb = {}
 
-        def tanh_unit(e, u):
-            return tanh_sb[e % 2][:, u * H : (u + 1) * H]
+        BANKS = 4
 
-        def make_tanh(e):
-            for u in range(UNITS):
-                bank = psum.tile([P, PACK, P], F32, name="a1_turned", tag="a1_turned", bufs=2)
+        def tanh_unit(u):
+            return tanh_sb[:, u * H : (u + 1) * H]
+
+        def make_tanh(e, units):
+            for u in units:
+                bank = psum.tile([P, PACK, P], F32, name="a1_turned", tag="turned", bufs=BANKS)
                 for r in range(PACK):
                     nc.tensor.transpose(bank[:, r, :], a1_unit(e, u)[:, r, :], ident[:])
-                nc.scalar.activation(tanh_unit(e, u), bank[:].rearrange("p r q -> p (r q)"), TANH, scale=0.5)
+                nc.scalar.activation(tanh_unit(u), bank[:].rearrange("p r q -> p (r q)"), TANH, scale=0.5)
 
-        def make_silu(e):
-            silu = work.tile([P, PACK, C], F32, name="silu_sb", tag="silu_sb", bufs=2)
-            for half in range(2):
-                cols = slice(half * HALF, (half + 1) * HALF)
-                nc.scalar.activation(silu[:, :, cols], a1_sb[e, half][:], SILU, scale=-1.0, bias=zero_bias[:])
-                if e == 0:
-                    nc.scalar.activation(less_sb[:, :, cols], silu[:, :, cols], COPY, bias=-1.0)
-            silu_sb[e] = silu
+        def make_silu(e, half):
+            silu = work.tile([P, PACK, HALF], F32, name="silu_sb", tag="silu_sb%d" % half, bufs=2)
+            nc.scalar.activation(silu[:], a1_sb[e, half], SILU, scale=-1.0, bias=zero_bias[:])
+            if half == 1:
+                nc.scalar.activation(silu[:], silu[:], COPY, scale=-1.0, bias=1.0)
+            elif e == 0:
+                nc.scalar.activation(less_sb[:], silu[:], COPY, scale=-1.0, bias=1.0)
+            silu_sb[e, half] = silu
 
         def subtract_one(e):
-            silu = silu_sb[e]
-            nc.gpsimd.tensor_scalar(less_sb[:, :, :ON_GPSIMD], silu[:, :, :ON_GPSIMD], 1.0, -1.0, op0=MULT, op1=ADD)
-            nc.scalar.activation(less_sb[:, :, ON_GPSIMD:], silu[:, :, ON_GPSIMD:], COPY, bias=-1.0)
+            nc.gpsimd.tensor_scalar(less_sb[:], silu_sb[e, 0][:], -1.0, 1.0, op0=MULT, op1=ADD)
 
-        def w_half(e, half):
+        w_sb = {}
+
+        def make_w(e, half):
             words = PACK * HALF
             if e > 0:
                 flat = da_grp[(e + 1) % 2][:].bitcast(F32)[:, half * words : (half + 1) * words]
             elif half == 0:
                 flat = gate_sb[:, S - words :]
             else:
-                flat = tanh_sb[0][:, words:]
-            return flat.rearrange("p (r s) -> p r s", r=PACK)
+                flat = held.tile([P, words], F32, name="w_first", tag="dy%d" % (PACK - 1))[:]
+            w_sb[e, half] = flat.rearrange("p (r s) -> p r s", r=PACK)
+            less = less_sb if half == 0 else silu_sb[e, half]
+            nc.gpsimd.tensor_tensor(w_sb[e, half], less[:], a3_sb[e][:, :, half * HALF : (half + 1) * HALF], MULT)
 
         def w_unit(e, u):
-            return w_half(e, u // 2)[:, :, unit_slots(u % 2)]
-
-        def make_w(e, half):
-            cols = slice(half * HALF, (half + 1) * HALF)
-            nc.gpsimd.tensor_tensor(w_half(e, half), less_sb[:, :, cols], a3_sb[e][:, :, cols], MULT)
+            return w_sb[e, u // 2][:, :, unit_slots(u % 2)]
 
         dh_ps, m_ps = {}, {}
-        DH_BANKS = 3
-        M_BANKS = 3
 
         def first_product(e, u):
             g_codes, g_scales = g_mx[e]
             w_codes, w_scales = w2_mx[e]
-            bank = psum.tile([P, H], F32, name="dh", tag="dh", bufs=DH_BANKS)
+            bank = psum.tile([P, H], F32, name="dh", tag="dh", bufs=BANKS)
             nc.tensor.matmul_mx(
                 out=bank[:],
                 lhsT=g_codes[:, unit_slots(u)].bitcast(E5M2X4),
@@ -238,11 +249,11 @@ def tile_moe_bdx_glu_silu_kernel(tc, dyT, a1, a3, w2, w1, w3, gate, offs, pos1, 
             dh_ps[e, u] = bank
 
         def make_m(e, u):
-            m = work.tile([P, H], F32, name="m_sb", tag="m_sb", bufs=M_BANKS)
+            m = work.tile([P, H], F32, name="m_sb", tag="m_sb", bufs=UNITS)
             nc.vector.scalar_tensor_tensor(
-                out=m[:], in0=tanh_unit(e, u), scalar=1.0, in1=dh_ps[e, u][:], op0=ADD, op1=MULT
+                out=m[:], in0=tanh_unit(u), scalar=1.0, in1=dh_ps[e, u][:], op0=ADD, op1=MULT
             )
-            bank = psum.tile([P, PACK, P], F32, name="m_turned", tag="m_turned", bufs=M_BANKS)
+            bank = psum.tile([P, PACK, P], F32, name="m_turned", tag="turned", bufs=BANKS)
             for r in range(PACK):
                 nc.tensor.transpose(bank[:, r, :], m[:, r * P : (r + 1) * P], ident[:])
             m_ps[e, u] = bank
@@ -257,28 +268,28 @@ def tile_moe_bdx_glu_silu_kernel(tc, dyT, a1, a3, w2, w1, w3, gate, offs, pos1, 
             )
 
         def run(e):
-            for u in range(DH_BANKS):
+            for u in range(UNITS):
                 first_product(e, u)
-            for step in range(UNITS + 3):
-                if step < UNITS:
-                    make_m(e, step)
-                    if step + DH_BANKS < UNITS:
-                        first_product(e, step + DH_BANKS)
-                    if step % 2 == 1:
-                        make_w(e, step // 2)
-                if 2 <= step < UNITS + 2:
-                    make_da(e, step - 2, 1, a1_unit(e, step - 2))
-                if (e, step - 2) == (E - 1, UNITS - 1):
-                    quantise_late_w13()
-                if step >= 3:
-                    make_da(e, step - 3, 0, w_unit(e, step - 3))
+            make_w(e, 0)
+            make_w(e, 1)
+            if e + 1 < E:
+                subtract_one(e + 1)
+            for u in range(UNITS):
+                make_m(e, u)
+            make_da(e, 0, 1, a1_unit(e, 0))
+            for u in range(UNITS):
+                if u + 1 < UNITS:
+                    make_da(e, u + 1, 1, a1_unit(e, u + 1))
+                if (e, u + 1) == (E - 1, UNITS - 1):
+                    quantise_w13(1)
+                make_da(e, u, 0, w_unit(e, u))
 
         def second_product(e):
-            w_codes, w_scales = w13_mx[e]
-            bank = psum.tile([P, C], F32, name="dx", tag="dh", bufs=DH_BANKS)
+            w_codes, w_scales = w13_mx[e // 2]
+            bank = psum.tile([P, C], F32, name="dx", tag="turned", bufs=BANKS)
             da_codes, da_scales = da_mx[e]
             for which in (1, 0):
-                cols = slice(which * K, (which + 1) * K)
+                cols = slice((2 * (e % 2) + which) * K, (2 * (e % 2) + which + 1) * K)
                 slots = slice(which * C, (which + 1) * C)
                 nc.tensor.matmul_mx(
                     out=bank[:],
@@ -295,70 +306,84 @@ def tile_moe_bdx_glu_silu_kernel(tc, dyT, a1, a3, w2, w1, w3, gate, offs, pos1, 
         load_dy(0)
         load_gate(0, HALF)
         load_gate(HALF, 2 * C)
-        load_a1(0, 0)
+        load_a1_half(0, 0)
+        load_gate(2 * C, 3 * C)
         load_dy(1)
-        load_a1(0, 1)
+        load_a1_half(0, 1)
         load_dy(2)
-        load_w2(0, 0)
+        load_w2(0)
         load_dy(3)
-        load_w2(0, 1)
-        load_gate(2 * C, S)
+        load_gate(3 * C, S)
+        load_a1(1)
+        load_w2(1)
         load_a3(0)
-        load_a1(1, 0)
-        load_a1(1, 1)
-        load_w2(1, 0)
-        load_w2(1, 1)
+        load_a1(2)
         load_w13(0)
-        load_a3(1)
-        load_a1(2, 0)
-        load_a1(2, 1)
         load_w13(1)
 
-        gather((0, 1))
+        gather((0, 1, 2), range(PACK))
+        for half in range(2):
+            make_tanh(0, (2 * half, 2 * half + 1))
+            make_silu(0, half)
         round_w2(0)
+        load_w2(2)
+        load_a3(1)
         round_g(0)
-        make_tanh(0)
-        make_silu(0)
-        gather((2,))
-        quantise_g_and_w2(0)
-        gather((3,))
-        for e in range(E):
-            run(e)
-            if e + 1 < E:
-                make_silu(e + 1)
-                round_w2(e + 1)
-                round_g(e + 1)
-            if e + 2 < E:
-                round_w13(e)
-            if e + 1 < E:
-                make_tanh(e + 1)
-                subtract_one(e + 1)
-            if e == 1:
-                second_product(0)
-            if e + 1 == E:
-                second_product(e - 2)
-                second_product(e - 1)
-            if e + 2 == E:
-                round_w13(e)
-                round_w13(e + 1)
-            if e + 1 < E:
-                quantise_g_and_w2(e + 1)
-            if e + 2 < E:
-                load_w2(e + 2, 0)
-                load_w2(e + 2, 1)
-                load_a3(e + 2)
-            if e + 3 < E:
-                load_a1(e + 3, 0)
-                load_a1(e + 3, 1)
-            if e + 2 < E:
-                w13_mx[e] = quantise(w13_grp[e], "w13", E4M3X4, 2 * K)
-            da_mx[e] = quantise(da_grp[e % 2], "da", E5M2X4, 2 * C, parts=1 if e + 1 < E else 2)
-            if e + 2 < E:
-                load_w13(e + 2)
-            if e == 0:
-                nc.sync.dma_start(pos1_sb[:], pos1)
-                nc.sync.dma_start(pos2_sb[:], pos2)
-        second_product(E - 1)
+        gather((3,), (0, 1))
+        quantise_w2(0)
+        quantise_g(0)
+        gather((3,), (2, 3))
+        make_silu(1, 0)
+        make_silu(1, 1)
+        round_w2(1)
+        load_w2(3)
+        round_g(1)
+        round_w13(0)
+        make_silu(2, 0)
+        round_w13(1)
+        round_w2(2)
+
+        run(0)
+        load_a1_half(3, 0)
+        load_a1_half(3, 1)
+        load_w13(2)
+        load_w13(3)
+        nc.sync.dma_start(pos1_sb[:], pos1)
+        nc.sync.dma_start(pos2_sb[:], pos2)
+        quantise_w2(1)
+        quantise_g(1)
+        quantise_da(0)
+        load_a3(2)
+        make_tanh(1, range(UNITS))
+        round_g(2)
+        make_silu(3, 0)
+        make_silu(2, 1)
+
+        run(1)
+        load_a3(3)
+        quantise_w2(2)
+        quantise_g(2)
+        quantise_w13(0)
+        quantise_da(1)
+        make_tanh(2, range(UNITS))
+        round_w2(3)
+        round_g(3)
+        make_silu(3, 1)
+
+        run(2)
+        quantise_w2(3)
+        quantise_g(3)
+        quantise_da(2)
+        make_tanh(3, range(UNITS))
+        round_w13(2)
+        round_w13(3)
+
+        run(3)
+        second_product(0)
+        second_product(1)
+        second_product(2)
+        quantise_da(3)
+        second_product(3)
 
         tokens = work.tile([P, 2, T], F32, name="tokens", tag="g_raw", bufs=E - 1)
         first, both = tokens[:, 0, :], tokens[:, 1, :]

@@ -9,6 +9,7 @@ P = 128
 PACK = 4
 UNITS = C // P
 HALF = C // 2
+FRONT = (E - 1) * C
 PAIR = 2
 FIRST_PIECES = ((0, 512), (512, 1024))
 SECOND_PIECES = ((0, 512), (512, 896), (896, 1024))
@@ -74,7 +75,7 @@ def tile_moe_bdx_glu_silu_kernel(tc, dyT, a1, a3, w2, w1, w3, gate, offs, pos1, 
             w2_raw[e] = raw
 
         def load_w13(e):
-            raw = work.tile([P, 2, PACK * K], F32, name="w13_raw", tag="w13_raw", bufs=2)
+            raw = work.tile([P, 2, PACK * K], F32, name="w13_raw", tag="w13_raw", bufs=E)
             nc.sync.dma_start(out=raw[:, 0, :], in_=w1[e].rearrange("(q r) k -> q (r k)", r=PACK))
             nc.sync.dma_start(out=raw[:, 1, :], in_=w3[e].rearrange("(q r) k -> q (r k)", r=PACK))
             w13_raw[e] = raw
@@ -102,21 +103,17 @@ def tile_moe_bdx_glu_silu_kernel(tc, dyT, a1, a3, w2, w1, w3, gate, offs, pos1, 
             nc.sync.dma_start(out=raw[:], in_=a3[:, e * C : (e + 1) * C].rearrange("(q r) s -> q r s", r=PACK))
             a3_sb[e] = raw
 
-        g_raw, g_grp, w2_grp, w13_grp = {}, {}, {}, {}
+        g_raw, g_grp, w2_grp = {}, {}, {}
+        w13_grp = held.tile([P, E, 2 * K * PACK], BF16, name="w13_grp", align_bytes=64)
         g_mx, w2_mx, w13_mx, da_mx = {}, {}, {}, {}
+        front = work.tile([P, PACK, FRONT], F32, name="front", tag="front", bufs=1)
         for e in range(E - 1):
-            g_raw[e] = work.tile([P, PACK, C], F32, name="g_raw", tag="g_raw", bufs=E - 1)
+            g_raw[e] = front[:, :, e * C : (e + 1) * C]
         g_raw[E - 1] = early_grp[:].bitcast(F32).rearrange("p (j c) -> p j c", j=PACK)
 
-        def gather(experts, planes):
-            for j in planes:
-                for e in experts:
-                    ends = (0, HALF, C) if (e, j) == (0, 0) else (0, C)
-                    for a, b in zip(ends, ends[1:]):
-                        cols = offs_sb[:, (e * C + a) // 16 : (e * C + b) // 16]
-                        nc.vector.tensor_tensor(
-                            g_raw[e][:, j, a:b], dy_sb[j][:].indirect(cols), gate_sb[:, e * C + a : e * C + b], MULT
-                        )
+        def gather(j, a, b):
+            into = front[:, j, a:b] if b <= FRONT else g_raw[E - 1][:, j, :]
+            nc.vector.tensor_tensor(into, dy_sb[j][:].indirect(offs_sb[:, a // 16 : b // 16]), gate_sb[:, a:b], MULT)
 
         def round_g(e):
             if e == 0:
@@ -125,7 +122,7 @@ def tile_moe_bdx_glu_silu_kernel(tc, dyT, a1, a3, w2, w1, w3, gate, offs, pos1, 
                 grp = work.tile([P, C * PACK], BF16, name="g_grp", tag="g_grp%d" % e, bufs=1, align_bytes=64)
             nc.scalar.copy(
                 out=grp[:].rearrange("p (c i j) -> p c j i", i=PAIR, j=PACK),
-                in_=g_raw[e][:].rearrange("p j (c i) -> p c j i", i=PAIR),
+                in_=g_raw[e].rearrange("p j (c i) -> p c j i", i=PAIR),
             )
             g_grp[e] = grp
 
@@ -140,13 +137,8 @@ def tile_moe_bdx_glu_silu_kernel(tc, dyT, a1, a3, w2, w1, w3, gate, offs, pos1, 
             w2_grp[e] = grp
 
         def round_w13(e):
-            if e % 2 == 0:
-                w13_grp[e // 2] = work.tile(
-                    [P, 4 * K * PACK], BF16, name="w13_grp", tag="w13_grp", bufs=1, align_bytes=64
-                )
-            a = (e % 2) * 2 * K * PACK
             nc.scalar.copy(
-                out=w13_grp[e // 2][:, a : a + 2 * K * PACK].rearrange("p (w c i r) -> p w c r i", w=2, i=PAIR, r=PACK),
+                out=w13_grp[:, e, :].rearrange("p (w c i r) -> p w c r i", w=2, i=PAIR, r=PACK),
                 in_=w13_raw[e][:].rearrange("p w (r c i) -> p w c r i", i=PAIR, r=PACK),
             )
 
@@ -168,7 +160,7 @@ def tile_moe_bdx_glu_silu_kernel(tc, dyT, a1, a3, w2, w1, w3, gate, offs, pos1, 
         def operand_codes(e):
             if e not in codes_sb:
                 tag = ("codes0", "a3_sb0", "a1_sb1", "a1_sb2")[e]
-                codes_sb[e] = work.tile([P, 3 * C], U32, name="codes", tag=tag, bufs=1, align_bytes=64)
+                codes_sb[e] = work.tile([P, H + C + 2 * K], U32, name="codes", tag=tag, bufs=1, align_bytes=64)
             return codes_sb[e]
 
         def quantise_w2(e):
@@ -181,12 +173,17 @@ def tile_moe_bdx_glu_silu_kernel(tc, dyT, a1, a3, w2, w1, w3, gate, offs, pos1, 
             codes = work.tile([P, 2 * C], U32, name="da_codes", tag="g_grp%d" % (e + 1), bufs=1, align_bytes=64)
             da_mx[e] = quantise(da_grp[e % 2], "da", E5M2X4, 2 * C, parts=1 if e + 1 < E else 2, codes=codes, bufs=E)
 
-        def quantise_w13(pair):
-            if pair == 0:
-                codes = operand_codes(2)[:, H + C :]
-            else:
-                codes = work.tile([P, 4 * K], U32, name="w13_codes", tag="a1_half1", bufs=1, align_bytes=64)
-            w13_mx[pair] = quantise(w13_grp[pair], "w13", E4M3X4, 4 * K, codes=codes)
+        def quantise_w13(first, count, codes):
+            grp = w13_grp[:, first : first + count, :].rearrange("p e c -> p (e c)")
+            codes, scales = quantise(grp, "w13_%d" % first, E4M3X4, count * 2 * K, codes=codes, bufs=1)
+            for j in range(count):
+                cols = slice(j * 2 * K, (j + 1) * 2 * K)
+                w13_mx[first + j] = codes[:, cols], scales[:, cols]
+
+        def quantise_late_w13():
+            codes = work.tile([P, (E - 1) * 2 * K], U32, name="late_codes", tag="a1_half1", bufs=1, align_bytes=64)
+            quantise_w13(1, 1, codes[:, : 2 * K])
+            quantise_w13(2, 2, codes[:, 2 * K :])
 
         silu_sb = {}
 
@@ -281,15 +278,15 @@ def tile_moe_bdx_glu_silu_kernel(tc, dyT, a1, a3, w2, w1, w3, gate, offs, pos1, 
                 if u + 1 < UNITS:
                     make_da(e, u + 1, 1, a1_unit(e, u + 1))
                 if (e, u + 1) == (E - 1, UNITS - 1):
-                    quantise_w13(1)
+                    quantise_late_w13()
                 make_da(e, u, 0, w_unit(e, u))
 
         def second_product(e):
-            w_codes, w_scales = w13_mx[e // 2]
+            w_codes, w_scales = w13_mx[e]
             bank = psum.tile([P, C], F32, name="dx", tag="turned", bufs=BANKS)
             da_codes, da_scales = da_mx[e]
             for which in (1, 0):
-                cols = slice((2 * (e % 2) + which) * K, (2 * (e % 2) + which + 1) * K)
+                cols = slice(which * K, (which + 1) * K)
                 slots = slice(which * C, (which + 1) * C)
                 nc.tensor.matmul_mx(
                     out=bank[:],
@@ -319,9 +316,11 @@ def tile_moe_bdx_glu_silu_kernel(tc, dyT, a1, a3, w2, w1, w3, gate, offs, pos1, 
         load_a3(0)
         load_a1(2)
         load_w13(0)
-        load_w13(1)
 
-        gather((0, 1, 2), range(PACK))
+        for j in range(PACK):
+            ends = (0, HALF, 2 * C, FRONT) if j == 0 else (0, FRONT // 2, FRONT)
+            for a, b in zip(ends, ends[1:]):
+                gather(j, a, b)
         for half in range(2):
             make_tanh(0, (2 * half, 2 * half + 1))
             make_silu(0, half)
@@ -329,25 +328,23 @@ def tile_moe_bdx_glu_silu_kernel(tc, dyT, a1, a3, w2, w1, w3, gate, offs, pos1, 
         load_w2(2)
         load_a3(1)
         round_g(0)
-        gather((3,), (0, 1))
+        gather(0, FRONT, S)
+        gather(1, FRONT, S)
         quantise_w2(0)
         quantise_g(0)
-        gather((3,), (2, 3))
+        gather(2, FRONT, S)
+        gather(3, FRONT, S)
         make_silu(1, 0)
         make_silu(1, 1)
         round_w2(1)
         load_w2(3)
         round_g(1)
-        round_w13(0)
         make_silu(2, 0)
-        round_w13(1)
-        round_w2(2)
+        round_w13(0)
 
         run(0)
         load_a1_half(3, 0)
         load_a1_half(3, 1)
-        load_w13(2)
-        load_w13(3)
         nc.sync.dma_start(pos1_sb[:], pos1)
         nc.sync.dma_start(pos2_sb[:], pos2)
         quantise_w2(1)
@@ -355,15 +352,17 @@ def tile_moe_bdx_glu_silu_kernel(tc, dyT, a1, a3, w2, w1, w3, gate, offs, pos1, 
         quantise_da(0)
         load_a3(2)
         make_tanh(1, range(UNITS))
+        round_w2(2)
         round_g(2)
         make_silu(3, 0)
         make_silu(2, 1)
 
         run(1)
         load_a3(3)
+        for e in range(1, E):
+            load_w13(e)
         quantise_w2(2)
         quantise_g(2)
-        quantise_w13(0)
         quantise_da(1)
         make_tanh(2, range(UNITS))
         round_w2(3)
@@ -373,10 +372,11 @@ def tile_moe_bdx_glu_silu_kernel(tc, dyT, a1, a3, w2, w1, w3, gate, offs, pos1, 
         run(2)
         quantise_w2(3)
         quantise_g(3)
+        quantise_w13(0, 1, operand_codes(3)[:, H + C :])
         quantise_da(2)
         make_tanh(3, range(UNITS))
-        round_w13(2)
-        round_w13(3)
+        for e in range(1, E):
+            round_w13(e)
 
         run(3)
         second_product(0)
@@ -385,7 +385,7 @@ def tile_moe_bdx_glu_silu_kernel(tc, dyT, a1, a3, w2, w1, w3, gate, offs, pos1, 
         quantise_da(3)
         second_product(3)
 
-        tokens = work.tile([P, 2, T], F32, name="tokens", tag="g_raw", bufs=E - 1)
+        tokens = work.tile([P, 2, T], F32, name="tokens", tag="front", bufs=1)
         first, both = tokens[:, 0, :], tokens[:, 1, :]
         for a, b in FIRST_PIECES:
             nc.vector.tensor_copy(first[:, a:b], dx_sb[:].indirect(pos1_sb[:, a // 16 : b // 16]))

@@ -9,10 +9,10 @@ P = 128
 PACK = 4
 UNITS = C // P
 HALF = C // 2
-FRONT = (E - 1) * C
+QUAD = 4
 PAIR = 2
-FIRST_PIECES = ((0, 512), (512, 1024))
-SECOND_PIECES = ((0, 512), (512, 896), (896, 1024))
+FIRST_PIECES = ((0, 128), (128, 384), (384, 704), (704, 1024))
+SECOND_PIECES = ((0, 128), (128, 384), (384, 704), (704, 896), (896, 1024))
 
 FLOPS = 2 * S * H * N + 2 * 2 * S * H * K
 BYTES = 4 * (N * T + 2 * H * S + S + E * N * H + 2 * E * H * K + K * T) + 2 * P * (S + 2 * T) // 16
@@ -43,11 +43,10 @@ def tile_moe_bdx_glu_silu_kernel(tc, dyT, a1, a3, w2, w1, w3, gate, offs, pos1, 
         pos1_sb = held.tile([P, T // 16], U16, name="pos1_sb")
         pos2_sb = held.tile([P, T // 16], U16, name="pos2_sb")
         dy_sb = [held.tile([P, T], F32, name="dy%d" % j, tag="dy%d" % j) for j in range(PACK)]
-        gate_sb = held.tile([P, S], F32, name="gate_sb")
+        gate_first = held.tile([P, C], F32, name="gate_first")
+        gate_quads = held.tile([P, E - 1, QUAD], F32, name="gate_quads")
         tanh_sb = held.tile([P, UNITS * H], F32, name="tanh_sb")
         da_grp = [held.tile([P, 2 * C * PACK], BF16, name="da_grp%d" % j, align_bytes=64) for j in range(2)]
-        less_sb = held.tile([P, PACK, HALF], F32, name="less_sb")
-        early_grp = held.tile([P, 2 * C * PACK], BF16, name="early_grp", align_bytes=64)
         dx_sb = held.tile([P, S], F32, name="dx_sb")
         ident = held.tile([P, P], F32, name="ident")
         zero_in = held.tile([P, 1], F32, name="zero_in")
@@ -66,19 +65,19 @@ def tile_moe_bdx_glu_silu_kernel(tc, dyT, a1, a3, w2, w1, w3, gate, offs, pos1, 
         def load_dy(j):
             nc.sync.dma_start(out=dy_sb[j][:], in_=dy_rows[:, j, :])
 
-        def load_gate(a, b):
-            nc.sync.dma_start(out=gate_sb[:, a:b], in_=gate[0:P, a:b])
-
         def load_w2(e):
             raw = work.tile([P, PACK, H], F32, name="w2_raw", tag="w2_raw", bufs=2)
             nc.sync.dma_start(out=raw[:], in_=w2[e].rearrange("(p j) i -> p j i", j=PACK))
             w2_raw[e] = raw
 
-        def load_w13(e):
-            raw = work.tile([P, 2, PACK * K], F32, name="w13_raw", tag="w13_raw", bufs=E)
-            nc.sync.dma_start(out=raw[:, 0, :], in_=w1[e].rearrange("(q r) k -> q (r k)", r=PACK))
-            nc.sync.dma_start(out=raw[:, 1, :], in_=w3[e].rearrange("(q r) k -> q (r k)", r=PACK))
-            w13_raw[e] = raw
+        def load_w13(first, slot):
+            raw = work.tile([P, 2, 2, PACK * K], F32, name="w13_raw", tag=slot, bufs=1, align_bytes=64)
+            for w, weights in enumerate((w1, w3)):
+                nc.sync.dma_start(
+                    out=raw[:, :, w, :], in_=weights[first : first + 2].rearrange("e (q r) k -> q e (r k)", r=PACK)
+                )
+            for j in range(2):
+                w13_raw[first + j] = raw[:, j, :, :]
 
         def a1_rows(a, b):
             return a1[:, a:b].rearrange("(q r) s -> q r s", r=PACK)
@@ -86,7 +85,9 @@ def tile_moe_bdx_glu_silu_kernel(tc, dyT, a1, a3, w2, w1, w3, gate, offs, pos1, 
         def load_a1_half(e, half):
             raw = work.tile([P, PACK, HALF], F32, name="a1_half", tag="a1_half%d" % half, bufs=1, align_bytes=64)
             a = e * C + half * HALF
-            nc.sync.dma_start(out=raw[:], in_=a1_rows(a, a + HALF))
+            step = P if (e, half) == (0, 1) else HALF
+            for c in range(0, HALF, step):
+                nc.sync.dma_start(out=raw[:, :, c : c + step], in_=a1_rows(a + c, a + c + step))
             a1_sb[e, half] = raw[:]
 
         def load_a1(e):
@@ -103,48 +104,64 @@ def tile_moe_bdx_glu_silu_kernel(tc, dyT, a1, a3, w2, w1, w3, gate, offs, pos1, 
             nc.sync.dma_start(out=raw[:], in_=a3[:, e * C : (e + 1) * C].rearrange("(q r) s -> q r s", r=PACK))
             a3_sb[e] = raw
 
-        g_raw, g_grp, w2_grp = {}, {}, {}
+        g_raw, g_grp, w2_grp, gate_ps = {}, {}, {}, {}
         w13_grp = held.tile([P, E, 2 * K * PACK], BF16, name="w13_grp", align_bytes=64)
         g_mx, w2_mx, w13_mx, da_mx = {}, {}, {}, {}
-        front = work.tile([P, PACK, FRONT], F32, name="front", tag="front", bufs=1)
-        for e in range(E - 1):
-            g_raw[e] = front[:, :, e * C : (e + 1) * C]
-        g_raw[E - 1] = early_grp[:].bitcast(F32).rearrange("p (j c) -> p j c", j=PACK)
+        BANKS = 4
 
-        def gather(j, a, b):
-            into = front[:, j, a:b] if b <= FRONT else g_raw[E - 1][:, j, :]
-            nc.vector.tensor_tensor(into, dy_sb[j][:].indirect(offs_sb[:, a // 16 : b // 16]), gate_sb[:, a:b], MULT)
+        def in_turn(slot, name, shape, dtype):
+            return work.tile(shape, dtype, name=name, tag=slot, bufs=1, align_bytes=64)
+
+        pieces = {0: ((0, C, "turn0"),), 1: ((0, C, "turn1"),)}
+        pieces[2] = ((0, HALF, "turn2"), (HALF, C, "turn3"))
+        pieces[3] = ((0, HALF, "turn1"), (HALF, C, "turn4"))
+
+        def gather(e, piece, planes):
+            a, b, slot = pieces[e][piece]
+            if (e, piece) not in g_raw:
+                g_raw[e, piece] = in_turn(slot, "g_raw", [P, PACK, b - a], F32)
+            for j in planes:
+                window = dy_sb[j][:].indirect(offs_sb[:, (e * C + a) // 16 : (e * C + b) // 16])
+                if e == 0:
+                    nc.vector.tensor_tensor(g_raw[e, piece][:, j, :], window, gate_first[:], MULT)
+                else:
+                    nc.scalar.activation(g_raw[e, piece][:, j, :], window, COPY)
+
+        def spread_gate(e):
+            bank = psum.tile([P, QUAD, P], F32, name="gate_ps", tag="dh", bufs=BANKS)
+            for i in range(QUAD):
+                nc.tensor.transpose(bank[:, i, :], gate_quads[:, e - 1, i : i + 1].to_broadcast([P, P]), ident[:])
+            gate_ps[e] = bank
 
         def round_g(e):
-            if e == 0:
-                grp = early_grp[:, H * PACK :]
-            else:
-                grp = work.tile([P, C * PACK], BF16, name="g_grp", tag="g_grp%d" % e, bufs=1, align_bytes=64)
-            nc.scalar.copy(
-                out=grp[:].rearrange("p (c i j) -> p c j i", i=PAIR, j=PACK),
-                in_=g_raw[e].rearrange("p j (c i) -> p c j i", i=PAIR),
-            )
+            grp = work.tile([P, C * PACK], BF16, name="g_grp", tag="g_grp%d" % e, bufs=1, align_bytes=64)
+            for piece, (a, b, slot) in enumerate(pieces[e]):
+                into = grp[:, a * PACK : b * PACK].rearrange("p (n i j) -> p n j i", i=QUAD, j=PACK)
+                values = g_raw[e, piece][:].rearrange("p j (n i) -> p n j i", i=QUAD)
+                if e == 0:
+                    nc.vector.tensor_copy(into, values)
+                else:
+                    gates = gate_ps[e][:, :, a // QUAD : b // QUAD].rearrange("p i n -> p n i").unsqueeze(2)
+                    nc.vector.tensor_tensor(into, values, gates.to_broadcast([P, (b - a) // QUAD, PACK, QUAD]), MULT)
             g_grp[e] = grp
 
         def round_w2(e):
-            grp = work.tile([P, H * PACK], BF16, name="w2_grp", tag="w2_grp", bufs=2, align_bytes=64)
-            nc.scalar.activation(
-                grp[:].rearrange("p (r q j) -> p q j r", r=PACK, j=PACK),
-                w2_raw[e][:].rearrange("p j (q r) -> p q j r", r=PACK),
-                COPY,
-                scale=0.5,
-            )
+            grp = in_turn("turn5" if e == 0 else "turn4", "w2_grp", [P, H * PACK], BF16)
+            into = grp[:].rearrange("p (r q j) -> p q j r", r=PACK, j=PACK)
+            values = w2_raw[e][:].rearrange("p j (q r) -> p q j r", r=PACK)
+            if e == 0:
+                nc.vector.tensor_scalar(into, values, 0.5, None, op0=MULT)
+            else:
+                nc.scalar.activation(into, values, COPY, scale=0.5)
             w2_grp[e] = grp
 
         def round_w13(e):
             nc.scalar.copy(
                 out=w13_grp[:, e, :].rearrange("p (w c i r) -> p w c r i", w=2, i=PAIR, r=PACK),
-                in_=w13_raw[e][:].rearrange("p w (r c i) -> p w c r i", i=PAIR, r=PACK),
+                in_=w13_raw[e].rearrange("p w (r c i) -> p w c r i", i=PAIR, r=PACK),
             )
 
-        def quantise(grp, tag, fmt, width, parts=1, codes=None, bufs=2):
-            if codes is None:
-                codes = work.tile([P, width], U32, name=tag + "_codes", tag=tag + "_codes", bufs=2, align_bytes=64)
+        def quantise(grp, tag, fmt, width, codes, parts=1, bufs=2):
             scales = work.tile([P, width], U8, name=tag + "_scales", tag=tag + "_scales", bufs=bufs, align_bytes=64)
             step = width // parts
             for a in reversed(range(0, width, step)):
@@ -159,71 +176,62 @@ def tile_moe_bdx_glu_silu_kernel(tc, dyT, a1, a3, w2, w1, w3, gate, offs, pos1, 
 
         def operand_codes(e):
             if e not in codes_sb:
-                tag = ("codes0", "a3_sb0", "a1_sb1", "a1_sb2")[e]
-                codes_sb[e] = work.tile([P, H + C + 2 * K], U32, name="codes", tag=tag, bufs=1, align_bytes=64)
+                codes_sb[e] = work.tile([P, H + C], U32, name="codes", tag="turns", bufs=1, align_bytes=64)
             return codes_sb[e]
 
         def quantise_w2(e):
-            w2_mx[e] = quantise(w2_grp[e], "w2", E4M3X4, H, codes=operand_codes(e)[:, :H])
+            w2_mx[e] = quantise(w2_grp[e], "w2", E4M3X4, H, operand_codes(e)[:, :H])
 
         def quantise_g(e):
-            g_mx[e] = quantise(g_grp[e], "g", E5M2X4, C, codes=operand_codes(e)[:, H : H + C])
+            g_mx[e] = quantise(g_grp[e], "g", E5M2X4, C, operand_codes(e)[:, H : H + C])
 
         def quantise_da(e):
-            codes = work.tile([P, 2 * C], U32, name="da_codes", tag="g_grp%d" % (e + 1), bufs=1, align_bytes=64)
-            da_mx[e] = quantise(da_grp[e % 2], "da", E5M2X4, 2 * C, parts=1 if e + 1 < E else 2, codes=codes, bufs=E)
+            codes = work.tile([P, 2 * C], U32, name="da_codes", tag="g_grp%d" % ((e + 1) % E), bufs=1, align_bytes=64)
+            da_mx[e] = quantise(da_grp[e % 2], "da", E5M2X4, 2 * C, codes, parts=1 if e + 1 < E else 2, bufs=E)
 
-        def quantise_w13(first, count, codes):
-            grp = w13_grp[:, first : first + count, :].rearrange("p e c -> p (e c)")
-            codes, scales = quantise(grp, "w13_%d" % first, E4M3X4, count * 2 * K, codes=codes, bufs=1)
-            for j in range(count):
+        def quantise_w13(first, slot):
+            codes = work.tile([P, 4 * K], U32, name="w13_codes", tag=slot, bufs=1, align_bytes=64)
+            grp = w13_grp[:, first : first + 2, :].rearrange("p e c -> p (e c)")
+            codes, scales = quantise(grp, "w13_%d" % first, E4M3X4, 4 * K, codes, bufs=1)
+            for j in range(2):
                 cols = slice(j * 2 * K, (j + 1) * 2 * K)
                 w13_mx[first + j] = codes[:, cols], scales[:, cols]
 
-        def quantise_late_w13():
-            codes = work.tile([P, (E - 1) * 2 * K], U32, name="late_codes", tag="a1_half1", bufs=1, align_bytes=64)
-            quantise_w13(1, 1, codes[:, : 2 * K])
-            quantise_w13(2, 2, codes[:, 2 * K :])
-
-        silu_sb = {}
-
-        BANKS = 4
+        silu_sb, less = {}, {}
 
         def tanh_unit(u):
             return tanh_sb[:, u * H : (u + 1) * H]
 
-        def make_tanh(e, units):
-            for u in units:
+        def make_tanh(e):
+            for u in range(UNITS):
                 bank = psum.tile([P, PACK, P], F32, name="a1_turned", tag="turned", bufs=BANKS)
                 for r in range(PACK):
                     nc.tensor.transpose(bank[:, r, :], a1_unit(e, u)[:, r, :], ident[:])
                 nc.scalar.activation(tanh_unit(u), bank[:].rearrange("p r q -> p (r q)"), TANH, scale=0.5)
 
-        def make_silu(e, half):
-            silu = work.tile([P, PACK, HALF], F32, name="silu_sb", tag="silu_sb%d" % half, bufs=2)
-            nc.scalar.activation(silu[:], a1_sb[e, half], SILU, scale=-1.0, bias=zero_bias[:])
-            if half == 1:
-                nc.scalar.activation(silu[:], silu[:], COPY, scale=-1.0, bias=1.0)
-            elif e == 0:
-                nc.scalar.activation(less_sb[:], silu[:], COPY, scale=-1.0, bias=1.0)
-            silu_sb[e, half] = silu
+        silu_slots = (("turn2", "turn6"), ("turn3", "turn1"), ("turn6", "turn2"), ("turn2", "turn1"))
 
-        def subtract_one(e):
-            nc.gpsimd.tensor_scalar(less_sb[:], silu_sb[e, 0][:], -1.0, 1.0, op0=MULT, op1=ADD)
+        def make_silu(e, half):
+            silu = in_turn(silu_slots[e][half], "silu_sb", [P, PACK, HALF], F32)[:]
+            nc.scalar.activation(silu, a1_sb[e, half], SILU, scale=-1.0, bias=zero_bias[:])
+            silu_sb[e, half] = silu
+            if half == 1 and e in (0, E - 1):
+                less[e, half] = silu
+                nc.scalar.activation(silu, silu, COPY, scale=-1.0, bias=1.0)
+
+        def subtract_from_one(e, half):
+            less[e, half] = in_turn("turn5", "less_sb", [P, PACK, HALF], F32)[:]
+            nc.gpsimd.tensor_scalar(less[e, half], silu_sb[e, half], -1.0, 1.0, op0=MULT, op1=ADD)
 
         w_sb = {}
 
         def make_w(e, half):
-            words = PACK * HALF
-            if e > 0:
-                flat = da_grp[(e + 1) % 2][:].bitcast(F32)[:, half * words : (half + 1) * words]
-            elif half == 0:
-                flat = gate_sb[:, S - words :]
+            if half == 0:
+                flat = da_grp[(e + 1) % 2][:].bitcast(F32)[:, : PACK * HALF]
+                w_sb[e, half] = flat.rearrange("p (r s) -> p r s", r=PACK)
             else:
-                flat = held.tile([P, words], F32, name="w_first", tag="dy%d" % (PACK - 1))[:]
-            w_sb[e, half] = flat.rearrange("p (r s) -> p r s", r=PACK)
-            less = less_sb if half == 0 else silu_sb[e, half]
-            nc.gpsimd.tensor_tensor(w_sb[e, half], less[:], a3_sb[e][:, :, half * HALF : (half + 1) * HALF], MULT)
+                w_sb[e, half] = work.tile([P, PACK, HALF], F32, name="w_late", tag="turns", bufs=1, align_bytes=64)[:]
+            nc.gpsimd.tensor_tensor(w_sb[e, half], less[e, half], a3_sb[e][:, :, half * HALF : (half + 1) * HALF], MULT)
 
         def w_unit(e, u):
             return w_sb[e, u // 2][:, :, unit_slots(u % 2)]
@@ -265,25 +273,35 @@ def tile_moe_bdx_glu_silu_kernel(tc, dyT, a1, a3, w2, w1, w3, gate, offs, pos1, 
             )
 
         def run(e):
+            last = e + 1 == E
             for u in range(UNITS):
                 first_product(e, u)
+            if e == 0:
+                subtract_from_one(e, 0)
             make_w(e, 0)
+            if (e, 1) not in less:
+                subtract_from_one(e, 1)
             make_w(e, 1)
-            if e + 1 < E:
-                subtract_one(e + 1)
+            if not last:
+                make_silu(e + 1, 0)
+                subtract_from_one(e + 1, 0)
             for u in range(UNITS):
                 make_m(e, u)
-            make_da(e, 0, 1, a1_unit(e, 0))
+            for u in range(UNITS if last else UNITS - 1):
+                make_da(e, u, 1, a1_unit(e, u))
+            if not last:
+                spread_gate(e + 1)
+                round_g(e + 1)
             for u in range(UNITS):
-                if u + 1 < UNITS:
-                    make_da(e, u + 1, 1, a1_unit(e, u + 1))
-                if (e, u + 1) == (E - 1, UNITS - 1):
-                    quantise_late_w13()
+                if last and u == 2:
+                    quantise_w13(2, "a1_half1")
                 make_da(e, u, 0, w_unit(e, u))
+            if not last:
+                make_da(e, UNITS - 1, 1, a1_unit(e, UNITS - 1))
 
         def second_product(e):
             w_codes, w_scales = w13_mx[e]
-            bank = psum.tile([P, C], F32, name="dx", tag="turned", bufs=BANKS)
+            bank = psum.tile([P, C], F32, name="dx", tag="dh", bufs=BANKS)
             da_codes, da_scales = da_mx[e]
             for which in (1, 0):
                 cols = slice(which * K, (which + 1) * K)
@@ -301,82 +319,73 @@ def tile_moe_bdx_glu_silu_kernel(tc, dyT, a1, a3, w2, w1, w3, gate, offs, pos1, 
 
         nc.sync.dma_start(offs_sb[:], offs)
         load_dy(0)
-        load_gate(0, HALF)
-        load_gate(HALF, 2 * C)
-        load_a1_half(0, 0)
-        load_gate(2 * C, 3 * C)
+        nc.sync.dma_start(out=gate_first[:], in_=gate[0:P, 0:C])
         load_dy(1)
-        load_a1_half(0, 1)
         load_dy(2)
-        load_w2(0)
         load_dy(3)
-        load_gate(3 * C, S)
+        load_a1_half(0, 0)
+        load_w2(0)
+        load_a1_half(0, 1)
+        load_a3(0)
+        nc.sync.dma_start(out=gate_quads[:], in_=gate[0, C:].rearrange("(e n i) -> n e i", n=P, i=QUAD))
         load_a1(1)
         load_w2(1)
-        load_a3(0)
-        load_a1(2)
-        load_w13(0)
-
-        for j in range(PACK):
-            ends = (0, HALF, 2 * C, FRONT) if j == 0 else (0, FRONT // 2, FRONT)
-            for a, b in zip(ends, ends[1:]):
-                gather(j, a, b)
-        for half in range(2):
-            make_tanh(0, (2 * half, 2 * half + 1))
-            make_silu(0, half)
-        round_w2(0)
-        load_w2(2)
         load_a3(1)
-        round_g(0)
-        gather(0, FRONT, S)
-        gather(1, FRONT, S)
-        quantise_w2(0)
-        quantise_g(0)
-        gather(2, FRONT, S)
-        gather(3, FRONT, S)
-        make_silu(1, 0)
-        make_silu(1, 1)
-        round_w2(1)
-        load_w2(3)
-        round_g(1)
-        make_silu(2, 0)
-        round_w13(0)
-
-        run(0)
-        load_a1_half(3, 0)
-        load_a1_half(3, 1)
+        load_a1(2)
         nc.sync.dma_start(pos1_sb[:], pos1)
         nc.sync.dma_start(pos2_sb[:], pos2)
+
+        for j in range(PACK):
+            gather(0, 0, [j])
+            gather(1, 0, [j])
+        round_g(0)
+        round_w2(0)
+        load_w2(2)
+        quantise_g(0)
+        quantise_w2(0)
+        make_tanh(0)
+        make_silu(0, 0)
+        make_silu(0, 1)
+
+        run(0)
+        round_w2(1)
+        load_w2(3)
+        load_a3(2)
+        load_a1_half(3, 0)
+        load_a1_half(3, 1)
         quantise_w2(1)
         quantise_g(1)
         quantise_da(0)
-        load_a3(2)
-        make_tanh(1, range(UNITS))
-        round_w2(2)
-        round_g(2)
-        make_silu(3, 0)
-        make_silu(2, 1)
+        make_tanh(1)
+        make_silu(1, 1)
+        gather(2, 0, range(PACK))
+        gather(2, 1, range(PACK))
 
         run(1)
         load_a3(3)
-        for e in range(1, E):
-            load_w13(e)
+        load_w13(0, "a1_sb1")
+        round_w2(2)
         quantise_w2(2)
         quantise_g(2)
         quantise_da(1)
-        make_tanh(2, range(UNITS))
-        round_w2(3)
-        round_g(3)
-        make_silu(3, 1)
+        make_tanh(2)
+        make_silu(2, 1)
+        gather(3, 0, range(PACK))
+        gather(3, 1, range(PACK))
 
         run(2)
+        load_w13(2, "a3_sb0")
+        round_w2(3)
+        round_w13(0)
+        round_w13(1)
         quantise_w2(3)
         quantise_g(3)
-        quantise_w13(0, 1, operand_codes(3)[:, H + C :])
+        quantise_w13(0, "a1_sb2")
         quantise_da(2)
-        make_tanh(3, range(UNITS))
-        for e in range(1, E):
-            round_w13(e)
+        make_tanh(3)
+        make_silu(3, 1)
+        round_w13(2)
+        round_w13(3)
 
         run(3)
         second_product(0)
@@ -385,10 +394,10 @@ def tile_moe_bdx_glu_silu_kernel(tc, dyT, a1, a3, w2, w1, w3, gate, offs, pos1, 
         quantise_da(3)
         second_product(3)
 
-        tokens = work.tile([P, 2, T], F32, name="tokens", tag="front", bufs=1)
+        tokens = in_turn("turn0", "tokens", [P, 2, T], F32)
         first, both = tokens[:, 0, :], tokens[:, 1, :]
         for a, b in FIRST_PIECES:
-            nc.vector.tensor_copy(first[:, a:b], dx_sb[:].indirect(pos1_sb[:, a // 16 : b // 16]))
+            nc.scalar.activation(first[:, a:b], dx_sb[:].indirect(pos1_sb[:, a // 16 : b // 16]), COPY)
         for a, b in SECOND_PIECES:
             nc.vector.tensor_tensor(both[:, a:b], dx_sb[:].indirect(pos2_sb[:, a // 16 : b // 16]), first[:, a:b], ADD)
             nc.sync.dma_start(out=out[:, a:b], in_=both[:, a:b])

@@ -85,9 +85,7 @@ def tile_moe_bdx_glu_silu_kernel(tc, dyT, a1, a3, w2, w1, w3, gate, offs, pos1, 
         def load_a1_half(e, half):
             raw = work.tile([P, PACK, HALF], F32, name="a1_half", tag="a1_half%d" % half, bufs=1, align_bytes=64)
             a = e * C + half * HALF
-            step = P if (e, half) == (0, 1) else HALF
-            for c in range(0, HALF, step):
-                nc.sync.dma_start(out=raw[:, :, c : c + step], in_=a1_rows(a + c, a + c + step))
+            nc.sync.dma_start(out=raw[:], in_=a1_rows(a, a + HALF))
             a1_sb[e, half] = raw[:]
 
         def load_a1(e):
@@ -101,7 +99,10 @@ def tile_moe_bdx_glu_silu_kernel(tc, dyT, a1, a3, w2, w1, w3, gate, offs, pos1, 
 
         def load_a3(e):
             raw = work.tile([P, PACK, C], F32, name="a3_sb", tag="a3_sb%d" % (e % 2), bufs=1, align_bytes=64)
-            nc.sync.dma_start(out=raw[:], in_=a3[:, e * C : (e + 1) * C].rearrange("(q r) s -> q r s", r=PACK))
+            step = HALF if e == 0 else C
+            for a in range(0, C, step):
+                rows = a3[:, e * C + a : e * C + a + step].rearrange("(q r) s -> q r s", r=PACK)
+                nc.sync.dma_start(out=raw[:, :, a : a + step], in_=rows)
             a3_sb[e] = raw
 
         g_raw, g_grp, w2_grp, gate_ps = {}, {}, {}, {}
@@ -113,8 +114,8 @@ def tile_moe_bdx_glu_silu_kernel(tc, dyT, a1, a3, w2, w1, w3, gate, offs, pos1, 
             return work.tile(shape, dtype, name=name, tag=slot, bufs=1, align_bytes=64)
 
         pieces = {0: ((0, C, "turn0"),), 1: ((0, C, "turn1"),)}
-        pieces[2] = ((0, HALF, "turn2"), (HALF, C, "turn3"))
-        pieces[3] = ((0, HALF, "turn1"), (HALF, C, "turn4"))
+        pieces[2] = ((0, HALF, "turn0"), (HALF, C, "turn3"))
+        pieces[3] = ((0, C, "turn1"),)
 
         def gather(e, piece, planes):
             a, b, slot = pieces[e][piece]
@@ -128,9 +129,9 @@ def tile_moe_bdx_glu_silu_kernel(tc, dyT, a1, a3, w2, w1, w3, gate, offs, pos1, 
                     nc.scalar.activation(g_raw[e, piece][:, j, :], window, COPY)
 
         def spread_gate(e):
-            bank = psum.tile([P, QUAD, P], F32, name="gate_ps", tag="dh", bufs=BANKS)
+            bank = psum.tile([P, P, QUAD], F32, name="gate_ps", tag="dh" if e > 1 else "turned", bufs=BANKS)
             for i in range(QUAD):
-                nc.tensor.transpose(bank[:, i, :], gate_quads[:, e - 1, i : i + 1].to_broadcast([P, P]), ident[:])
+                nc.tensor.transpose(bank[:, :, i], gate_quads[:, e - 1, i : i + 1].to_broadcast([P, P]), ident[:])
             gate_ps[e] = bank
 
         def round_g(e):
@@ -141,12 +142,12 @@ def tile_moe_bdx_glu_silu_kernel(tc, dyT, a1, a3, w2, w1, w3, gate, offs, pos1, 
                 if e == 0:
                     nc.vector.tensor_copy(into, values)
                 else:
-                    gates = gate_ps[e][:, :, a // QUAD : b // QUAD].rearrange("p i n -> p n i").unsqueeze(2)
+                    gates = gate_ps[e][:, a // QUAD : b // QUAD, :].unsqueeze(2)
                     nc.vector.tensor_tensor(into, values, gates.to_broadcast([P, (b - a) // QUAD, PACK, QUAD]), MULT)
             g_grp[e] = grp
 
         def round_w2(e):
-            grp = in_turn("turn5" if e == 0 else "turn4", "w2_grp", [P, H * PACK], BF16)
+            grp = in_turn("g_grp1" if e == 0 else "turn4", "w2_grp", [P, H * PACK], BF16)
             into = grp[:].rearrange("p (r q j) -> p q j r", r=PACK, j=PACK)
             values = w2_raw[e][:].rearrange("p j (q r) -> p q j r", r=PACK)
             if e == 0:
@@ -202,9 +203,9 @@ def tile_moe_bdx_glu_silu_kernel(tc, dyT, a1, a3, w2, w1, w3, gate, offs, pos1, 
         def tanh_unit(u):
             return tanh_sb[:, u * H : (u + 1) * H]
 
-        def make_tanh(e):
-            for u in range(UNITS):
-                bank = psum.tile([P, PACK, P], F32, name="a1_turned", tag="turned", bufs=BANKS)
+        def make_tanh(e, units=range(UNITS)):
+            for u in units:
+                bank = psum.tile([P, PACK, P], F32, name="a1_turned", tag="dh" if e > 0 else "turned", bufs=BANKS)
                 for r in range(PACK):
                     nc.tensor.transpose(bank[:, r, :], a1_unit(e, u)[:, r, :], ident[:])
                 nc.scalar.activation(tanh_unit(u), bank[:].rearrange("p r q -> p (r q)"), TANH, scale=0.5)
@@ -215,7 +216,7 @@ def tile_moe_bdx_glu_silu_kernel(tc, dyT, a1, a3, w2, w1, w3, gate, offs, pos1, 
             silu = in_turn(silu_slots[e][half], "silu_sb", [P, PACK, HALF], F32)[:]
             nc.scalar.activation(silu, a1_sb[e, half], SILU, scale=-1.0, bias=zero_bias[:])
             silu_sb[e, half] = silu
-            if half == 1 and e in (0, E - 1):
+            if (e, half) in ((0, 0), (E - 1, 1)):
                 less[e, half] = silu
                 nc.scalar.activation(silu, silu, COPY, scale=-1.0, bias=1.0)
 
@@ -276,8 +277,6 @@ def tile_moe_bdx_glu_silu_kernel(tc, dyT, a1, a3, w2, w1, w3, gate, offs, pos1, 
             last = e + 1 == E
             for u in range(UNITS):
                 first_product(e, u)
-            if e == 0:
-                subtract_from_one(e, 0)
             make_w(e, 0)
             if (e, 1) not in less:
                 subtract_from_one(e, 1)
@@ -287,14 +286,18 @@ def tile_moe_bdx_glu_silu_kernel(tc, dyT, a1, a3, w2, w1, w3, gate, offs, pos1, 
                 subtract_from_one(e + 1, 0)
             for u in range(UNITS):
                 make_m(e, u)
+            if not last:
+                if e > 0:
+                    spread_gate(e + 1)
+                round_w2(e + 1)
+                make_tanh(e + 1)
             for u in range(UNITS if last else UNITS - 1):
                 make_da(e, u, 1, a1_unit(e, u))
-            if not last:
-                spread_gate(e + 1)
-                round_g(e + 1)
             for u in range(UNITS):
-                if last and u == 2:
+                if u == 2 and last:
                     quantise_w13(2, "a1_half1")
+                elif u == 2 and e > 0:
+                    round_g(e + 1)
                 make_da(e, u, 0, w_unit(e, u))
             if not last:
                 make_da(e, UNITS - 1, 1, a1_unit(e, UNITS - 1))
@@ -325,11 +328,11 @@ def tile_moe_bdx_glu_silu_kernel(tc, dyT, a1, a3, w2, w1, w3, gate, offs, pos1, 
         load_dy(3)
         load_a1_half(0, 0)
         load_w2(0)
+        nc.sync.dma_start(out=gate_quads[:], in_=gate[0, C:].rearrange("(e n i) -> n e i", n=P, i=QUAD))
         load_a1_half(0, 1)
         load_a3(0)
-        nc.sync.dma_start(out=gate_quads[:], in_=gate[0, C:].rearrange("(e n i) -> n e i", n=P, i=QUAD))
-        load_a1(1)
         load_w2(1)
+        load_a1(1)
         load_a3(1)
         load_a1(2)
         nc.sync.dma_start(pos1_sb[:], pos1)
@@ -343,12 +346,14 @@ def tile_moe_bdx_glu_silu_kernel(tc, dyT, a1, a3, w2, w1, w3, gate, offs, pos1, 
         load_w2(2)
         quantise_g(0)
         quantise_w2(0)
-        make_tanh(0)
         make_silu(0, 0)
+        make_tanh(0, (0, 1))
+        spread_gate(1)
+        make_tanh(0, (2, 3))
         make_silu(0, 1)
+        round_g(1)
 
         run(0)
-        round_w2(1)
         load_w2(3)
         load_a3(2)
         load_a1_half(3, 0)
@@ -356,7 +361,6 @@ def tile_moe_bdx_glu_silu_kernel(tc, dyT, a1, a3, w2, w1, w3, gate, offs, pos1, 
         quantise_w2(1)
         quantise_g(1)
         quantise_da(0)
-        make_tanh(1)
         make_silu(1, 1)
         gather(2, 0, range(PACK))
         gather(2, 1, range(PACK))
@@ -364,25 +368,20 @@ def tile_moe_bdx_glu_silu_kernel(tc, dyT, a1, a3, w2, w1, w3, gate, offs, pos1, 
         run(1)
         load_a3(3)
         load_w13(0, "a1_sb1")
-        round_w2(2)
         quantise_w2(2)
         quantise_g(2)
         quantise_da(1)
-        make_tanh(2)
         make_silu(2, 1)
         gather(3, 0, range(PACK))
-        gather(3, 1, range(PACK))
 
         run(2)
         load_w13(2, "a3_sb0")
-        round_w2(3)
         round_w13(0)
         round_w13(1)
         quantise_w2(3)
         quantise_g(3)
         quantise_w13(0, "a1_sb2")
         quantise_da(2)
-        make_tanh(3)
         make_silu(3, 1)
         round_w13(2)
         round_w13(3)
@@ -397,7 +396,11 @@ def tile_moe_bdx_glu_silu_kernel(tc, dyT, a1, a3, w2, w1, w3, gate, offs, pos1, 
         tokens = in_turn("turn0", "tokens", [P, 2, T], F32)
         first, both = tokens[:, 0, :], tokens[:, 1, :]
         for a, b in FIRST_PIECES:
-            nc.scalar.activation(first[:, a:b], dx_sb[:].indirect(pos1_sb[:, a // 16 : b // 16]), COPY)
+            window = dx_sb[:].indirect(pos1_sb[:, a // 16 : b // 16])
+            if a == 0:
+                nc.vector.tensor_copy(first[:, a:b], window)
+            else:
+                nc.scalar.activation(first[:, a:b], window, COPY)
         for a, b in SECOND_PIECES:
             nc.vector.tensor_tensor(both[:, a:b], dx_sb[:].indirect(pos2_sb[:, a // 16 : b // 16]), first[:, a:b], ADD)
             nc.sync.dma_start(out=out[:, a:b], in_=both[:, a:b])

@@ -11,8 +11,8 @@ UNITS = C // P
 HALF = C // 2
 QUAD = 4
 PAIR = 2
-FIRST_PIECES = ((0, 128), (128, 384), (384, 704), (704, 1024))
-SECOND_PIECES = ((0, 128), (128, 384), (384, 704), (704, 896), (896, 1024))
+PIECE_ENDS = (160, 448, 672, 864, 1024)
+STORE_ENDS = (448, 672, 864, 1024)
 
 FLOPS = 2 * S * H * N + 2 * 2 * S * H * K
 BYTES = 4 * (N * T + 2 * H * S + S + E * N * H + 2 * E * H * K + K * T) + 2 * P * (S + 2 * T) // 16
@@ -66,17 +66,17 @@ def tile_moe_bdx_glu_silu_kernel(tc, dyT, a1, a3, w2, w1, w3, gate, offs, pos1, 
             nc.sync.dma_start(out=dy_sb[j][:], in_=dy_rows[:, j, :])
 
         def load_w2(e):
-            raw = work.tile([P, PACK, H], F32, name="w2_raw", tag="w2_raw", bufs=2)
+            raw = work.tile([P, PACK, H], F32, name="w2_raw", tag="w2_raw%d" % (0, 1, 2, 1)[e], bufs=1, align_bytes=64)
             nc.sync.dma_start(out=raw[:], in_=w2[e].rearrange("(p j) i -> p j i", j=PACK))
             w2_raw[e] = raw
 
-        def load_w13(first, slot):
-            raw = work.tile([P, 2, 2, PACK * K], F32, name="w13_raw", tag=slot, bufs=1, align_bytes=64)
+        def load_w13(first, count, slot):
+            raw = work.tile([P, count, 2, PACK * K], F32, name="w13_raw", tag=slot, bufs=1, align_bytes=64)
             for w, weights in enumerate((w1, w3)):
                 nc.sync.dma_start(
-                    out=raw[:, :, w, :], in_=weights[first : first + 2].rearrange("e (q r) k -> q e (r k)", r=PACK)
+                    out=raw[:, :, w, :], in_=weights[first : first + count].rearrange("e (q r) k -> q e (r k)", r=PACK)
                 )
-            for j in range(2):
+            for j in range(count):
                 w13_raw[first + j] = raw[:, j, :, :]
 
         def a1_rows(a, b):
@@ -106,15 +106,23 @@ def tile_moe_bdx_glu_silu_kernel(tc, dyT, a1, a3, w2, w1, w3, gate, offs, pos1, 
             a3_sb[e] = raw
 
         g_raw, g_grp, w2_grp, gate_ps = {}, {}, {}, {}
-        w13_grp = held.tile([P, E, 2 * K * PACK], BF16, name="w13_grp", align_bytes=64)
+        w13_grp = {}
         g_mx, w2_mx, w13_mx, da_mx = {}, {}, {}, {}
-        BANKS = 4
+        RING = 4
+        handed = {"dh": [], "turned": []}
+
+        def bank_tile(name, shape, tag):
+            return psum.tile(shape, F32, name=name, tag=tag, bufs=1)
+
+        def next_bank(ring, name, shape):
+            handed[ring].append("%s%d" % (ring, len(handed[ring]) % RING))
+            return bank_tile(name, shape, handed[ring][-1])
 
         def in_turn(slot, name, shape, dtype):
             return work.tile(shape, dtype, name=name, tag=slot, bufs=1, align_bytes=64)
 
         pieces = {0: ((0, C, "turn0"),), 1: ((0, C, "turn1"),)}
-        pieces[2] = ((0, HALF, "turn0"), (HALF, C, "turn3"))
+        pieces[2] = ((0, P, "w2_raw0"), (P, C, "turn3"))
         pieces[3] = ((0, C, "turn1"),)
 
         def gather(e, piece, planes):
@@ -129,48 +137,57 @@ def tile_moe_bdx_glu_silu_kernel(tc, dyT, a1, a3, w2, w1, w3, gate, offs, pos1, 
                     nc.scalar.activation(g_raw[e, piece][:, j, :], window, COPY)
 
         def spread_gate(e):
-            bank = psum.tile([P, P, QUAD], F32, name="gate_ps", tag="dh" if e > 1 else "turned", bufs=BANKS)
+            bank = next_bank("dh", "gate_ps", [P, P, QUAD])
             for i in range(QUAD):
                 nc.tensor.transpose(bank[:, :, i], gate_quads[:, e - 1, i : i + 1].to_broadcast([P, P]), ident[:])
             gate_ps[e] = bank
 
-        def round_g(e):
-            grp = work.tile([P, C * PACK], BF16, name="g_grp", tag="g_grp%d" % e, bufs=1, align_bytes=64)
-            for piece, (a, b, slot) in enumerate(pieces[e]):
-                into = grp[:, a * PACK : b * PACK].rearrange("p (n i j) -> p n j i", i=QUAD, j=PACK)
-                values = g_raw[e, piece][:].rearrange("p j (n i) -> p n j i", i=QUAD)
-                if e == 0:
-                    nc.vector.tensor_copy(into, values)
-                else:
-                    gates = gate_ps[e][:, a // QUAD : b // QUAD, :].unsqueeze(2)
-                    nc.vector.tensor_tensor(into, values, gates.to_broadcast([P, (b - a) // QUAD, PACK, QUAD]), MULT)
-            g_grp[e] = grp
+        shared_grp = in_turn("g_grp1", "shared_grp", [P, (C + HALF) * PACK], BF16)
+
+        def round_g(e, a, b):
+            if e not in g_grp:
+                g_grp[e] = shared_grp[:, : C * PACK] if e == 1 else in_turn("g_grp%d" % e, "g_grp", [P, C * PACK], BF16)
+            piece = max(k for k in range(len(pieces[e])) if pieces[e][k][0] <= a)
+            first = pieces[e][piece][0]
+            into = g_grp[e][:, a * PACK : b * PACK].rearrange("p (n i j) -> p n j i", i=QUAD, j=PACK)
+            values = g_raw[e, piece][:, :, a - first : b - first].rearrange("p j (n i) -> p n j i", i=QUAD)
+            if e == 0:
+                nc.vector.tensor_copy(into, values)
+            else:
+                gates = gate_ps[e][:, a // QUAD : b // QUAD, :].unsqueeze(2)
+                nc.vector.tensor_tensor(into, values, gates.to_broadcast([P, (b - a) // QUAD, PACK, QUAD]), MULT)
 
         def round_w2(e):
-            grp = in_turn("g_grp1" if e == 0 else "turn4", "w2_grp", [P, H * PACK], BF16)
+            grp = shared_grp[:, HALF * PACK :] if e == 0 else in_turn("turn4", "w2_grp", [P, H * PACK], BF16)
             into = grp[:].rearrange("p (r q j) -> p q j r", r=PACK, j=PACK)
             values = w2_raw[e][:].rearrange("p j (q r) -> p q j r", r=PACK)
             if e == 0:
-                nc.vector.tensor_scalar(into, values, 0.5, None, op0=MULT)
+                nc.vector.tensor_scalar(into[:, :, :, :PAIR], values[:, :, :, :PAIR], 0.5, None, op0=MULT)
+                nc.scalar.activation(into[:, :, :, PAIR:], values[:, :, :, PAIR:], COPY, scale=0.5)
             else:
                 nc.scalar.activation(into, values, COPY, scale=0.5)
             w2_grp[e] = grp
 
         def round_w13(e):
-            nc.scalar.copy(
-                out=w13_grp[:, e, :].rearrange("p (w c i r) -> p w c r i", w=2, i=PAIR, r=PACK),
-                in_=w13_raw[e].rearrange("p w (r c i) -> p w c r i", i=PAIR, r=PACK),
-            )
-
-        def quantise(grp, tag, fmt, width, codes, parts=1, bufs=2):
-            scales = work.tile([P, width], U8, name=tag + "_scales", tag=tag + "_scales", bufs=bufs, align_bytes=64)
-            step = width // parts
-            for a in reversed(range(0, width, step)):
-                nc.vector.quantize_mx(
-                    out=codes[:, a : a + step].bitcast(fmt),
-                    scales=scales[:, a : a + step],
-                    in_=grp[:, a * PACK : (a + step) * PACK],
+            w13_grp[e] = in_turn(("turn6", "w13_grp1", "w13_grp2", "w13_grp3")[e], "w13_grp", [P, 2 * K * PACK], BF16)
+            if e == 0:
+                nc.gpsimd.tensor_scalar(
+                    w13_grp[e][:].rearrange("p (w c r) -> p w c r", w=2, r=PACK),
+                    w13_raw[e].rearrange("p w (r c) -> p w c r", r=PACK),
+                    1.0,
+                    0.0,
+                    op0=MULT,
+                    op1=ADD,
                 )
+            else:
+                nc.scalar.copy(
+                    out=w13_grp[e][:].rearrange("p (w c i r) -> p w c r i", w=2, i=PAIR, r=PACK),
+                    in_=w13_raw[e].rearrange("p w (r c i) -> p w c r i", i=PAIR, r=PACK),
+                )
+
+        def quantise(grp, tag, fmt, width, codes, bufs=2):
+            scales = work.tile([P, width], U8, name=tag + "_scales", tag=tag + "_scales", bufs=bufs, align_bytes=64)
+            nc.vector.quantize_mx(out=codes.bitcast(fmt), scales=scales[:], in_=grp[:])
             return codes, scales
 
         codes_sb = {}
@@ -186,17 +203,21 @@ def tile_moe_bdx_glu_silu_kernel(tc, dyT, a1, a3, w2, w1, w3, gate, offs, pos1, 
         def quantise_g(e):
             g_mx[e] = quantise(g_grp[e], "g", E5M2X4, C, operand_codes(e)[:, H : H + C])
 
-        def quantise_da(e):
-            codes = work.tile([P, 2 * C], U32, name="da_codes", tag="g_grp%d" % ((e + 1) % E), bufs=1, align_bytes=64)
-            da_mx[e] = quantise(da_grp[e % 2], "da", E5M2X4, 2 * C, codes, parts=1 if e + 1 < E else 2, bufs=E)
+        def quantise_da(e, columns):
+            if e not in da_mx:
+                codes = in_turn("g_grp%d" % ((e + 1) % E), "da_codes", [P, 2 * C], U32)
+                da_mx[e] = codes, work.tile([P, 2 * C], U8, name="da_scales", tag="da_scales", bufs=E, align_bytes=64)
+            codes, scales = da_mx[e]
+            a, b = columns
+            nc.vector.quantize_mx(
+                out=codes[:, a:b].bitcast(E5M2X4), scales=scales[:, a:b], in_=da_grp[e % 2][:, a * PACK : b * PACK]
+            )
 
         def quantise_w13(first, slot):
             codes = work.tile([P, 4 * K], U32, name="w13_codes", tag=slot, bufs=1, align_bytes=64)
-            grp = w13_grp[:, first : first + 2, :].rearrange("p e c -> p (e c)")
-            codes, scales = quantise(grp, "w13_%d" % first, E4M3X4, 4 * K, codes, bufs=1)
             for j in range(2):
                 cols = slice(j * 2 * K, (j + 1) * 2 * K)
-                w13_mx[first + j] = codes[:, cols], scales[:, cols]
+                w13_mx[first + j] = quantise(w13_grp[first + j], "w13", E4M3X4, 2 * K, codes[:, cols], bufs=E)
 
         silu_sb, less = {}, {}
 
@@ -205,7 +226,7 @@ def tile_moe_bdx_glu_silu_kernel(tc, dyT, a1, a3, w2, w1, w3, gate, offs, pos1, 
 
         def make_tanh(e, units=range(UNITS)):
             for u in units:
-                bank = psum.tile([P, PACK, P], F32, name="a1_turned", tag="dh" if e > 0 else "turned", bufs=BANKS)
+                bank = next_bank("dh" if e > 0 else "turned", "a1_turned", [P, PACK, P])
                 for r in range(PACK):
                     nc.tensor.transpose(bank[:, r, :], a1_unit(e, u)[:, r, :], ident[:])
                 nc.scalar.activation(tanh_unit(u), bank[:].rearrange("p r q -> p (r q)"), TANH, scale=0.5)
@@ -216,7 +237,7 @@ def tile_moe_bdx_glu_silu_kernel(tc, dyT, a1, a3, w2, w1, w3, gate, offs, pos1, 
             silu = in_turn(silu_slots[e][half], "silu_sb", [P, PACK, HALF], F32)[:]
             nc.scalar.activation(silu, a1_sb[e, half], SILU, scale=-1.0, bias=zero_bias[:])
             silu_sb[e, half] = silu
-            if (e, half) in ((0, 0), (E - 1, 1)):
+            if (e, half) == (E - 1, 1):
                 less[e, half] = silu
                 nc.scalar.activation(silu, silu, COPY, scale=-1.0, bias=1.0)
 
@@ -231,7 +252,7 @@ def tile_moe_bdx_glu_silu_kernel(tc, dyT, a1, a3, w2, w1, w3, gate, offs, pos1, 
                 flat = da_grp[(e + 1) % 2][:].bitcast(F32)[:, : PACK * HALF]
                 w_sb[e, half] = flat.rearrange("p (r s) -> p r s", r=PACK)
             else:
-                w_sb[e, half] = work.tile([P, PACK, HALF], F32, name="w_late", tag="turns", bufs=1, align_bytes=64)[:]
+                w_sb[e, half] = in_turn("turns" if e + 1 < E else "turn5", "w_late", [P, PACK, HALF], F32)[:]
             nc.gpsimd.tensor_tensor(w_sb[e, half], less[e, half], a3_sb[e][:, :, half * HALF : (half + 1) * HALF], MULT)
 
         def w_unit(e, u):
@@ -242,7 +263,7 @@ def tile_moe_bdx_glu_silu_kernel(tc, dyT, a1, a3, w2, w1, w3, gate, offs, pos1, 
         def first_product(e, u):
             g_codes, g_scales = g_mx[e]
             w_codes, w_scales = w2_mx[e]
-            bank = psum.tile([P, H], F32, name="dh", tag="dh", bufs=BANKS)
+            bank = next_bank("dh", "dh", [P, H])
             nc.tensor.matmul_mx(
                 out=bank[:],
                 lhsT=g_codes[:, unit_slots(u)].bitcast(E5M2X4),
@@ -259,7 +280,7 @@ def tile_moe_bdx_glu_silu_kernel(tc, dyT, a1, a3, w2, w1, w3, gate, offs, pos1, 
             nc.vector.scalar_tensor_tensor(
                 out=m[:], in0=tanh_unit(u), scalar=1.0, in1=dh_ps[e, u][:], op0=ADD, op1=MULT
             )
-            bank = psum.tile([P, PACK, P], F32, name="m_turned", tag="turned", bufs=BANKS)
+            bank = next_bank("turned", "m_turned", [P, PACK, P])
             for r in range(PACK):
                 nc.tensor.transpose(bank[:, r, :], m[:, r * P : (r + 1) * P], ident[:])
             m_ps[e, u] = bank
@@ -284,6 +305,8 @@ def tile_moe_bdx_glu_silu_kernel(tc, dyT, a1, a3, w2, w1, w3, gate, offs, pos1, 
             if not last:
                 make_silu(e + 1, 0)
                 subtract_from_one(e + 1, 0)
+                if e == 1:
+                    round_w13(0)
             for u in range(UNITS):
                 make_m(e, u)
             if not last:
@@ -296,19 +319,22 @@ def tile_moe_bdx_glu_silu_kernel(tc, dyT, a1, a3, w2, w1, w3, gate, offs, pos1, 
             for u in range(UNITS):
                 if u == 2 and last:
                     quantise_w13(2, "a1_half1")
+                    quantise_da(e, (C, C + HALF))
+                    quantise_da(e, (0, HALF))
                 elif u == 2 and e > 0:
-                    round_g(e + 1)
+                    for a, b, slot in pieces[e + 1]:
+                        round_g(e + 1, a, b)
                 make_da(e, u, 0, w_unit(e, u))
             if not last:
                 make_da(e, UNITS - 1, 1, a1_unit(e, UNITS - 1))
 
-        def second_product(e):
+        def second_product(e, a, b, tag, copy):
             w_codes, w_scales = w13_mx[e]
-            bank = psum.tile([P, C], F32, name="dx", tag="dh", bufs=BANKS)
+            bank = bank_tile("dx", [P, b - a], tag)
             da_codes, da_scales = da_mx[e]
             for which in (1, 0):
                 cols = slice(which * K, (which + 1) * K)
-                slots = slice(which * C, (which + 1) * C)
+                slots = slice(which * C + a, which * C + b)
                 nc.tensor.matmul_mx(
                     out=bank[:],
                     lhsT=w_codes[:, cols].bitcast(E4M3X4),
@@ -318,7 +344,7 @@ def tile_moe_bdx_glu_silu_kernel(tc, dyT, a1, a3, w2, w1, w3, gate, offs, pos1, 
                     start=which == 1,
                     stop=which == 0,
                 )
-            nc.scalar.copy(out=dx_sb[:, e * C : (e + 1) * C], in_=bank[:])
+            copy(dx_sb[:, e * C + a : e * C + b], bank[:])
 
         nc.sync.dma_start(offs_sb[:], offs)
         load_dy(0)
@@ -326,9 +352,9 @@ def tile_moe_bdx_glu_silu_kernel(tc, dyT, a1, a3, w2, w1, w3, gate, offs, pos1, 
         load_dy(1)
         load_dy(2)
         load_dy(3)
+        nc.sync.dma_start(out=gate_quads[:], in_=gate[0, C:].rearrange("(e n i) -> n e i", n=P, i=QUAD))
         load_a1_half(0, 0)
         load_w2(0)
-        nc.sync.dma_start(out=gate_quads[:], in_=gate[0, C:].rearrange("(e n i) -> n e i", n=P, i=QUAD))
         load_a1_half(0, 1)
         load_a3(0)
         load_w2(1)
@@ -341,66 +367,74 @@ def tile_moe_bdx_glu_silu_kernel(tc, dyT, a1, a3, w2, w1, w3, gate, offs, pos1, 
         for j in range(PACK):
             gather(0, 0, [j])
             gather(1, 0, [j])
-        round_g(0)
+        spread_gate(1)
+        make_silu(0, 0)
+        subtract_from_one(0, 0)
+        make_tanh(0, (0, 1))
+        round_g(0, 0, C)
+        round_g(1, 0, HALF)
+        quantise_g(0)
         round_w2(0)
         load_w2(2)
-        quantise_g(0)
         quantise_w2(0)
-        make_silu(0, 0)
-        make_tanh(0, (0, 1))
-        spread_gate(1)
+        round_g(1, HALF, C)
         make_tanh(0, (2, 3))
         make_silu(0, 1)
-        round_g(1)
 
         run(0)
         load_w2(3)
         load_a3(2)
+        load_w13(0, 1, "w13_early")
         load_a1_half(3, 0)
         load_a1_half(3, 1)
         quantise_w2(1)
         quantise_g(1)
-        quantise_da(0)
+        quantise_da(0, (0, 2 * C))
         make_silu(1, 1)
         gather(2, 0, range(PACK))
         gather(2, 1, range(PACK))
 
         run(1)
         load_a3(3)
-        load_w13(0, "a1_sb1")
+        load_w13(1, 1, "a1_sb1")
         quantise_w2(2)
         quantise_g(2)
-        quantise_da(1)
+        quantise_da(1, (0, 2 * C))
         make_silu(2, 1)
         gather(3, 0, range(PACK))
 
         run(2)
-        load_w13(2, "a3_sb0")
-        round_w13(0)
+        load_w13(2, 2, "a3_sb0")
         round_w13(1)
         quantise_w2(3)
         quantise_g(3)
         quantise_w13(0, "a1_sb2")
-        quantise_da(2)
+        quantise_da(2, (0, 2 * C))
         make_silu(3, 1)
         round_w13(2)
         round_w13(3)
 
         run(3)
-        second_product(0)
-        second_product(1)
-        second_product(2)
-        quantise_da(3)
-        second_product(3)
+        quantise_da(3, (C + HALF, 2 * C))
+        quantise_da(3, (HALF, C))
+        dh_banks, turned_banks = handed["dh"][-RING:], handed["turned"][-RING:]
+        second_product(0, 0, C, dh_banks[3], nc.scalar.copy)
+        second_product(1, 0, C, turned_banks[0], nc.scalar.copy)
+        second_product(2, 0, C, dh_banks[0], nc.scalar.copy)
+        second_product(3, 0, HALF, dh_banks[1], nc.scalar.copy)
+        second_product(3, HALF, C, dh_banks[2], nc.vector.tensor_copy)
 
         tokens = in_turn("turn0", "tokens", [P, 2, T], F32)
         first, both = tokens[:, 0, :], tokens[:, 1, :]
-        for a, b in FIRST_PIECES:
+        token_pieces = list(zip((0,) + PIECE_ENDS, PIECE_ENDS))
+        stored = 0
+        for a, b in token_pieces:
             window = dx_sb[:].indirect(pos1_sb[:, a // 16 : b // 16])
             if a == 0:
                 nc.vector.tensor_copy(first[:, a:b], window)
             else:
                 nc.scalar.activation(first[:, a:b], window, COPY)
-        for a, b in SECOND_PIECES:
             nc.vector.tensor_tensor(both[:, a:b], dx_sb[:].indirect(pos2_sb[:, a // 16 : b // 16]), first[:, a:b], ADD)
-            nc.sync.dma_start(out=out[:, a:b], in_=both[:, a:b])
+            if b in STORE_ENDS:
+                nc.sync.dma_start(out=out[:, stored:b], in_=both[:, stored:b])
+                stored = b

@@ -108,15 +108,8 @@ def tile_moe_bdx_glu_silu_kernel(tc, dyT, a1, a3, w2, w1, w3, gate, offs, pos1, 
         g_raw, g_grp, w2_grp, gate_ps = {}, {}, {}, {}
         w13_grp = {}
         g_mx, w2_mx, w13_mx, da_mx = {}, {}, {}, {}
-        RING = 4
-        handed = {"dh": [], "turned": []}
-
         def bank_tile(name, shape, tag):
             return psum.tile(shape, F32, name=name, tag=tag, bufs=1)
-
-        def next_bank(ring, name, shape):
-            handed[ring].append("%s%d" % (ring, len(handed[ring]) % RING))
-            return bank_tile(name, shape, handed[ring][-1])
 
         def in_turn(slot, name, shape, dtype):
             return work.tile(shape, dtype, name=name, tag=slot, bufs=1, align_bytes=64)
@@ -137,7 +130,7 @@ def tile_moe_bdx_glu_silu_kernel(tc, dyT, a1, a3, w2, w1, w3, gate, offs, pos1, 
                     nc.scalar.activation(g_raw[e, piece][:, j, :], window, COPY)
 
         def spread_gate(e):
-            bank = next_bank("dh", "gate_ps", [P, P, QUAD])
+            bank = bank_tile("gate_ps", [P, P, QUAD], "dh2" if e > 1 else "dh3")
             for i in range(QUAD):
                 nc.tensor.transpose(bank[:, :, i], gate_quads[:, e - 1, i : i + 1].to_broadcast([P, P]), ident[:])
             gate_ps[e] = bank
@@ -226,7 +219,7 @@ def tile_moe_bdx_glu_silu_kernel(tc, dyT, a1, a3, w2, w1, w3, gate, offs, pos1, 
 
         def make_tanh(e, units=range(UNITS)):
             for u in units:
-                bank = next_bank("dh" if e > 0 else "turned", "a1_turned", [P, PACK, P])
+                bank = bank_tile("a1_turned", [P, PACK, P], ("dh3", "turned0", "turned1", "dh3")[u] if e > 0 else "turned%d" % u)
                 for r in range(PACK):
                     nc.tensor.transpose(bank[:, r, :], a1_unit(e, u)[:, r, :], ident[:])
                 nc.scalar.activation(tanh_unit(u), bank[:].rearrange("p r q -> p (r q)"), TANH, scale=0.5)
@@ -263,7 +256,7 @@ def tile_moe_bdx_glu_silu_kernel(tc, dyT, a1, a3, w2, w1, w3, gate, offs, pos1, 
         def first_product(e, u):
             g_codes, g_scales = g_mx[e]
             w_codes, w_scales = w2_mx[e]
-            bank = next_bank("dh", "dh", [P, H])
+            bank = bank_tile("dh", [P, H], "dh%d" % u)
             nc.tensor.matmul_mx(
                 out=bank[:],
                 lhsT=g_codes[:, unit_slots(u)].bitcast(E5M2X4),
@@ -280,7 +273,7 @@ def tile_moe_bdx_glu_silu_kernel(tc, dyT, a1, a3, w2, w1, w3, gate, offs, pos1, 
             nc.vector.scalar_tensor_tensor(
                 out=m[:], in0=tanh_unit(u), scalar=1.0, in1=dh_ps[e, u][:], op0=ADD, op1=MULT
             )
-            bank = next_bank("turned", "m_turned", [P, PACK, P])
+            bank = bank_tile("m_turned", [P, PACK, P], "turned%d" % u)
             for r in range(PACK):
                 nc.tensor.transpose(bank[:, r, :], m[:, r * P : (r + 1) * P], ident[:])
             m_ps[e, u] = bank
@@ -313,20 +306,24 @@ def tile_moe_bdx_glu_silu_kernel(tc, dyT, a1, a3, w2, w1, w3, gate, offs, pos1, 
                 if e > 0:
                     spread_gate(e + 1)
                 round_w2(e + 1)
-                make_tanh(e + 1)
-            for u in range(UNITS if last else UNITS - 1):
+            for u in range(2):
                 make_da(e, u, 1, a1_unit(e, u))
-            for u in range(UNITS):
-                if u == 2 and last:
-                    quantise_w13(2, "a1_half1")
-                    quantise_da(e, (C, C + HALF))
-                    quantise_da(e, (0, HALF))
-                elif u == 2 and e > 0:
-                    for a, b, slot in pieces[e + 1]:
-                        round_g(e + 1, a, b)
                 make_da(e, u, 0, w_unit(e, u))
             if not last:
-                make_da(e, UNITS - 1, 1, a1_unit(e, UNITS - 1))
+                make_tanh(e + 1)
+            make_da(e, 2, 1, a1_unit(e, 2))
+            if last:
+                make_da(e, 3, 1, a1_unit(e, 3))
+                quantise_w13(2, "a1_half1")
+                quantise_da(e, (C, 2 * C))
+                quantise_da(e, (0, HALF))
+            elif e > 0:
+                for a, b, slot in pieces[e + 1]:
+                    round_g(e + 1, a, b)
+            make_da(e, 2, 0, w_unit(e, 2))
+            make_da(e, 3, 0, w_unit(e, 3))
+            if not last:
+                make_da(e, 3, 1, a1_unit(e, 3))
 
         def second_product(e, a, b, tag, copy):
             w_codes, w_scales = w13_mx[e]
@@ -376,6 +373,7 @@ def tile_moe_bdx_glu_silu_kernel(tc, dyT, a1, a3, w2, w1, w3, gate, offs, pos1, 
         quantise_g(0)
         round_w2(0)
         load_w2(2)
+        load_w13(0, 1, "w13_early")
         quantise_w2(0)
         round_g(1, HALF, C)
         make_tanh(0, (2, 3))
@@ -384,7 +382,6 @@ def tile_moe_bdx_glu_silu_kernel(tc, dyT, a1, a3, w2, w1, w3, gate, offs, pos1, 
         run(0)
         load_w2(3)
         load_a3(2)
-        load_w13(0, 1, "w13_early")
         load_a1_half(3, 0)
         load_a1_half(3, 1)
         quantise_w2(1)
@@ -415,14 +412,14 @@ def tile_moe_bdx_glu_silu_kernel(tc, dyT, a1, a3, w2, w1, w3, gate, offs, pos1, 
         round_w13(3)
 
         run(3)
-        quantise_da(3, (C + HALF, 2 * C))
-        quantise_da(3, (HALF, C))
-        dh_banks, turned_banks = handed["dh"][-RING:], handed["turned"][-RING:]
-        second_product(0, 0, C, dh_banks[3], nc.scalar.copy)
-        second_product(1, 0, C, turned_banks[0], nc.scalar.copy)
-        second_product(2, 0, C, dh_banks[0], nc.scalar.copy)
-        second_product(3, 0, HALF, dh_banks[1], nc.scalar.copy)
-        second_product(3, HALF, C, dh_banks[2], nc.vector.tensor_copy)
+        quantise_da(3, (HALF, HALF + P))
+        quantise_da(3, (HALF + P, C))
+        second_product(0, 0, C, "dh3", nc.scalar.copy)
+        second_product(1, 0, C, "turned0", nc.scalar.copy)
+        second_product(2, 0, C, "dh0", nc.scalar.copy)
+        second_product(3, 0, HALF, "dh1", nc.scalar.copy)
+        second_product(3, HALF, HALF + P, "dh2", nc.scalar.copy)
+        second_product(3, HALF + P, C, "turned1", nc.vector.tensor_copy)
 
         tokens = in_turn("turn0", "tokens", [P, 2, T], F32)
         first, both = tokens[:, 0, :], tokens[:, 1, :]

@@ -11,11 +11,11 @@ UNITS = C // P
 HALF = C // 2
 QUAD = 4
 PAIR = 2
-PIECE_ENDS = (160, 448, 672, 864, 1024)
-STORE_ENDS = (448, 672, 864, 1024)
+LIST_ROWS = 16
+RANGE_ENDS = (160, 448, 672, 864, 1024)
 
 FLOPS = 2 * S * H * N + 2 * 2 * S * H * K
-BYTES = 4 * (N * T + 2 * H * S + S + E * N * H + 2 * E * H * K + K * T) + 2 * P * (S + 2 * T) // 16
+BYTES = 4 * (N * T + 2 * H * S + S + E * N * H + 2 * E * H * K + K * T) + 2 * P * (S + 2 * T) // LIST_ROWS
 
 F32 = mybir.dt.float32
 BF16 = mybir.dt.bfloat16
@@ -36,12 +36,18 @@ def tile_moe_bdx_glu_silu_kernel(tc, dyT, a1, a3, w2, w1, w3, gate, offs, pos1, 
     nc = tc.nc
     with ExitStack() as ctx:
         held = ctx.enter_context(tc.tile_pool(name="held", bufs=1))
-        work = ctx.enter_context(tc.tile_pool(name="work", bufs=2))
-        psum = ctx.enter_context(tc.psum_pool(name="psum", bufs=2))
+        work = ctx.enter_context(tc.tile_pool(name="work", bufs=1))
+        psum = ctx.enter_context(tc.psum_pool(name="psum", bufs=1))
 
-        offs_sb = held.tile([P, S // 16], U16, name="offs_sb")
-        pos1_sb = held.tile([P, T // 16], U16, name="pos1_sb")
-        pos2_sb = held.tile([P, T // 16], U16, name="pos2_sb")
+        def in_place(place, name, shape, dtype):
+            return work.tile(shape, dtype, name=name, tag=place, align_bytes=64)
+
+        def in_bank(bank, name, shape):
+            return psum.tile(shape, F32, name=name, tag=bank)
+
+        offs_sb = held.tile([P, S // LIST_ROWS], U16, name="offs_sb")
+        pos1_sb = held.tile([P, T // LIST_ROWS], U16, name="pos1_sb")
+        pos2_sb = held.tile([P, T // LIST_ROWS], U16, name="pos2_sb")
         dy_sb = [held.tile([P, T], F32, name="dy%d" % j, tag="dy%d" % j) for j in range(PACK)]
         gate_first = held.tile([P, C], F32, name="gate_first")
         gate_quads = held.tile([P, E - 1, QUAD], F32, name="gate_quads")
@@ -59,6 +65,9 @@ def tile_moe_bdx_glu_silu_kernel(tc, dyT, a1, a3, w2, w1, w3, gate, offs, pos1, 
         def unit_slots(u):
             return slice(u * P, (u + 1) * P)
 
+        def entries(list_sb, a, b):
+            return list_sb[:, a // LIST_ROWS : b // LIST_ROWS]
+
         w2_raw, w13_raw, a1_sb, a3_sb = {}, {}, {}, {}
         dy_rows = dyT.rearrange("(p j) c -> p j c", j=PACK)
 
@@ -66,30 +75,28 @@ def tile_moe_bdx_glu_silu_kernel(tc, dyT, a1, a3, w2, w1, w3, gate, offs, pos1, 
             nc.sync.dma_start(out=dy_sb[j][:], in_=dy_rows[:, j, :])
 
         def load_w2(e):
-            raw = work.tile([P, PACK, H], F32, name="w2_raw", tag="w2_raw%d" % (0, 1, 2, 1)[e], bufs=1, align_bytes=64)
+            raw = in_place("w2_raw%d" % (e if e + 1 < E else 1), "w2_raw", [P, PACK, H], F32)
             nc.sync.dma_start(out=raw[:], in_=w2[e].rearrange("(p j) i -> p j i", j=PACK))
             w2_raw[e] = raw
 
-        def load_w13(first, count, slot):
-            raw = work.tile([P, count, 2, PACK * K], F32, name="w13_raw", tag=slot, bufs=1, align_bytes=64)
+        def load_w13(pair, place):
+            raw = in_place(place, "w13_raw", [P, 2, 2, PACK * K], F32)
             for w, weights in enumerate((w1, w3)):
-                nc.sync.dma_start(
-                    out=raw[:, :, w, :], in_=weights[first : first + count].rearrange("e (q r) k -> q e (r k)", r=PACK)
-                )
-            for j in range(count):
-                w13_raw[first + j] = raw[:, j, :, :]
+                rows = weights[2 * pair : 2 * pair + 2].rearrange("e (q r) k -> q e (r k)", r=PACK)
+                nc.sync.dma_start(out=raw[:, :, w, :], in_=rows)
+            w13_raw[pair] = raw
 
         def a1_rows(a, b):
             return a1[:, a:b].rearrange("(q r) s -> q r s", r=PACK)
 
         def load_a1_half(e, half):
-            raw = work.tile([P, PACK, HALF], F32, name="a1_half", tag="a1_half%d" % half, bufs=1, align_bytes=64)
+            raw = in_place("a1_half%d" % half, "a1_half", [P, PACK, HALF], F32)
             a = e * C + half * HALF
             nc.sync.dma_start(out=raw[:], in_=a1_rows(a, a + HALF))
             a1_sb[e, half] = raw[:]
 
         def load_a1(e):
-            raw = work.tile([P, PACK, C], F32, name="a1_sb", tag="a1_sb%d" % e, bufs=1, align_bytes=64)
+            raw = in_place("a1_whole%d" % e, "a1_whole", [P, PACK, C], F32)
             nc.sync.dma_start(out=raw[:], in_=a1_rows(e * C, (e + 1) * C))
             for half in range(2):
                 a1_sb[e, half] = raw[:, :, half * HALF : (half + 1) * HALF]
@@ -98,49 +105,45 @@ def tile_moe_bdx_glu_silu_kernel(tc, dyT, a1, a3, w2, w1, w3, gate, offs, pos1, 
             return a1_sb[e, u // 2][:, :, unit_slots(u % 2)]
 
         def load_a3(e):
-            raw = work.tile([P, PACK, C], F32, name="a3_sb", tag="a3_sb%d" % (e % 2), bufs=1, align_bytes=64)
+            raw = in_place("a3_%d" % (e % 2), "a3_sb", [P, PACK, C], F32)
             step = HALF if e == 0 else C
             for a in range(0, C, step):
                 rows = a3[:, e * C + a : e * C + a + step].rearrange("(q r) s -> q r s", r=PACK)
                 nc.sync.dma_start(out=raw[:, :, a : a + step], in_=rows)
             a3_sb[e] = raw
 
-        g_raw, g_grp, w2_grp, gate_ps = {}, {}, {}, {}
-        w13_grp = {}
+        g_raw, g_grp, w2_grp, w13_grp, gate_ps = {}, {}, {}, {}, {}
         g_mx, w2_mx, w13_mx, da_mx = {}, {}, {}, {}
-        def bank_tile(name, shape, tag):
-            return psum.tile(shape, F32, name=name, tag=tag, bufs=1)
 
-        def in_turn(slot, name, shape, dtype):
-            return work.tile(shape, dtype, name=name, tag=slot, bufs=1, align_bytes=64)
-
-        pieces = {0: ((0, C, "turn0"),), 1: ((0, C, "turn1"),)}
-        pieces[2] = ((0, P, "w2_raw0"), (P, C, "turn3"))
-        pieces[3] = ((0, C, "turn1"),)
+        pieces = (
+            ((0, C, "gathered0"),),
+            ((0, C, "gathered1"),),
+            ((0, P, "w2_raw0"), (P, C, "silu_b")),
+            ((0, C, "gathered1"),),
+        )
 
         def gather(e, piece, planes):
-            a, b, slot = pieces[e][piece]
+            a, b, place = pieces[e][piece]
             if (e, piece) not in g_raw:
-                g_raw[e, piece] = in_turn(slot, "g_raw", [P, PACK, b - a], F32)
+                g_raw[e, piece] = in_place(place, "g_raw", [P, PACK, b - a], F32)
             for j in planes:
-                window = dy_sb[j][:].indirect(offs_sb[:, (e * C + a) // 16 : (e * C + b) // 16])
+                window = dy_sb[j][:].indirect(entries(offs_sb, e * C + a, e * C + b))
                 if e == 0:
                     nc.vector.tensor_tensor(g_raw[e, piece][:, j, :], window, gate_first[:], MULT)
                 else:
                     nc.scalar.activation(g_raw[e, piece][:, j, :], window, COPY)
 
         def spread_gate(e):
-            bank = bank_tile("gate_ps", [P, P, QUAD], "dh2" if e > 1 else "dh3")
+            bank = in_bank("dh3" if e == 1 else "dh2", "gate_ps", [P, P, QUAD])
             for i in range(QUAD):
                 nc.tensor.transpose(bank[:, :, i], gate_quads[:, e - 1, i : i + 1].to_broadcast([P, P]), ident[:])
             gate_ps[e] = bank
 
-        shared_grp = in_turn("g_grp1", "shared_grp", [P, (C + HALF) * PACK], BF16)
+        shared_grp = in_place("g_grp1", "shared_grp", [P, (C + HALF) * PACK], BF16)
 
-        def round_g(e, a, b):
+        def round_g(e, piece, a, b):
             if e not in g_grp:
-                g_grp[e] = shared_grp[:, : C * PACK] if e == 1 else in_turn("g_grp%d" % e, "g_grp", [P, C * PACK], BF16)
-            piece = max(k for k in range(len(pieces[e])) if pieces[e][k][0] <= a)
+                g_grp[e] = shared_grp[:, : C * PACK] if e == 1 else in_place("g_grp%d" % e, "g_grp", [P, C * PACK], BF16)
             first = pieces[e][piece][0]
             into = g_grp[e][:, a * PACK : b * PACK].rearrange("p (n i j) -> p n j i", i=QUAD, j=PACK)
             values = g_raw[e, piece][:, :, a - first : b - first].rearrange("p j (n i) -> p n j i", i=QUAD)
@@ -151,66 +154,60 @@ def tile_moe_bdx_glu_silu_kernel(tc, dyT, a1, a3, w2, w1, w3, gate, offs, pos1, 
                 nc.vector.tensor_tensor(into, values, gates.to_broadcast([P, (b - a) // QUAD, PACK, QUAD]), MULT)
 
         def round_w2(e):
-            grp = shared_grp[:, HALF * PACK :] if e == 0 else in_turn("turn4", "w2_grp", [P, H * PACK], BF16)
+            grp = shared_grp[:, HALF * PACK :] if e == 0 else in_place("w2_grp", "w2_grp", [P, H * PACK], BF16)
             into = grp[:].rearrange("p (r q j) -> p q j r", r=PACK, j=PACK)
             values = w2_raw[e][:].rearrange("p j (q r) -> p q j r", r=PACK)
             if e == 0:
-                nc.vector.tensor_scalar(into[:, :, :, :PAIR], values[:, :, :, :PAIR], 0.5, None, op0=MULT)
-                nc.scalar.activation(into[:, :, :, PAIR:], values[:, :, :, PAIR:], COPY, scale=0.5)
+                nc.vector.tensor_scalar(into[:, :, :, :2], values[:, :, :, :2], 0.5, None, op0=MULT)
+                nc.scalar.activation(into[:, :, :, 2:], values[:, :, :, 2:], COPY, scale=0.5)
             else:
                 nc.scalar.activation(into, values, COPY, scale=0.5)
             w2_grp[e] = grp
 
-        def round_w13(e):
-            w13_grp[e] = in_turn(("turn6", "w13_grp1", "w13_grp2", "w13_grp3")[e], "w13_grp", [P, 2 * K * PACK], BF16)
-            if e == 0:
-                nc.gpsimd.tensor_scalar(
-                    w13_grp[e][:].rearrange("p (w c r) -> p w c r", w=2, r=PACK),
-                    w13_raw[e].rearrange("p w (r c) -> p w c r", r=PACK),
-                    1.0,
-                    0.0,
-                    op0=MULT,
-                    op1=ADD,
-                )
-            else:
+        def round_w13(pair):
+            w13_grp[pair] = in_place(("w13_grp", "w2_grp")[pair], "w13_grp", [P, 2, 2 * K * PACK], BF16)
+            for j in range(2):
                 nc.scalar.copy(
-                    out=w13_grp[e][:].rearrange("p (w c i r) -> p w c r i", w=2, i=PAIR, r=PACK),
-                    in_=w13_raw[e].rearrange("p w (r c i) -> p w c r i", i=PAIR, r=PACK),
+                    out=w13_grp[pair][:, j, :].rearrange("p (w c i r) -> p w c r i", w=2, i=PAIR, r=PACK),
+                    in_=w13_raw[pair][:, j, :, :].rearrange("p w (r c i) -> p w c r i", i=PAIR, r=PACK),
                 )
 
-        def quantise(grp, tag, fmt, width, codes, bufs=2):
-            scales = work.tile([P, width], U8, name=tag + "_scales", tag=tag + "_scales", bufs=bufs, align_bytes=64)
-            nc.vector.quantize_mx(out=codes.bitcast(fmt), scales=scales[:], in_=grp[:])
-            return codes, scales
+        def scale_tile(name, width, bufs):
+            return work.tile([P, width], U8, name=name, tag=name, bufs=bufs, align_bytes=64)
 
         codes_sb = {}
 
         def operand_codes(e):
             if e not in codes_sb:
-                codes_sb[e] = work.tile([P, H + C], U32, name="codes", tag="turns", bufs=1, align_bytes=64)
+                codes_sb[e] = in_place("codes_or_w", "codes", [P, H + C], U32)
             return codes_sb[e]
 
         def quantise_w2(e):
-            w2_mx[e] = quantise(w2_grp[e], "w2", E4M3X4, H, operand_codes(e)[:, :H])
+            codes, scales = operand_codes(e)[:, :H], scale_tile("w2_scales", H, 2)
+            nc.vector.quantize_mx(out=codes.bitcast(E4M3X4), scales=scales[:], in_=w2_grp[e][:])
+            w2_mx[e] = codes, scales
 
         def quantise_g(e):
-            g_mx[e] = quantise(g_grp[e], "g", E5M2X4, C, operand_codes(e)[:, H : H + C])
+            codes, scales = operand_codes(e)[:, H:], scale_tile("g_scales", C, 2)
+            nc.vector.quantize_mx(out=codes.bitcast(E5M2X4), scales=scales[:], in_=g_grp[e][:])
+            g_mx[e] = codes, scales
 
-        def quantise_da(e, columns):
+        def quantise_da(e, a, b):
             if e not in da_mx:
-                codes = in_turn("g_grp%d" % ((e + 1) % E), "da_codes", [P, 2 * C], U32)
-                da_mx[e] = codes, work.tile([P, 2 * C], U8, name="da_scales", tag="da_scales", bufs=E, align_bytes=64)
+                codes = in_place("g_grp%d" % ((e + 1) % E), "da_codes", [P, 2 * C], U32)
+                da_mx[e] = codes, scale_tile("da_scales", 2 * C, E)
             codes, scales = da_mx[e]
-            a, b = columns
             nc.vector.quantize_mx(
                 out=codes[:, a:b].bitcast(E5M2X4), scales=scales[:, a:b], in_=da_grp[e % 2][:, a * PACK : b * PACK]
             )
 
-        def quantise_w13(first, slot):
-            codes = work.tile([P, 4 * K], U32, name="w13_codes", tag=slot, bufs=1, align_bytes=64)
+        def quantise_w13(pair, place):
+            codes, scales = in_place(place, "w13_codes", [P, 4 * K], U32), scale_tile("w13_scales", 4 * K, 2)
+            grp = w13_grp[pair][:].rearrange("p e c -> p (e c)")
+            nc.vector.quantize_mx(out=codes[:].bitcast(E4M3X4), scales=scales[:], in_=grp)
             for j in range(2):
                 cols = slice(j * 2 * K, (j + 1) * 2 * K)
-                w13_mx[first + j] = quantise(w13_grp[first + j], "w13", E4M3X4, 2 * K, codes[:, cols], bufs=E)
+                w13_mx[2 * pair + j] = codes[:, cols], scales[:, cols]
 
         silu_sb, less = {}, {}
 
@@ -219,15 +216,16 @@ def tile_moe_bdx_glu_silu_kernel(tc, dyT, a1, a3, w2, w1, w3, gate, offs, pos1, 
 
         def make_tanh(e, units=range(UNITS)):
             for u in units:
-                bank = bank_tile("a1_turned", [P, PACK, P], ("dh3", "turned0", "turned1", "dh3")[u] if e > 0 else "turned%d" % u)
+                name = ("dh3", "turned0", "turned1", "dh3")[u] if e > 0 else "turned%d" % u
+                bank = in_bank(name, "a1_turned", [P, PACK, P])
                 for r in range(PACK):
                     nc.tensor.transpose(bank[:, r, :], a1_unit(e, u)[:, r, :], ident[:])
                 nc.scalar.activation(tanh_unit(u), bank[:].rearrange("p r q -> p (r q)"), TANH, scale=0.5)
 
-        silu_slots = (("turn2", "turn6"), ("turn3", "turn1"), ("turn6", "turn2"), ("turn2", "turn1"))
+        silu_places = (("silu_a", "silu_c"), ("silu_b", "gathered1"), ("silu_c", "silu_a"), ("gathered0", "gathered1"))
 
         def make_silu(e, half):
-            silu = in_turn(silu_slots[e][half], "silu_sb", [P, PACK, HALF], F32)[:]
+            silu = in_place(silu_places[e][half], "silu_sb", [P, PACK, HALF], F32)[:]
             nc.scalar.activation(silu, a1_sb[e, half], SILU, scale=-1.0, bias=zero_bias[:])
             silu_sb[e, half] = silu
             if (e, half) == (E - 1, 1):
@@ -235,7 +233,7 @@ def tile_moe_bdx_glu_silu_kernel(tc, dyT, a1, a3, w2, w1, w3, gate, offs, pos1, 
                 nc.scalar.activation(silu, silu, COPY, scale=-1.0, bias=1.0)
 
         def subtract_from_one(e, half):
-            less[e, half] = in_turn("turn5", "less_sb", [P, PACK, HALF], F32)[:]
+            less[e, half] = in_place("less", "less_sb", [P, PACK, HALF], F32)[:]
             nc.gpsimd.tensor_scalar(less[e, half], silu_sb[e, half], -1.0, 1.0, op0=MULT, op1=ADD)
 
         w_sb = {}
@@ -245,7 +243,7 @@ def tile_moe_bdx_glu_silu_kernel(tc, dyT, a1, a3, w2, w1, w3, gate, offs, pos1, 
                 flat = da_grp[(e + 1) % 2][:].bitcast(F32)[:, : PACK * HALF]
                 w_sb[e, half] = flat.rearrange("p (r s) -> p r s", r=PACK)
             else:
-                w_sb[e, half] = in_turn("turns" if e + 1 < E else "turn5", "w_late", [P, PACK, HALF], F32)[:]
+                w_sb[e, half] = in_place("codes_or_w" if e + 1 < E else "less", "w_late", [P, PACK, HALF], F32)[:]
             nc.gpsimd.tensor_tensor(w_sb[e, half], less[e, half], a3_sb[e][:, :, half * HALF : (half + 1) * HALF], MULT)
 
         def w_unit(e, u):
@@ -256,7 +254,7 @@ def tile_moe_bdx_glu_silu_kernel(tc, dyT, a1, a3, w2, w1, w3, gate, offs, pos1, 
         def first_product(e, u):
             g_codes, g_scales = g_mx[e]
             w_codes, w_scales = w2_mx[e]
-            bank = bank_tile("dh", [P, H], "dh%d" % u)
+            bank = in_bank("dh%d" % u, "dh", [P, H])
             nc.tensor.matmul_mx(
                 out=bank[:],
                 lhsT=g_codes[:, unit_slots(u)].bitcast(E5M2X4),
@@ -273,7 +271,7 @@ def tile_moe_bdx_glu_silu_kernel(tc, dyT, a1, a3, w2, w1, w3, gate, offs, pos1, 
             nc.vector.scalar_tensor_tensor(
                 out=m[:], in0=tanh_unit(u), scalar=1.0, in1=dh_ps[e, u][:], op0=ADD, op1=MULT
             )
-            bank = bank_tile("m_turned", [P, PACK, P], "turned%d" % u)
+            bank = in_bank("turned%d" % u, "m_turned", [P, PACK, P])
             for r in range(PACK):
                 nc.tensor.transpose(bank[:, r, :], m[:, r * P : (r + 1) * P], ident[:])
             m_ps[e, u] = bank
@@ -292,20 +290,20 @@ def tile_moe_bdx_glu_silu_kernel(tc, dyT, a1, a3, w2, w1, w3, gate, offs, pos1, 
             for u in range(UNITS):
                 first_product(e, u)
             make_w(e, 0)
-            if (e, 1) not in less:
+            if not last:
                 subtract_from_one(e, 1)
             make_w(e, 1)
             if not last:
                 make_silu(e + 1, 0)
                 subtract_from_one(e + 1, 0)
-                if e == 1:
-                    round_w13(0)
             for u in range(UNITS):
                 make_m(e, u)
             if not last:
                 if e > 0:
                     spread_gate(e + 1)
                 round_w2(e + 1)
+            if e + 2 == E:
+                round_w13(0)
             for u in range(2):
                 make_da(e, u, 1, a1_unit(e, u))
                 make_da(e, u, 0, w_unit(e, u))
@@ -314,30 +312,30 @@ def tile_moe_bdx_glu_silu_kernel(tc, dyT, a1, a3, w2, w1, w3, gate, offs, pos1, 
             make_da(e, 2, 1, a1_unit(e, 2))
             if last:
                 make_da(e, 3, 1, a1_unit(e, 3))
-                quantise_w13(2, "a1_half1")
-                quantise_da(e, (C, 2 * C))
-                quantise_da(e, (0, HALF))
+                quantise_w13(1, "a1_half1")
+                quantise_da(e, C, 2 * C)
+                quantise_da(e, 0, HALF)
             elif e > 0:
-                for a, b, slot in pieces[e + 1]:
-                    round_g(e + 1, a, b)
+                for piece, (a, b, place) in enumerate(pieces[e + 1]):
+                    round_g(e + 1, piece, a, b)
             make_da(e, 2, 0, w_unit(e, 2))
             make_da(e, 3, 0, w_unit(e, 3))
             if not last:
                 make_da(e, 3, 1, a1_unit(e, 3))
 
-        def second_product(e, a, b, tag, copy):
+        def second_product(e, a, b, bank_name, copy):
             w_codes, w_scales = w13_mx[e]
-            bank = bank_tile("dx", [P, b - a], tag)
+            bank = in_bank(bank_name, "dx", [P, b - a])
             da_codes, da_scales = da_mx[e]
             for which in (1, 0):
                 cols = slice(which * K, (which + 1) * K)
-                slots = slice(which * C + a, which * C + b)
+                words = slice(which * C + a, which * C + b)
                 nc.tensor.matmul_mx(
                     out=bank[:],
                     lhsT=w_codes[:, cols].bitcast(E4M3X4),
                     lhsT_scale=w_scales[:, cols],
-                    rhs=da_codes[:, slots].bitcast(E5M2X4),
-                    rhs_scale=da_scales[:, slots],
+                    rhs=da_codes[:, words].bitcast(E5M2X4),
+                    rhs_scale=da_scales[:, words],
                     start=which == 1,
                     stop=which == 0,
                 )
@@ -368,14 +366,13 @@ def tile_moe_bdx_glu_silu_kernel(tc, dyT, a1, a3, w2, w1, w3, gate, offs, pos1, 
         make_silu(0, 0)
         subtract_from_one(0, 0)
         make_tanh(0, (0, 1))
-        round_g(0, 0, C)
-        round_g(1, 0, HALF)
+        round_g(0, 0, 0, C)
+        round_g(1, 0, 0, HALF)
         quantise_g(0)
         round_w2(0)
         load_w2(2)
-        load_w13(0, 1, "w13_early")
         quantise_w2(0)
-        round_g(1, HALF, C)
+        round_g(1, 0, HALF, C)
         make_tanh(0, (2, 3))
         make_silu(0, 1)
 
@@ -386,34 +383,32 @@ def tile_moe_bdx_glu_silu_kernel(tc, dyT, a1, a3, w2, w1, w3, gate, offs, pos1, 
         load_a1_half(3, 1)
         quantise_w2(1)
         quantise_g(1)
-        quantise_da(0, (0, 2 * C))
+        quantise_da(0, 0, 2 * C)
         make_silu(1, 1)
         gather(2, 0, range(PACK))
         gather(2, 1, range(PACK))
 
         run(1)
+        load_w13(0, "w2_raw2")
         load_a3(3)
-        load_w13(1, 1, "a1_sb1")
         quantise_w2(2)
         quantise_g(2)
-        quantise_da(1, (0, 2 * C))
+        quantise_da(1, 0, 2 * C)
         make_silu(2, 1)
         gather(3, 0, range(PACK))
 
         run(2)
-        load_w13(2, 2, "a3_sb0")
-        round_w13(1)
+        load_w13(1, "a1_whole1")
         quantise_w2(3)
         quantise_g(3)
-        quantise_w13(0, "a1_sb2")
-        quantise_da(2, (0, 2 * C))
+        quantise_w13(0, "a1_whole2")
+        quantise_da(2, 0, 2 * C)
         make_silu(3, 1)
-        round_w13(2)
-        round_w13(3)
+        round_w13(1)
 
         run(3)
-        quantise_da(3, (HALF, HALF + P))
-        quantise_da(3, (HALF + P, C))
+        quantise_da(3, HALF, HALF + P)
+        quantise_da(3, HALF + P, C)
         second_product(0, 0, C, "dh3", nc.scalar.copy)
         second_product(1, 0, C, "turned0", nc.scalar.copy)
         second_product(2, 0, C, "dh0", nc.scalar.copy)
@@ -421,17 +416,15 @@ def tile_moe_bdx_glu_silu_kernel(tc, dyT, a1, a3, w2, w1, w3, gate, offs, pos1, 
         second_product(3, HALF, HALF + P, "dh2", nc.scalar.copy)
         second_product(3, HALF + P, C, "turned1", nc.vector.tensor_copy)
 
-        tokens = in_turn("turn0", "tokens", [P, 2, T], F32)
+        tokens = in_place("gathered0", "tokens", [P, 2, T], F32)
         first, both = tokens[:, 0, :], tokens[:, 1, :]
-        token_pieces = list(zip((0,) + PIECE_ENDS, PIECE_ENDS))
-        stored = 0
-        for a, b in token_pieces:
-            window = dx_sb[:].indirect(pos1_sb[:, a // 16 : b // 16])
+        for a, b in zip((0,) + RANGE_ENDS, RANGE_ENDS):
+            window = dx_sb[:].indirect(entries(pos1_sb, a, b))
             if a == 0:
                 nc.vector.tensor_copy(first[:, a:b], window)
             else:
                 nc.scalar.activation(first[:, a:b], window, COPY)
-            nc.vector.tensor_tensor(both[:, a:b], dx_sb[:].indirect(pos2_sb[:, a // 16 : b // 16]), first[:, a:b], ADD)
-            if b in STORE_ENDS:
-                nc.sync.dma_start(out=out[:, stored:b], in_=both[:, stored:b])
-                stored = b
+            nc.vector.tensor_tensor(both[:, a:b], dx_sb[:].indirect(entries(pos2_sb, a, b)), first[:, a:b], ADD)
+            if a > 0:
+                begin = 0 if a == RANGE_ENDS[0] else a
+                nc.sync.dma_start(out=out[:, begin:b], in_=both[:, begin:b])

@@ -155,11 +155,11 @@ def tile_moe_bdx_glu_silu_kernel(tc, dyT, a1, a3, w2, w1, w3, gate, offs, pos1, 
 
         def round_w2(e):
             grp = shared_grp[:, HALF * PACK :] if e == 0 else in_place("w2_grp", "w2_grp", [P, H * PACK], BF16)
-            into = grp[:].rearrange("p (r q j) -> p q j r", r=PACK, j=PACK)
-            values = w2_raw[e][:].rearrange("p j (q r) -> p q j r", r=PACK)
+            into = grp[:].rearrange("p (n i j) -> p n j i", i=QUAD, j=PACK)
+            values = w2_raw[e][:].rearrange("p j (n i) -> p n j i", i=QUAD)
             if e == 0:
-                nc.vector.tensor_scalar(into[:, :, :, :2], values[:, :, :, :2], 0.5, None, op0=MULT)
-                nc.scalar.activation(into[:, :, :, 2:], values[:, :, :, 2:], COPY, scale=0.5)
+                nc.vector.tensor_scalar(into[:, : P // 2], values[:, : P // 2], 0.5, None, op0=MULT)
+                nc.scalar.activation(into[:, P // 2 :], values[:, P // 2 :], COPY, scale=0.5)
             else:
                 nc.scalar.activation(into, values, COPY, scale=0.5)
             w2_grp[e] = grp
@@ -269,7 +269,12 @@ def tile_moe_bdx_glu_silu_kernel(tc, dyT, a1, a3, w2, w1, w3, gate, offs, pos1, 
         def make_m(e, u):
             m = work.tile([P, H], F32, name="m_sb", tag="m_sb", bufs=UNITS)
             nc.vector.scalar_tensor_tensor(
-                out=m[:], in0=tanh_unit(u), scalar=1.0, in1=dh_ps[e, u][:], op0=ADD, op1=MULT
+                out=m[:].rearrange("p (r q) -> p r q", r=PACK),
+                in0=tanh_unit(u).rearrange("p (r q) -> p r q", r=PACK),
+                scalar=1.0,
+                in1=dh_ps[e, u][:].rearrange("p (q r) -> p r q", r=PACK),
+                op0=ADD,
+                op1=MULT,
             )
             bank = in_bank("turned%d" % u, "m_turned", [P, PACK, P])
             for r in range(PACK):

@@ -51,6 +51,7 @@ def tile_moe_bdx_glu_silu_kernel(tc, dyT, a1, a3, w2, w1, w3, gate, offs, pos1, 
         dy_sb = [held.tile([P, T], F32, name="dy%d" % j, tag="dy%d" % j) for j in range(PACK)]
         gate_first = held.tile([P, C], F32, name="gate_first")
         gate_quads = held.tile([P, E - 1, QUAD], F32, name="gate_quads")
+        gate_column = held.tile([P, 2], F32, name="gate_column")
         tanh_sb = held.tile([P, UNITS * H], F32, name="tanh_sb")
         da_grp = [held.tile([P, 2 * C * PACK], BF16, name="da_grp%d" % j, align_bytes=64) for j in range(2)]
         dx_sb = held.tile([P, S], F32, name="dx_sb")
@@ -119,7 +120,7 @@ def tile_moe_bdx_glu_silu_kernel(tc, dyT, a1, a3, w2, w1, w3, gate, offs, pos1, 
             ((0, C, "gathered0"),),
             ((0, C, "gathered1"),),
             ((0, P, "w2_raw0"), (P, C, "silu_b")),
-            ((0, C, "gathered1"),),
+            ((0, P, "a1_whole1"), (P, C, "gathered1")),
         )
 
         def gather(e, piece, planes):
@@ -139,6 +140,11 @@ def tile_moe_bdx_glu_silu_kernel(tc, dyT, a1, a3, w2, w1, w3, gate, offs, pos1, 
                 nc.tensor.transpose(bank[:, :, i], gate_quads[:, e - 1, i : i + 1].to_broadcast([P, P]), ident[:])
             gate_ps[e] = bank
 
+        def spread_first_gates(e):
+            bank = in_bank("turned3", "gate_ps", [P, P])
+            nc.tensor.transpose(bank[:], gate_column[:, e - 2 : e - 1].to_broadcast([P, P]), ident[:])
+            gate_ps[e, 0] = bank[:].rearrange("p (n i) -> p n i", i=QUAD)
+
         shared_grp = in_place("g_grp1", "shared_grp", [P, (C + HALF) * PACK], BF16)
 
         def round_g(e, piece, a, b):
@@ -150,7 +156,7 @@ def tile_moe_bdx_glu_silu_kernel(tc, dyT, a1, a3, w2, w1, w3, gate, offs, pos1, 
             if e == 0:
                 nc.vector.tensor_copy(into, values)
             else:
-                gates = gate_ps[e][:, a // QUAD : b // QUAD, :].unsqueeze(2)
+                gates = (gate_ps[e, a] if (e, a) in gate_ps else gate_ps[e][:, a // QUAD : b // QUAD, :]).unsqueeze(2)
                 nc.vector.tensor_tensor(into, values, gates.to_broadcast([P, (b - a) // QUAD, PACK, QUAD]), MULT)
 
         def round_w2(e):
@@ -164,12 +170,12 @@ def tile_moe_bdx_glu_silu_kernel(tc, dyT, a1, a3, w2, w1, w3, gate, offs, pos1, 
                 nc.scalar.activation(into, values, COPY, scale=0.5)
             w2_grp[e] = grp
 
-        def round_w13(pair):
-            w13_grp[pair] = in_place(("w13_grp", "w2_grp")[pair], "w13_grp", [P, 2, 2 * K * PACK], BF16)
-            for j in range(2):
+        def round_w13(experts, place):
+            w13_grp[experts] = in_place(place, "w13_grp", [P, len(experts), 2 * K * PACK], BF16)
+            for j, e in enumerate(experts):
                 nc.scalar.copy(
-                    out=w13_grp[pair][:, j, :].rearrange("p (w c i r) -> p w c r i", w=2, i=PAIR, r=PACK),
-                    in_=w13_raw[pair][:, j, :, :].rearrange("p w (r c i) -> p w c r i", i=PAIR, r=PACK),
+                    out=w13_grp[experts][:, j, :].rearrange("p (w c i r) -> p w c r i", w=2, i=PAIR, r=PACK),
+                    in_=w13_raw[e // 2][:, e % 2, :, :].rearrange("p w (r c i) -> p w c r i", i=PAIR, r=PACK),
                 )
 
         def scale_tile(name, width, bufs):
@@ -201,13 +207,16 @@ def tile_moe_bdx_glu_silu_kernel(tc, dyT, a1, a3, w2, w1, w3, gate, offs, pos1, 
                 out=codes[:, a:b].bitcast(E5M2X4), scales=scales[:, a:b], in_=da_grp[e % 2][:, a * PACK : b * PACK]
             )
 
-        def quantise_w13(pair, place):
-            codes, scales = in_place(place, "w13_codes", [P, 4 * K], U32), scale_tile("w13_scales", 4 * K, 2)
-            grp = w13_grp[pair][:].rearrange("p e c -> p (e c)")
-            nc.vector.quantize_mx(out=codes[:].bitcast(E4M3X4), scales=scales[:], in_=grp)
-            for j in range(2):
+        def quantise_w13(experts, place):
+            words = len(experts) * 2 * K
+            codes, scales = in_place(place, "w13_codes", [P, words], U32), scale_tile("w13_scales", 6 * K, 2)
+            grp = w13_grp[experts][:].rearrange("p e c -> p (e c)")
+            for a in range(0, words, 4 * K):
+                b = min(a + 4 * K, words)
+                nc.vector.quantize_mx(out=codes[:, a:b].bitcast(E4M3X4), scales=scales[:, a:b], in_=grp[:, a * PACK : b * PACK])
+            for j, e in enumerate(experts):
                 cols = slice(j * 2 * K, (j + 1) * 2 * K)
-                w13_mx[2 * pair + j] = codes[:, cols], scales[:, cols]
+                w13_mx[e] = codes[:, cols], scales[:, cols]
 
         silu_sb, less = {}, {}
 
@@ -276,6 +285,8 @@ def tile_moe_bdx_glu_silu_kernel(tc, dyT, a1, a3, w2, w1, w3, gate, offs, pos1, 
                 op0=ADD,
                 op1=MULT,
             )
+            if 0 < e < E - 1 and u == UNITS - 1:
+                round_g(e + 1, 0, 0, P)
             bank = in_bank("turned%d" % u, "m_turned", [P, PACK, P])
             for r in range(PACK):
                 nc.tensor.transpose(bank[:, r, :], m[:, r * P : (r + 1) * P], ident[:])
@@ -301,6 +312,8 @@ def tile_moe_bdx_glu_silu_kernel(tc, dyT, a1, a3, w2, w1, w3, gate, offs, pos1, 
             if not last:
                 make_silu(e + 1, 0)
                 subtract_from_one(e + 1, 0)
+            if 0 < e < E - 1:
+                spread_first_gates(e + 1)
             for u in range(UNITS):
                 make_m(e, u)
             if not last:
@@ -308,7 +321,7 @@ def tile_moe_bdx_glu_silu_kernel(tc, dyT, a1, a3, w2, w1, w3, gate, offs, pos1, 
                     spread_gate(e + 1)
                 round_w2(e + 1)
             if e + 2 == E:
-                round_w13(0)
+                round_w13((0,), "w13_grp")
             for u in range(2):
                 make_da(e, u, 1, a1_unit(e, u))
                 make_da(e, u, 0, w_unit(e, u))
@@ -317,12 +330,11 @@ def tile_moe_bdx_glu_silu_kernel(tc, dyT, a1, a3, w2, w1, w3, gate, offs, pos1, 
             make_da(e, 2, 1, a1_unit(e, 2))
             if last:
                 make_da(e, 3, 1, a1_unit(e, 3))
-                quantise_w13(1, "a1_half1")
+                quantise_w13((1, 2, 3), "a1_whole3")
                 quantise_da(e, C, 2 * C)
                 quantise_da(e, 0, HALF)
             elif e > 0:
-                for piece, (a, b, place) in enumerate(pieces[e + 1]):
-                    round_g(e + 1, piece, a, b)
+                round_g(e + 1, len(pieces[e + 1]) - 1, *pieces[e + 1][-1][:2])
             make_da(e, 2, 0, w_unit(e, 2))
             make_da(e, 3, 0, w_unit(e, 3))
             if not last:
@@ -360,6 +372,7 @@ def tile_moe_bdx_glu_silu_kernel(tc, dyT, a1, a3, w2, w1, w3, gate, offs, pos1, 
         load_w2(1)
         load_a1(1)
         load_a3(1)
+        nc.sync.dma_start(out=gate_column[:], in_=gate[0, 2 * C :].rearrange("(e n) -> n e", e=2)[:P, :])
         load_a1(2)
         nc.sync.dma_start(pos1_sb[:], pos1)
         nc.sync.dma_start(pos2_sb[:], pos2)
@@ -384,8 +397,7 @@ def tile_moe_bdx_glu_silu_kernel(tc, dyT, a1, a3, w2, w1, w3, gate, offs, pos1, 
         run(0)
         load_w2(3)
         load_a3(2)
-        load_a1_half(3, 0)
-        load_a1_half(3, 1)
+        load_a1(3)
         quantise_w2(1)
         quantise_g(1)
         quantise_da(0, 0, 2 * C)
@@ -399,17 +411,18 @@ def tile_moe_bdx_glu_silu_kernel(tc, dyT, a1, a3, w2, w1, w3, gate, offs, pos1, 
         quantise_w2(2)
         quantise_g(2)
         quantise_da(1, 0, 2 * C)
-        make_silu(2, 1)
         gather(3, 0, range(PACK))
+        make_silu(2, 1)
+        gather(3, 1, range(PACK))
 
         run(2)
         load_w13(1, "a1_whole1")
         quantise_w2(3)
         quantise_g(3)
-        quantise_w13(0, "a1_whole2")
+        quantise_w13((0,), "a1_whole2")
         quantise_da(2, 0, 2 * C)
         make_silu(3, 1)
-        round_w13(1)
+        round_w13((1, 2, 3), "w2_grp")
 
         run(3)
         quantise_da(3, HALF, HALF + P)

@@ -135,10 +135,10 @@ def tile_moe_bdx_glu_silu_kernel(tc, dyT, a1, a3, w2, w1, w3, gate, offs, pos1, 
                     nc.scalar.activation(g_raw[e, piece][:, j, :], window, COPY)
 
         def spread_gate(e):
-            bank = in_bank("dh3" if e == 1 else "dh2", "gate_ps", [P, P, QUAD])
+            bank = in_bank("dh3" if e == 1 else "dh2", "gate_ps", [P, QUAD, P])
             for i in range(QUAD):
-                nc.tensor.transpose(bank[:, :, i], gate_quads[:, e - 1, i : i + 1].to_broadcast([P, P]), ident[:])
-            gate_ps[e] = bank
+                nc.tensor.transpose(bank[:, i, :], gate_quads[:, e - 1, i : i + 1].to_broadcast([P, P]), ident[:])
+            gate_ps[e] = bank[:].rearrange("p i n -> p n i")
 
         def spread_first_gates(e):
             bank = in_bank("turned3", "gate_ps", [P, P])

@@ -50,8 +50,8 @@ def tile_moe_bdx_glu_silu_kernel(tc, dyT, a1, a3, w2, w1, w3, gate, offs, pos1, 
         pos2_sb = held.tile([P, T // LIST_ROWS], U16, name="pos2_sb")
         dy_sb = [held.tile([P, T], F32, name="dy%d" % j, tag="dy%d" % j) for j in range(PACK)]
         gate_first = held.tile([P, C], F32, name="gate_first")
-        gate_quads = held.tile([P, E - 1, QUAD], F32, name="gate_quads")
-        gate_column = held.tile([P, 2], F32, name="gate_column")
+        gate_quads = held.tile([P, QUAD], F32, name="gate_quads")
+        gate_units = held.tile([P, 2 * UNITS], F32, name="gate_units")
         tanh_sb = held.tile([P, UNITS * H], F32, name="tanh_sb")
         da_grp = [held.tile([P, 2 * C * PACK], BF16, name="da_grp%d" % j, align_bytes=64) for j in range(2)]
         dx_sb = held.tile([P, S], F32, name="dx_sb")
@@ -134,16 +134,22 @@ def tile_moe_bdx_glu_silu_kernel(tc, dyT, a1, a3, w2, w1, w3, gate, offs, pos1, 
                 else:
                     nc.scalar.activation(g_raw[e, piece][:, j, :], window, COPY)
 
-        def spread_gate(e):
-            bank = in_bank("dh3" if e == 1 else "dh2", "gate_ps", [P, QUAD, P])
-            for i in range(QUAD):
-                nc.tensor.transpose(bank[:, i, :], gate_quads[:, e - 1, i : i + 1].to_broadcast([P, P]), ident[:])
-            gate_ps[e] = bank[:].rearrange("p i n -> p n i")
+        def spread(column):
+            return column.to_broadcast([P, P])
 
-        def spread_first_gates(e):
-            bank = in_bank("turned3", "gate_ps", [P, P])
-            nc.tensor.transpose(bank[:], gate_column[:, e - 2 : e - 1].to_broadcast([P, P]), ident[:])
-            gate_ps[e, 0] = bank[:].rearrange("p (n i) -> p n i", i=QUAD)
+        def spread_second_gates():
+            bank = in_bank("dh3", "gate_ps", [P, QUAD, P])
+            for i in range(QUAD):
+                nc.tensor.transpose(bank[:, i, :], spread(gate_quads[:, i : i + 1]), ident[:])
+            for a in (0, HALF):
+                gate_ps[1, a] = bank[:].rearrange("p i n -> p n i")[:, a // QUAD : (a + HALF) // QUAD, :]
+
+        def spread_gates(e, units, name):
+            bank = in_bank(name, "gate_ps", [P, len(units) * P])
+            for x, u in enumerate(units):
+                column = (e - 2) * UNITS + u
+                nc.tensor.transpose(bank[:, unit_slots(x)], spread(gate_units[:, column : column + 1]), ident[:])
+            gate_ps[e, units[0] * P] = bank[:].rearrange("p (n i) -> p n i", i=QUAD)
 
         shared_grp = in_place("g_grp1", "shared_grp", [P, (C + HALF) * PACK], BF16)
 
@@ -156,7 +162,7 @@ def tile_moe_bdx_glu_silu_kernel(tc, dyT, a1, a3, w2, w1, w3, gate, offs, pos1, 
             if e == 0:
                 nc.vector.tensor_copy(into, values)
             else:
-                gates = (gate_ps[e, a] if (e, a) in gate_ps else gate_ps[e][:, a // QUAD : b // QUAD, :]).unsqueeze(2)
+                gates = gate_ps[e, a].unsqueeze(2)
                 nc.vector.tensor_tensor(into, values, gates.to_broadcast([P, (b - a) // QUAD, PACK, QUAD]), MULT)
 
         def round_w2(e):
@@ -313,12 +319,12 @@ def tile_moe_bdx_glu_silu_kernel(tc, dyT, a1, a3, w2, w1, w3, gate, offs, pos1, 
                 make_silu(e + 1, 0)
                 subtract_from_one(e + 1, 0)
             if 0 < e < E - 1:
-                spread_first_gates(e + 1)
+                spread_gates(e + 1, (0,), "turned3")
             for u in range(UNITS):
                 make_m(e, u)
             if not last:
                 if e > 0:
-                    spread_gate(e + 1)
+                    spread_gates(e + 1, (1, 2, 3), "dh2")
                 round_w2(e + 1)
             if e + 2 == E:
                 round_w13((0,), "w13_grp")
@@ -364,7 +370,7 @@ def tile_moe_bdx_glu_silu_kernel(tc, dyT, a1, a3, w2, w1, w3, gate, offs, pos1, 
         load_dy(1)
         load_dy(2)
         load_dy(3)
-        nc.sync.dma_start(out=gate_quads[:], in_=gate[0, C:].rearrange("(e n i) -> n e i", n=P, i=QUAD))
+        nc.sync.dma_start(out=gate_quads[:], in_=gate[0, C : 2 * C].rearrange("(n i) -> n i", i=QUAD))
         load_a1_half(0, 0)
         load_w2(0)
         load_a1_half(0, 1)
@@ -372,7 +378,7 @@ def tile_moe_bdx_glu_silu_kernel(tc, dyT, a1, a3, w2, w1, w3, gate, offs, pos1, 
         load_w2(1)
         load_a1(1)
         load_a3(1)
-        nc.sync.dma_start(out=gate_column[:], in_=gate[0, 2 * C :].rearrange("(e n) -> n e", e=2)[:P, :])
+        nc.sync.dma_start(out=gate_units[:], in_=gate[0, 2 * C :].rearrange("(x n) -> n x", n=P))
         load_a1(2)
         nc.sync.dma_start(pos1_sb[:], pos1)
         nc.sync.dma_start(pos2_sb[:], pos2)
@@ -380,7 +386,7 @@ def tile_moe_bdx_glu_silu_kernel(tc, dyT, a1, a3, w2, w1, w3, gate, offs, pos1, 
         for j in range(PACK):
             gather(0, 0, [j])
             gather(1, 0, [j])
-        spread_gate(1)
+        spread_second_gates()
         make_silu(0, 0)
         subtract_from_one(0, 0)
         make_tanh(0, (0, 1))
@@ -395,8 +401,8 @@ def tile_moe_bdx_glu_silu_kernel(tc, dyT, a1, a3, w2, w1, w3, gate, offs, pos1, 
         make_silu(0, 1)
 
         run(0)
-        load_w2(3)
         load_a3(2)
+        load_w2(3)
         load_a1(3)
         quantise_w2(1)
         quantise_g(1)
@@ -427,12 +433,12 @@ def tile_moe_bdx_glu_silu_kernel(tc, dyT, a1, a3, w2, w1, w3, gate, offs, pos1, 
         run(3)
         quantise_da(3, HALF, HALF + P)
         quantise_da(3, HALF + P, C)
-        second_product(0, 0, C, "dh3", nc.scalar.copy)
+        second_product(0, 0, C, "turned1", nc.scalar.copy)
         second_product(1, 0, C, "turned0", nc.scalar.copy)
         second_product(2, 0, C, "dh0", nc.scalar.copy)
         second_product(3, 0, HALF, "dh1", nc.scalar.copy)
         second_product(3, HALF, HALF + P, "dh2", nc.scalar.copy)
-        second_product(3, HALF + P, C, "turned1", nc.vector.tensor_copy)
+        second_product(3, HALF + P, C, "dh3", nc.vector.tensor_copy)
 
         tokens = in_place("gathered0", "tokens", [P, 2, T], F32)
         first, both = tokens[:, 0, :], tokens[:, 1, :]

from contextlib import ExitStack

import concourse.mybir as mybir
from concourse.masks import make_identity

K, T, E, C, H, N = 128, 1024, 4, 512, 512, 512
S = E * C
P = 128
PACK = 4
UNITS = C // P
HALF = C // 2
QUAD = 4
PAIR = 2
LIST_ROWS = 16
RANGE_ENDS = (160, 448, 672, 864, 1024)

FLOPS = 2 * S * H * N + 2 * 2 * S * H * K
BYTES = 4 * (N * T + 2 * H * S + S + E * N * H + 2 * E * H * K + K * T) + 2 * P * (S + 2 * T) // LIST_ROWS

F32 = mybir.dt.float32
BF16 = mybir.dt.bfloat16
U32 = mybir.dt.uint32
U16 = mybir.dt.uint16
U8 = mybir.dt.uint8
E4M3X4 = mybir.dt.float8_e4m3fn_x4
E5M2X4 = mybir.dt.float8_e5m2_x4

ADD = mybir.AluOpType.add
MULT = mybir.AluOpType.mult
TANH = mybir.ActivationFunctionType.Tanh
COPY = mybir.ActivationFunctionType.Copy
SILU = mybir.ActivationFunctionType.Silu


def tile_moe_bdx_glu_silu_kernel(tc, dyT, a1, a3, w2, w1, w3, gate, offs, pos1, pos2, out):
    nc = tc.nc
    with ExitStack() as ctx:
        held = ctx.enter_context(tc.tile_pool(name="held", bufs=1))
        work = ctx.enter_context(tc.tile_pool(name="work", bufs=1))
        psum = ctx.enter_context(tc.psum_pool(name="psum", bufs=1))

        def in_place(place, name, shape, dtype):
            return work.tile(shape, dtype, name=name, tag=place, align_bytes=64)

        def in_bank(bank, name, shape):
            return psum.tile(shape, F32, name=name, tag=bank)

        offs_sb = held.tile([P, S // LIST_ROWS], U16, name="offs_sb")
        pos1_sb = held.tile([P, T // LIST_ROWS], U16, name="pos1_sb")
        pos2_sb = held.tile([P, T // LIST_ROWS], U16, name="pos2_sb")
        dy_sb = [held.tile([P, T], F32, name="dy%d" % j, tag="dy%d" % j) for j in range(PACK)]
        gate_first = held.tile([P, C], F32, name="gate_first")
        gate_quads = held.tile([P, QUAD], F32, name="gate_quads")
        gate_units = held.tile([P, 2 * UNITS], F32, name="gate_units")
        tanh_sb = held.tile([P, UNITS * H], F32, name="tanh_sb")
        da_grp = [held.tile([P, 2 * C * PACK], BF16, name="da_grp%d" % j, align_bytes=64) for j in range(2)]
        dx_sb = held.tile([P, S], F32, name="dx_sb")
        ident = held.tile([P, P], F32, name="ident")
        zero_in = held.tile([P, 1], F32, name="zero_in")
        zero_bias = held.tile([P, 1], F32, name="zero_bias")

        nc.vector.memset(zero_in[:], 0.0)
        nc.scalar.activation(zero_bias[:], zero_in[:], SILU)
        make_identity(nc, ident[:])

        def unit_slots(u):
            return slice(u * P, (u + 1) * P)

        def entries(list_sb, a, b):
            return list_sb[:, a // LIST_ROWS : b // LIST_ROWS]

        w2_raw, w13_raw, a1_sb, a3_sb = {}, {}, {}, {}
        dy_rows = dyT.rearrange("(p j) c -> p j c", j=PACK)

        def load_dy(j):
            nc.sync.dma_start(out=dy_sb[j][:], in_=dy_rows[:, j, :])

        def load_w2(e):
            raw = in_place("w2_raw%d" % (e if e + 1 < E else 1), "w2_raw", [P, PACK, H], F32)
            nc.sync.dma_start(out=raw[:], in_=w2[e].rearrange("(p j) i -> p j i", j=PACK))
            w2_raw[e] = raw

        def load_w13(pair, place):
            raw = in_place(place, "w13_raw", [P, 2, 2, PACK * K], F32)
            for w, weights in enumerate((w1, w3)):
                rows = weights[2 * pair : 2 * pair + 2].rearrange("e (q r) k -> q e (r k)", r=PACK)
                nc.sync.dma_start(out=raw[:, :, w, :], in_=rows)
            w13_raw[pair] = raw

        def a1_rows(a, b):
            return a1[:, a:b].rearrange("(q r) s -> q r s", r=PACK)

        def load_a1_half(e, half):
            raw = in_place("a1_half%d" % half, "a1_half", [P, PACK, HALF], F32)
            a = e * C + half * HALF
            nc.sync.dma_start(out=raw[:], in_=a1_rows(a, a + HALF))
            a1_sb[e, half] = raw[:]

        def load_a1(e):
            raw = in_place("a1_whole%d" % e, "a1_whole", [P, PACK, C], F32)
            nc.sync.dma_start(out=raw[:], in_=a1_rows(e * C, (e + 1) * C))
            for half in range(2):
                a1_sb[e, half] = raw[:, :, half * HALF : (half + 1) * HALF]

        def a1_unit(e, u):
            return a1_sb[e, u // 2][:, :, unit_slots(u % 2)]

        def load_a3(e):
            raw = in_place("a3_%d" % (e % 2), "a3_sb", [P, PACK, C], F32)
            step = HALF if e == 0 else C
            for a in range(0, C, step):
                rows = a3[:, e * C + a : e * C + a + step].rearrange("(q r) s -> q r s", r=PACK)
                nc.sync.dma_start(out=raw[:, :, a : a + step], in_=rows)
            a3_sb[e] = raw

        g_raw, g_grp, w2_grp, w13_grp, gate_ps = {}, {}, {}, {}, {}
        g_mx, w2_mx, w13_mx, da_mx = {}, {}, {}, {}

        pieces = (
            ((0, C, "gathered0"),),
            ((0, C, "gathered1"),),
            ((0, P, "w2_raw0"), (P, C, "silu_b")),
            ((0, P, "a1_whole1"), (P, C, "gathered1")),
        )

        def gather(e, piece, planes):
            a, b, place = pieces[e][piece]
            if (e, piece) not in g_raw:
                g_raw[e, piece] = in_place(place, "g_raw", [P, PACK, b - a], F32)
            for j in planes:
                window = dy_sb[j][:].indirect(entries(offs_sb, e * C + a, e * C + b))
                if e == 0:
                    nc.vector.tensor_tensor(g_raw[e, piece][:, j, :], window, gate_first[:], MULT)
                else:
                    nc.scalar.activation(g_raw[e, piece][:, j, :], window, COPY)

        def spread(column):
            return column.to_broadcast([P, P])

        def spread_second_gates():
            bank = in_bank("dh3", "gate_ps", [P, QUAD, P])
            for i in range(QUAD):
                nc.tensor.transpose(bank[:, i, :], spread(gate_quads[:, i : i + 1]), ident[:])
            for a in (0, HALF):
                gate_ps[1, a] = bank[:].rearrange("p i n -> p n i")[:, a // QUAD : (a + HALF) // QUAD, :]

        def spread_gates(e, units, name):
            bank = in_bank(name, "gate_ps", [P, len(units) * P])
            for x, u in enumerate(units):
                column = (e - 2) * UNITS + u
                nc.tensor.transpose(bank[:, unit_slots(x)], spread(gate_units[:, column : column + 1]), ident[:])
            gate_ps[e, units[0] * P] = bank[:].rearrange("p (n i) -> p n i", i=QUAD)

        shared_grp = in_place("g_grp1", "shared_grp", [P, (C + HALF) * PACK], BF16)

        def round_g(e, piece, a, b):
            if e not in g_grp:
                g_grp[e] = shared_grp[:, : C * PACK] if e == 1 else in_place("g_grp%d" % e, "g_grp", [P, C * PACK], BF16)
            first = pieces[e][piece][0]
            into = g_grp[e][:, a * PACK : b * PACK].rearrange("p (n i j) -> p n j i", i=QUAD, j=PACK)
            values = g_raw[e, piece][:, :, a - first : b - first].rearrange("p j (n i) -> p n j i", i=QUAD)
            if e == 0:
                nc.vector.tensor_copy(into, values)
            else:
                gates = gate_ps[e, a].unsqueeze(2)
                nc.vector.tensor_tensor(into, values, gates.to_broadcast([P, (b - a) // QUAD, PACK, QUAD]), MULT)

        def round_w2(e):
            grp = shared_grp[:, HALF * PACK :] if e == 0 else in_place("w2_grp", "w2_grp", [P, H * PACK], BF16)
            into = grp[:].rearrange("p (n i j) -> p n j i", i=QUAD, j=PACK)
            values = w2_raw[e][:].rearrange("p j (n i) -> p n j i", i=QUAD)
            if e == 0:
                nc.vector.tensor_scalar(into[:, : P // 2], values[:, : P // 2], 0.5, None, op0=MULT)
                nc.scalar.activation(into[:, P // 2 :], values[:, P // 2 :], COPY, scale=0.5)
            else:
                nc.scalar.activation(into, values, COPY, scale=0.5)
            w2_grp[e] = grp

        def round_w13(experts, place):
            w13_grp[experts] = in_place(place, "w13_grp", [P, len(experts), 2 * K * PACK], BF16)
            for j, e in enumerate(experts):
                nc.scalar.copy(
                    out=w13_grp[experts][:, j, :].rearrange("p (w c i r) -> p w c r i", w=2, i=PAIR, r=PACK),
                    in_=w13_raw[e // 2][:, e % 2, :, :].rearrange("p w (r c i) -> p w c r i", i=PAIR, r=PACK),
                )

        def scale_tile(name, width, bufs):
            return work.tile([P, width], U8, name=name, tag=name, bufs=bufs, align_bytes=64)

        codes_sb = {}

        def operand_codes(e):
            if e not in codes_sb:
                codes_sb[e] = in_place("codes_or_w", "codes", [P, H + C], U32)
            return codes_sb[e]

        def quantise_w2(e):
            codes, scales = operand_codes(e)[:, :H], scale_tile("w2_scales", H, 2)
            nc.vector.quantize_mx(out=codes.bitcast(E4M3X4), scales=scales[:], in_=w2_grp[e][:])
            w2_mx[e] = codes, scales

        def quantise_g(e):
            codes, scales = operand_codes(e)[:, H:], scale_tile("g_scales", C, 2)
            nc.vector.quantize_mx(out=codes.bitcast(E5M2X4), scales=scales[:], in_=g_grp[e][:])
            g_mx[e] = codes, scales

        def quantise_da(e, a, b):
            if e not in da_mx:
                codes = in_place("g_grp%d" % ((e + 1) % E), "da_codes", [P, 2 * C], U32)
                da_mx[e] = codes, scale_tile("da_scales", 2 * C, E)
            codes, scales = da_mx[e]
            nc.vector.quantize_mx(
                out=codes[:, a:b].bitcast(E5M2X4), scales=scales[:, a:b], in_=da_grp[e % 2][:, a * PACK : b * PACK]
            )

        def quantise_w13(experts, place):
            words = len(experts) * 2 * K
            codes, scales = in_place(place, "w13_codes", [P, words], U32), scale_tile("w13_scales", 6 * K, 2)
            grp = w13_grp[experts][:].rearrange("p e c -> p (e c)")
            for a in range(0, words, 4 * K):
                b = min(a + 4 * K, words)
                nc.vector.quantize_mx(out=codes[:, a:b].bitcast(E4M3X4), scales=scales[:, a:b], in_=grp[:, a * PACK : b * PACK])
            for j, e in enumerate(experts):
                cols = slice(j * 2 * K, (j + 1) * 2 * K)
                w13_mx[e] = codes[:, cols], scales[:, cols]

        silu_sb, less = {}, {}

        def tanh_unit(u):
            return tanh_sb[:, u * H : (u + 1) * H]

        def make_tanh(e, units=range(UNITS)):
            for u in units:
                name = ("dh3", "turned0", "turned1", "dh3")[u] if e > 0 else "turned%d" % u
                bank = in_bank(name, "a1_turned", [P, PACK, P])
                for r in range(PACK):
                    nc.tensor.transpose(bank[:, r, :], a1_unit(e, u)[:, r, :], ident[:])
                nc.scalar.activation(tanh_unit(u), bank[:].rearrange("p r q -> p (r q)"), TANH, scale=0.5)

        silu_places = (("silu_a", "silu_c"), ("silu_b", "gathered1"), ("silu_c", "silu_a"), ("gathered0", "gathered1"))

        def make_silu(e, half):
            silu = in_place(silu_places[e][half], "silu_sb", [P, PACK, HALF], F32)[:]
            nc.scalar.activation(silu, a1_sb[e, half], SILU, scale=-1.0, bias=zero_bias[:])
            silu_sb[e, half] = silu
            if (e, half) == (E - 1, 1):
                less[e, half] = silu
                nc.scalar.activation(silu, silu, COPY, scale=-1.0, bias=1.0)

        def subtract_from_one(e, half):
            less[e, half] = in_place("less", "less_sb", [P, PACK, HALF], F32)[:]
            nc.gpsimd.tensor_scalar(less[e, half], silu_sb[e, half], -1.0, 1.0, op0=MULT, op1=ADD)

        w_sb = {}

        def make_w(e, half):
            if half == 0:
                flat = da_grp[(e + 1) % 2][:].bitcast(F32)[:, : PACK * HALF]
                w_sb[e, half] = flat.rearrange("p (r s) -> p r s", r=PACK)
            else:
                w_sb[e, half] = in_place("codes_or_w" if e + 1 < E else "less", "w_late", [P, PACK, HALF], F32)[:]
            nc.gpsimd.tensor_tensor(w_sb[e, half], less[e, half], a3_sb[e][:, :, half * HALF : (half + 1) * HALF], MULT)

        def w_unit(e, u):
            return w_sb[e, u // 2][:, :, unit_slots(u % 2)]

        dh_ps, m_ps = {}, {}

        def first_product(e, u):
            g_codes, g_scales = g_mx[e]
            w_codes, w_scales = w2_mx[e]
            bank = in_bank("dh%d" % u, "dh", [P, H])
            nc.tensor.matmul_mx(
                out=bank[:],
                lhsT=g_codes[:, unit_slots(u)].bitcast(E5M2X4),
                lhsT_scale=g_scales[:, unit_slots(u)],
                rhs=w_codes[:].bitcast(E4M3X4),
                rhs_scale=w_scales[:],
                start=True,
                stop=True,
            )
            dh_ps[e, u] = bank

        def make_m(e, u):
            m = work.tile([P, H], F32, name="m_sb", tag="m_sb", bufs=UNITS)
            nc.vector.scalar_tensor_tensor(
                out=m[:].rearrange("p (r q) -> p r q", r=PACK),
                in0=tanh_unit(u).rearrange("p (r q) -> p r q", r=PACK),
                scalar=1.0,
                in1=dh_ps[e, u][:].rearrange("p (q r) -> p r q", r=PACK),
                op0=ADD,
                op1=MULT,
            )
            if 0 < e < E - 1 and u == UNITS - 1:
                round_g(e + 1, 0, 0, P)
            bank = in_bank("turned%d" % u, "m_turned", [P, PACK, P])
            for r in range(PACK):
                nc.tensor.transpose(bank[:, r, :], m[:, r * P : (r + 1) * P], ident[:])
            m_ps[e, u] = bank

        def make_da(e, u, which, factor):
            a = (which * C + u * P) * PACK
            nc.vector.tensor_tensor(
                da_grp[e % 2][:, a : a + P * PACK].rearrange("p (c i r) -> p c r i", i=PAIR, r=PACK),
                m_ps[e, u][:].rearrange("p r (c i) -> p c r i", i=PAIR),
                factor.rearrange("p r (c i) -> p c r i", i=PAIR),
                MULT,
            )

        def run(e):
            last = e + 1 == E
            for u in range(UNITS):
                first_product(e, u)
            make_w(e, 0)
            if not last:
                subtract_from_one(e, 1)
            make_w(e, 1)
            if not last:
                make_silu(e + 1, 0)
                subtract_from_one(e + 1, 0)
            if 0 < e < E - 1:
                spread_gates(e + 1, (0,), "turned3")
            for u in range(UNITS):
                make_m(e, u)
            if not last:
                if e > 0:
                    spread_gates(e + 1, (1, 2, 3), "dh2")
                round_w2(e + 1)
            if e + 2 == E:
                round_w13((0,), "w13_grp")
            for u in range(2):
                make_da(e, u, 1, a1_unit(e, u))
                make_da(e, u, 0, w_unit(e, u))
            if not last:
                make_tanh(e + 1)
            make_da(e, 2, 1, a1_unit(e, 2))
            if last:
                make_da(e, 3, 1, a1_unit(e, 3))
                quantise_w13((1, 2, 3), "a1_whole3")
                quantise_da(e, C, 2 * C)
                quantise_da(e, 0, HALF)
            elif e > 0:
                round_g(e + 1, len(pieces[e + 1]) - 1, *pieces[e + 1][-1][:2])
            make_da(e, 2, 0, w_unit(e, 2))
            make_da(e, 3, 0, w_unit(e, 3))
            if not last:
                make_da(e, 3, 1, a1_unit(e, 3))

        def second_product(e, a, b, bank_name, copy):
            w_codes, w_scales = w13_mx[e]
            bank = in_bank(bank_name, "dx", [P, b - a])
            da_codes, da_scales = da_mx[e]
            for which in (1, 0):
                cols = slice(which * K, (which + 1) * K)
                words = slice(which * C + a, which * C + b)
                nc.tensor.matmul_mx(
                    out=bank[:],
                    lhsT=w_codes[:, cols].bitcast(E4M3X4),
                    lhsT_scale=w_scales[:, cols],
                    rhs=da_codes[:, words].bitcast(E5M2X4),
                    rhs_scale=da_scales[:, words],
                    start=which == 1,
                    stop=which == 0,
                )
            copy(dx_sb[:, e * C + a : e * C + b], bank[:])

        nc.sync.dma_start(offs_sb[:], offs)
        load_dy(0)
        nc.sync.dma_start(out=gate_first[:], in_=gate[0:P, 0:C])
        load_dy(1)
        load_dy(2)
        load_dy(3)
        nc.sync.dma_start(out=gate_quads[:], in_=gate[0, C : 2 * C].rearrange("(n i) -> n i", i=QUAD))
        load_a1_half(0, 0)
        load_w2(0)
        load_a1_half(0, 1)
        load_a3(0)
        load_w2(1)
        load_a1(1)
        load_a3(1)
        nc.sync.dma_start(out=gate_units[:], in_=gate[0, 2 * C :].rearrange("(x n) -> n x", n=P))
        load_a1(2)
        nc.sync.dma_start(pos1_sb[:], pos1)
        nc.sync.dma_start(pos2_sb[:], pos2)

        for j in range(PACK):
            gather(0, 0, [j])
            gather(1, 0, [j])
        spread_second_gates()
        make_silu(0, 0)
        subtract_from_one(0, 0)
        make_tanh(0, (0, 1))
        round_g(0, 0, 0, C)
        round_g(1, 0, 0, HALF)
        quantise_g(0)
        round_w2(0)
        load_w2(2)
        quantise_w2(0)
        round_g(1, 0, HALF, C)
        make_tanh(0, (2, 3))
        make_silu(0, 1)

        run(0)
        load_a3(2)
        load_w2(3)
        load_a1(3)
        quantise_w2(1)
        quantise_g(1)
        quantise_da(0, 0, 2 * C)
        make_silu(1, 1)
        gather(2, 0, range(PACK))
        gather(2, 1, range(PACK))

        run(1)
        load_w13(0, "w2_raw2")
        load_a3(3)
        quantise_w2(2)
        quantise_g(2)
        quantise_da(1, 0, 2 * C)
        gather(3, 0, range(PACK))
        make_silu(2, 1)
        gather(3, 1, range(PACK))

        run(2)
        load_w13(1, "a1_whole1")
        quantise_w2(3)
        quantise_g(3)
        quantise_w13((0,), "a1_whole2")
        quantise_da(2, 0, 2 * C)
        make_silu(3, 1)
        round_w13((1, 2, 3), "w2_grp")

        run(3)
        quantise_da(3, HALF, HALF + P)
        quantise_da(3, HALF + P, C)
        second_product(0, 0, C, "turned1", nc.scalar.copy)
        second_product(1, 0, C, "turned0", nc.scalar.copy)
        second_product(2, 0, C, "dh0", nc.scalar.copy)
        second_product(3, 0, HALF, "dh1", nc.scalar.copy)
        second_product(3, HALF, HALF + P, "dh2", nc.scalar.copy)
        second_product(3, HALF + P, C, "dh3", nc.vector.tensor_copy)

        tokens = in_place("gathered0", "tokens", [P, 2, T], F32)
        first, both = tokens[:, 0, :], tokens[:, 1, :]
        for a, b in zip((0,) + RANGE_ENDS, RANGE_ENDS):
            window = dx_sb[:].indirect(entries(pos1_sb, a, b))
            if a == 0:
                nc.vector.tensor_copy(first[:, a:b], window)
            else:
                nc.scalar.activation(first[:, a:b], window, COPY)
            nc.vector.tensor_tensor(both[:, a:b], dx_sb[:].indirect(entries(pos2_sb, a, b)), first[:, a:b], ADD)
            if a > 0:
                begin = 0 if a == RANGE_ENDS[0] else a
                nc.sync.dma_start(out=out[:, begin:b], in_=both[:, begin:b])
